import numpy as np
import ml_dtypes


def mxq(x, axis, fmt="e4m3"):
    dtype, down = {"e4m3": (ml_dtypes.float8_e4m3fn, 7), "e5m2": (ml_dtypes.float8_e5m2, 14)}[fmt]
    v = np.moveaxis(np.asarray(x, np.float32).astype(ml_dtypes.bfloat16).astype(np.float64), axis, -1)
    blocks = v.reshape(v.shape[:-1] + (-1, 32))
    amax = np.abs(blocks).max(-1, keepdims=True)
    byte = np.maximum(np.where(amax > 0, np.frexp(amax)[1] - 1 + 127, 0) - down, 1)
    scale = np.exp2(byte - 127.0)
    codes = (blocks / scale).astype(np.float32).astype(dtype).astype(np.float64)
    return np.moveaxis((codes * scale).reshape(v.shape), -1, axis)


WIDE = False


def mx_kscale(k):
    if not WIDE:
        return np.ones(k)
    levels = np.array([10, -10, 5, -5, 0])
    if k % 512:
        return np.exp2(np.random.permutation(np.resize(levels, k // 32))).repeat(32)
    a = np.empty((k // 512, 16))
    for p in range(k // 512):
        a[p, :8] = np.random.permutation(np.resize(levels, 8))
        for g in range(8):
            far = levels[np.abs(levels - a[p, g]) >= 10]
            a[p, g + 8] = far[np.random.randint(len(far))]
    return np.exp2(a.ravel()).repeat(32)


def f64(x):
    return np.asarray(x).astype(np.float64)


def striped(idx):
    return np.tile(idx.reshape(-1, 16).T, (8, 1)).astype(np.uint16)


def unstriped(offs):
    return offs[:16].T.reshape(-1).astype(np.int64)


E2M1 = np.array([0.0, 0.5, 1.0, 1.5, 2.0, 3.0, 4.0, 6.0, -0.0, -0.5, -1.0, -1.5, -2.0, -3.0, -4.0, -6.0])


def pack_weight(w, fmt):
    k, n = w.shape
    w = f64(np.asarray(w, np.float32).astype(ml_dtypes.bfloat16)).reshape(k // 32, 32, n)
    amax = np.abs(w).max(1)
    if fmt == "e4m3":
        byte = np.frexp(amax)[1] - 1 + 127 - 7
    else:
        mant, ex = np.frexp(amax / 6.0)
        byte = np.where(mant > 0.5, ex, ex - 1) + 127
    byte = np.clip(np.where(amax > 0, byte, 1), 1, 254)
    scaled = (w * np.exp2(127.0 - byte)[:, None, :]).reshape(k, n).astype(np.float32)
    by_word = np.ascontiguousarray(scaled.reshape(k // 512, 128, 4, n).transpose(0, 1, 3, 2))
    if fmt == "e4m3":
        words = by_word.astype(ml_dtypes.float8_e4m3fn).view(np.uint8)
    else:
        c = by_word.astype(ml_dtypes.float4_e2m1fn).view(np.uint8) & 0xF
        words = (c[..., 0::2] | (c[..., 1::2] << 4)).reshape(k // 512, 128, 2 * n)
    return np.ascontiguousarray(words), np.ascontiguousarray(byte.astype(np.uint8).reshape(k // 512, 16, n))


def unpack_weight(words, scales, fmt):
    g, _, n = scales.shape
    words = np.ascontiguousarray(words).reshape(g, 128, n, -1)
    if fmt == "e4m3":
        vals = words.view(ml_dtypes.float8_e4m3fn).astype(np.float64)
    else:
        nib = np.empty((g, 128, n, 4), np.uint8)
        nib[..., 0::2] = words & 0xF
        nib[..., 1::2] = words >> 4
        vals = E2M1[nib]
    vals = vals * np.repeat(np.exp2(scales.astype(np.float64) - 127.0), 8, axis=1)[..., None]
    return vals.transpose(0, 1, 3, 2).reshape(g * 512, n)


def d_silu(v):
    s = 1.0 / (1.0 + np.exp(-np.maximum(v, -700.0)))
    return s * (1.0 + v * (1.0 - s))


K, T, E, C, H, N = 768, 512, 6, 256, 512, 1024
TOP = 3


def by_expert(wq, xq):
    return np.concatenate([wq[e].T @ xq[:, e * C:(e + 1) * C] for e in range(E)], axis=1)


def setup_inputs():
    n = np.random.standard_normal
    s = mx_kscale(N)[:, None]
    u = mx_kscale(H)
    deal = np.repeat(np.arange(E), C).reshape(TOP, T)[:, np.random.permutation(T)]
    deal = np.take_along_axis(deal, np.argsort(np.random.rand(TOP, T), axis=0), axis=0)
    for _ in range(8):
        s_, t_ = np.random.permutation(T).reshape(2, -1); r = np.random.randint(TOP, size=T // 2); x, y = deal[r, s_].copy(), deal[r, t_].copy()
        ok = ~((deal[:, s_] == y).any(0) | (deal[:, t_] == x).any(0)); deal[r[ok], s_[ok]] = y[ok]; deal[r[ok], t_[ok]] = x[ok]
    order = np.lexsort((np.random.rand(TOP * T), deal.reshape(-1)))
    slot_token = order % T; pos = np.empty(TOP * T, np.int64); pos[order] = np.arange(TOP * T); pos = pos.reshape(TOP, T)
    g = np.random.uniform(0.5, 1.5, (TOP, T)); g = g / g.sum(0)
    w_slot = np.empty(E * C)
    for r in range(TOP): w_slot[pos[r]] = g[r]
    dy = pack_weight(n((N, T)) * s, "e4m3")
    return {
        "dy_words": dy[0],
        "dy_scales": dy[1],
        "a": n((H, E * C)).astype(np.float32),
        "w2": (n((E, N, H)) / np.sqrt(N) / s[None] * u[None, None, :]).astype(np.float32),
        "w1": (n((E, H, K)) / np.sqrt(H) / u[None, :, None]).astype(np.float32),
        "gate": np.tile(w_slot, (H, 1)).astype(np.float32),
        "offs": striped(slot_token),
        "pos1": striped(pos[0]),
        "pos2": striped(pos[1]),
        "pos3": striped(pos[2]),
    }


def reference(dy_words, dy_scales, a, w2, w1, gate, offs, pos1, pos2, pos3):
    idx = unstriped(offs)
    gq = unpack_weight(dy_words, dy_scales, "e4m3")[:, idx]
    dh = f64(gate) * by_expert(mxq(f64(w2), 1, "e4m3"), gq)
    da = dh * d_silu(f64(a))
    dx = by_expert(mxq(f64(w1), 1, "e4m3"), mxq(da, 0, "e4m3"))
    return dx[:, unstriped(pos1)] + dx[:, unstriped(pos2)] + dx[:, unstriped(pos3)]

@@ -1,0 +1,264 @@
+from contextlib import ExitStack
+
+import concourse.mybir as mybir
+
+K, T, E, C, H, N = 768, 512, 6, 256, 512, 1024
+S = E * C
+FLOPS = 2 * S * (N * H + H * K)
+BYTES = N * T + N * T // 32 + 4 * (H * S + E * N * H + E * H * K + 128 * S + K * T) + 2 * 128 * (S + 3 * T) // 16
+
+F32 = mybir.dt.float32
+BF16 = mybir.dt.bfloat16
+I32 = mybir.dt.int32
+U32 = mybir.dt.uint32
+U16 = mybir.dt.uint16
+U8 = mybir.dt.uint8
+FP8X4 = mybir.dt.float8_e4m3fn_x4
+ACT = mybir.ActivationFunctionType
+ALU = mybir.AluOpType
+
+P = 128
+PACK = 4
+PASSES = N // (P * PACK)
+KT = K // P
+VM = ((0,32),(0,32),(0,32),(0,32),(0,32),(0,64))
+W1_ENG = {}
+W1_CHUNKS = ((0, 256), (256, 256), (512, 256))
+
+
+def tile_moe_bdx_mlp_silu_kernel(tc, dy_words, dy_scales, a, w2, w1, gate, offs, pos1, pos2, pos3, out):
+    nc = tc.nc
+    with ExitStack() as ctx:
+        lists = ctx.enter_context(tc.tile_pool(name="lists", bufs=1))
+        keep = ctx.enter_context(tc.tile_pool(name="keep", bufs=1))
+        ring = ctx.enter_context(tc.tile_pool(name="ring", bufs=2))
+        psum = ctx.enter_context(tc.psum_pool(name="psum", bufs=1))
+
+        offs_t = lists.tile([P, S // 16], U16, name="offs_t")
+        pos_t = [lists.tile([P, T // 16], U16, name=f"pos_t{r}") for r in range(3)]
+        words = keep.tile([P, PASSES, T], I32, name="words", align_bytes=64)
+        plane = keep.tile([P, T // 4], I32, name="plane", align_bytes=64)
+
+        nc.vector.memset(plane[:], 0)
+        nc.sync.dma_start(offs_t[:], offs)
+        nc.sync.dma_start(out=words[:], in_=dy_words.rearrange("o p t d -> p o (t d)").bitcast(I32))
+        scales_i32 = dy_scales.bitcast(I32)
+        for q in range(4):
+            nc.sync.dma_start(out=plane[32 * q : 32 * q + 8, :], in_=scales_i32[:, 4 * q : 4 * q + 4, :])
+
+        a_rows = a.rearrange("(p j) s -> p j s", j=PACK)
+        a_t, gate_t, w2_raw, w1_raw = {}, {}, {}, {}
+
+        def load_a(first, count):
+            tile = ring.tile([P, PACK, count * C], F32, name="a_t", tag="a_t", bufs=3)
+            nc.sync.dma_start(out=tile[:], in_=a_rows[:, :, C * first : C * (first + count)])
+            for n in range(count):
+                a_t[first + n] = tile[:, :, C * n : C * (n + 1)]
+
+        def load_gate(first, count):
+            tile = keep.tile([P, count * C], F32, name=f"gate{first}")
+            nc.sync.dma_start(out=tile[:], in_=gate[0:P, C * first : C * (first + count)])
+            nc.gpsimd.tensor_scalar(out=tile[:], in0=tile[:], scalar1=-0.5, scalar2=0.0, op0=ALU.mult, op1=ALU.add)
+            for n in range(count):
+                gate_t[first + n] = tile[:, C * n : C * (n + 1)]
+
+        def load_w2(e, o):
+            raw = ring.tile([P, PACK, H], F32, name="raw", tag="raw", bufs=9)
+            nc.sync.dma_start(out=raw[:], in_=w2[e, 512 * o : 512 * (o + 1), :].rearrange("(p j) i -> p j i", j=PACK))
+            w2_raw[e, o] = raw
+
+        def load_lists():
+            for r, pos in enumerate((pos1, pos2, pos3)):
+                nc.sync.dma_start(pos_t[r][:], pos)
+
+        def load_w1(chunk, experts):
+            k0, width = W1_CHUNKS[chunk]
+            if chunk == 0 and False:
+                raw = keep.tile([P, len(experts), PACK, width], F32, name=f"w1_first{experts[0]}")
+            else:
+                raw = ring.tile([P, len(experts), PACK, width], F32, name="raw", tag="raw", bufs=9)
+            for n, e in enumerate(experts):
+                nc.sync.dma_start(out=raw[:, n], in_=w1[e].rearrange("(p j) k -> p j k", j=PACK)[:, :, k0 : k0 + width])
+                for kt in range(k0 // P, (k0 + width) // P):
+                    w1_raw[kt, e] = raw[:, n, :, kt * P - k0 : (kt + 1) * P - k0]
+
+        load_a(0, 1)
+        load_w2(0, 0)
+        load_gate(0, 2)
+        load_a(1, 1)
+        load_w2(0, 1)
+        load_w2(1, 0)
+        load_a(2, 1)
+        load_gate(2, 4)
+        load_w2(1, 1)
+        load_w2(2, 0)
+        load_a(3, 1)
+        load_w2(2, 1)
+        load_w2(3, 0)
+        load_a(4, 1)
+        load_w2(3, 1)
+        load_w2(4, 0)
+        load_a(5, 1)
+        load_w2(4, 1)
+        load_w2(5, 0)
+        load_w1(0, (0, 1))
+        load_w2(5, 1)
+        load_w1(0, (2, 3))
+        load_w1(0, (4, 5))
+        load_lists()
+        for chunk in (1, 2):
+            for pair in range(3):
+                load_w1(chunk, (2 * pair, 2 * pair + 1))
+
+        g_words, g_scales = {}, {}
+
+        def gather_dy(e):
+            g_words[e] = ring.tile([P, PASSES, C], U32, name="g_words", tag="g_words", bufs=4, align_bytes=64)
+            g_scales[e] = ring.tile([P, C], U8, name="g_scales", tag="g_scales", bufs=4, align_bytes=64)
+            slots = offs_t[:, 16 * e : 16 * (e + 1)]
+            for o in range(PASSES):
+                nc.vector.tensor_copy(g_words[e][:, o, :], words[:, o, :].bitcast(U32).indirect(slots))
+            nc.vector.tensor_copy(g_scales[e][:], plane[:].bitcast(U8).indirect(slots))
+
+        da_codes, da_scales = {}, {}
+
+        silu_neg, factor, codes, scales, grouped, da = {}, {}, {}, {}, {}, {}
+
+        def activations(e):
+            silu_neg[e] = ring.tile([P, PACK, C], F32, name="silu_neg", tag="silu_neg", bufs=3)
+            factor[e] = ring.tile([P, PACK, C], F32, name="factor", tag="factor", bufs=3)
+            nc.scalar.activation(out=silu_neg[e][:], in_=a_t[e], func=ACT.Silu, scale=-1.0)
+            nc.scalar.activation(out=factor[e][:], in_=a_t[e], func=ACT.Tanh, scale=0.5)
+
+        def cast_w2(e, o):
+            grouped[e, o] = ring.tile([P, PACK * H], BF16, name="w2_grouped", tag="w2_grouped", bufs=5, align_bytes=64)
+            src = w2_raw[e, o][:].rearrange("p j (m t) -> p m j t", t=PACK)
+            dst = grouped[e, o][:].rearrange("p (t m j) -> p m j t", t=PACK, j=PACK)
+            cut = P - VM[e][o]
+            if cut > 0:
+                nc.scalar.copy(out=dst[:, :cut], in_=src[:, :cut])
+            if cut < P:
+                nc.vector.tensor_copy(out=dst[:, cut:], in_=src[:, cut:])
+
+        def quantize_w2(e, o):
+            codes[e, o] = ring.tile([P, H], U32, name="w2_codes", tag="w2_codes", bufs=4, align_bytes=64)
+            scales[e, o] = ring.tile([P, H], U8, name="w2_scales", tag="w2_scales", bufs=4, align_bytes=64)
+            nc.vector.quantize_mx(out=codes[e, o][:].bitcast(FP8X4), scales=scales[e, o][:], in_=grouped[e, o][:])
+
+        def make_factor(e):
+            gate_e = gate_t[e].unsqueeze(1).to_broadcast([P, PACK, C])
+            if e > 0:
+                room = grouped[e - 1, 1][:].bitcast(F32).rearrange("p (j s) -> p j s", j=PACK)
+            else:
+                room = silu_neg[e][:]
+            nc.vector.scalar_tensor_tensor(out=room, in0=silu_neg[e][:], scalar=1.0, in1=gate_e, op0=ALU.subtract, op1=ALU.mult)
+            nc.vector.scalar_tensor_tensor(out=factor[e][:], in0=factor[e][:], scalar=1.0, in1=room, op0=ALU.add, op1=ALU.mult)
+
+        def first_product(e):
+            da[e] = ring.tile([P, C * PACK], BF16, name="da", tag="da", align_bytes=64)
+            for h in range(C // P):
+                cols = slice(P * h, P * (h + 1))
+                acc = psum.tile([P, PACK, P], F32, name="acc", tag="acc", bufs=3)
+                for t in range(PACK):
+                    for o in range(PASSES):
+                        nc.tensor.matmul_mx(
+                            out=acc[:, t, :],
+                            lhsT=codes[e, o][:, P * t : P * (t + 1)].bitcast(FP8X4),
+                            lhsT_scale=scales[e, o][:, P * t : P * (t + 1)],
+                            rhs=g_words[e][:, o, cols].bitcast(FP8X4),
+                            rhs_scale=g_scales[e][4 * o : P, cols],
+                            start=(o == 0),
+                            stop=(o == PASSES - 1),
+                        )
+                nc.vector.tensor_tensor(
+                    out=da[e][:, PACK * P * h : PACK * P * (h + 1)].rearrange("p (c i j) -> p c j i", i=4, j=PACK),
+                    in0=acc[:].rearrange("p j (c i) -> p c j i", i=4),
+                    in1=factor[e][:, :, cols].rearrange("p j (c i) -> p c j i", i=4),
+                    op=ALU.mult,
+                )
+
+        def quantize_da(e):
+            da_codes[e] = keep.tile([P, C], U32, name=f"da_codes{e}", align_bytes=64)
+            da_scales[e] = keep.tile([P, C], U8, name=f"da_scales{e}", align_bytes=64)
+            nc.vector.quantize_mx(out=da_codes[e][:].bitcast(FP8X4), scales=da_scales[e][:], in_=da[e][:])
+
+        w1_grouped, w1_codes, w1_scales, dx = {}, {}, {}, {}
+
+        def quantize_w1(kt, experts):
+            if experts[0] == 0:
+                w1_grouped[kt] = ring.tile([P, E * P * PACK], BF16, name="w1_grouped", tag="w1_grouped", bufs=4, align_bytes=64)
+                w1_codes[kt] = ring.tile([P, E * P], U32, name="w1_codes", tag="w1_codes", bufs=3, align_bytes=64)
+                w1_scales[kt] = ring.tile([P, E * P], U8, name="w1_scales", tag="w1_scales", bufs=3, align_bytes=64)
+            for e in experts:
+                copy = {"v": nc.vector.tensor_copy, "g": nc.gpsimd.tensor_copy}.get(W1_ENG.get((kt, e)), nc.scalar.copy)
+                copy(
+                    out=w1_grouped[kt][:, PACK * P * e : PACK * P * (e + 1)].rearrange("p (c i j) -> p c j i", i=4, j=PACK),
+                    in_=w1_raw[kt, e].rearrange("p j (c i) -> p c j i", i=4),
+                )
+            cols = slice(P * experts[0], P * (experts[-1] + 1))
+            nc.vector.quantize_mx(
+                out=w1_codes[kt][:, cols].bitcast(FP8X4),
+                scales=w1_scales[kt][:, cols],
+                in_=w1_grouped[kt][:, PACK * cols.start : PACK * cols.stop],
+            )
+
+        def second_layer(kt, pair):
+            if pair == 0:
+                dx[kt] = ring.tile([P, S], F32, name="dx", tag="dx", bufs=3)
+            bank = psum.tile([P, 2 * C], F32, name="bank", tag="bank", bufs=5)
+            for n in range(2):
+                e = 2 * pair + n
+                nc.tensor.matmul_mx(
+                    out=bank[:, C * n : C * (n + 1)],
+                    lhsT=w1_codes[kt][:, P * e : P * (e + 1)].bitcast(FP8X4),
+                    lhsT_scale=w1_scales[kt][:, P * e : P * (e + 1)],
+                    rhs=da_codes[e][:].bitcast(FP8X4),
+                    rhs_scale=da_scales[e][:],
+                    start=True,
+                    stop=True,
+                )
+            nc.scalar.copy(out=dx[kt][:, 2 * C * pair : 2 * C * (pair + 1)], in_=bank[:])
+
+        def combine(kt):
+            if kt + 1 < KT:
+                room = w1_grouped[kt + 1]
+            else:
+                room = ring.tile([P, E * P * PACK], BF16, name="w1_grouped", tag="w1_grouped", bufs=4, align_bytes=64)
+            picked = [room[:, 2 * T * r : 2 * T * (r + 1)].bitcast(F32) for r in range(3)]
+            total = ring.tile([P, T], F32, name="total", tag="total")
+            for r in range(3):
+                nc.vector.tensor_copy(picked[r], dx[kt][:].indirect(pos_t[r][:]))
+            nc.vector.tensor_tensor(out=picked[0], in0=picked[0], in1=picked[1], op=ALU.add)
+            nc.vector.tensor_tensor(out=total[:], in0=picked[0], in1=picked[2], op=ALU.add)
+            nc.sync.dma_start(out=out[P * kt : P * (kt + 1), :], in_=total[:])
+
+        for e in range(1):
+            gather_dy(e)
+        activations(0)
+        make_factor(0)
+        for e in range(E):
+            cast_w2(e, 0)
+            quantize_w2(e, 0)
+            if e + 1 < E:
+                activations(e + 1)
+            cast_w2(e, 1)
+            quantize_w2(e, 1)
+            if e + 1 < E:
+                make_factor(e + 1)
+            first_product(e)
+            if e + 1 < E:
+                gather_dy(e + 1)
+            quantize_da(e)
+        for kt in range(2):
+            quantize_w1(kt, (0, 1, 2, 3))
+            quantize_w1(kt, (4, 5))
+        for pair in range(3):
+            second_layer(0, pair)
+        for kt in range(KT):
+            if kt + 2 < KT:
+                quantize_w1(kt + 2, (0, 1, 2, 3))
+                quantize_w1(kt + 2, (4, 5))
+            if kt + 1 < KT:
+                for pair in range(3):
+                    second_layer(kt + 1, pair)
+            combine(kt)

@@ -41,7 +41,8 @@ def tile_moe_bdx_mlp_silu_kernel(tc, dy_words, dy_scales, a, w2, w1, gate, offs,
 
         nc.vector.memset(plane[:], 0)
         nc.sync.dma_start(offs_t[:], offs)
-        nc.sync.dma_start(out=words[:], in_=dy_words.rearrange("o p t d -> p o (t d)").bitcast(I32))
+        words_i32 = dy_words.rearrange("o p t d -> p o (t d)").bitcast(I32)
+        nc.sync.dma_start(out=words[:, 0, :], in_=words_i32[:, 0, :])
         scales_i32 = dy_scales.bitcast(I32)
         for q in range(4):
             nc.sync.dma_start(out=plane[32 * q : 32 * q + 8, :], in_=scales_i32[:, 4 * q : 4 * q + 4, :])
@@ -58,12 +59,13 @@ def tile_moe_bdx_mlp_silu_kernel(tc, dy_words, dy_scales, a, w2, w1, gate, offs,
         def load_gate(first, count):
             tile = keep.tile([P, count * C], F32, name=f"gate{first}")
             nc.sync.dma_start(out=tile[:], in_=gate[0:P, C * first : C * (first + count)])
-            nc.gpsimd.tensor_scalar(out=tile[:], in0=tile[:], scalar1=-0.5, scalar2=0.0, op0=ALU.mult, op1=ALU.add)
+            for cols in (slice(0, 2 * C), slice(2 * C, count * C)):
+                nc.gpsimd.tensor_scalar(out=tile[:, cols], in0=tile[:, cols], scalar1=-0.5, scalar2=0.0, op0=ALU.mult, op1=ALU.add)
             for n in range(count):
                 gate_t[first + n] = tile[:, C * n : C * (n + 1)]
 
         def load_w2(e, o):
-            raw = ring.tile([P, PACK, H], F32, name="raw", tag="raw", bufs=9)
+            raw = ring.tile([P, PACK, H], F32, name="raw", tag="raw", bufs=5)
             nc.sync.dma_start(out=raw[:], in_=w2[e, 512 * o : 512 * (o + 1), :].rearrange("(p j) i -> p j i", j=PACK))
             w2_raw[e, o] = raw
 
@@ -71,25 +73,23 @@ def tile_moe_bdx_mlp_silu_kernel(tc, dy_words, dy_scales, a, w2, w1, gate, offs,
             for r, pos in enumerate((pos1, pos2, pos3)):
                 nc.sync.dma_start(pos_t[r][:], pos)
 
-        def load_w1(chunk, experts):
-            k0, width = W1_CHUNKS[chunk]
-            if chunk == 0 and False:
-                raw = keep.tile([P, len(experts), PACK, width], F32, name=f"w1_first{experts[0]}")
-            else:
-                raw = ring.tile([P, len(experts), PACK, width], F32, name="raw", tag="raw", bufs=9)
-            for n, e in enumerate(experts):
-                nc.sync.dma_start(out=raw[:, n], in_=w1[e].rearrange("(p j) k -> p j k", j=PACK)[:, :, k0 : k0 + width])
-                for kt in range(k0 // P, (k0 + width) // P):
-                    w1_raw[kt, e] = raw[:, n, :, kt * P - k0 : (kt + 1) * P - k0]
+        w1_tile = {}
+
+        def load_w1(kt, experts):
+            if kt not in w1_tile:
+                w1_tile[kt] = ring.tile([P, E * PACK * P], F32, name="w1_tile", tag="w1_tile", bufs=4)
+            for e in experts:
+                w1_raw[kt, e] = w1_tile[kt][:, PACK * P * e : PACK * P * (e + 1)].rearrange("p (j k) -> p j k", j=PACK)
+                nc.sync.dma_start(out=w1_raw[kt, e], in_=w1[e].rearrange("(p j) k -> p j k", j=PACK)[:, :, P * kt : P * (kt + 1)])
 
         load_a(0, 1)
+        nc.sync.dma_start(out=words[:, 1, :], in_=words_i32[:, 1, :])
         load_w2(0, 0)
-        load_gate(0, 2)
+        load_gate(0, 6)
         load_a(1, 1)
         load_w2(0, 1)
         load_w2(1, 0)
         load_a(2, 1)
-        load_gate(2, 4)
         load_w2(1, 1)
         load_w2(2, 0)
         load_a(3, 1)
@@ -100,15 +100,13 @@ def tile_moe_bdx_mlp_silu_kernel(tc, dy_words, dy_scales, a, w2, w1, gate, offs,
         load_w2(4, 0)
         load_a(5, 1)
         load_w2(4, 1)
+        load_w1(0, range(0, 4))
         load_w2(5, 0)
-        load_w1(0, (0, 1))
         load_w2(5, 1)
-        load_w1(0, (2, 3))
-        load_w1(0, (4, 5))
+        load_w1(0, range(4, E))
         load_lists()
-        for chunk in (1, 2):
-            for pair in range(3):
-                load_w1(chunk, (2 * pair, 2 * pair + 1))
+        for kt in range(1, KT):
+            load_w1(kt, range(E))
 
         g_words, g_scales = {}, {}
 
@@ -136,7 +134,8 @@ def tile_moe_bdx_mlp_silu_kernel(tc, dy_words, dy_scales, a, w2, w1, gate, offs,
             dst = grouped[e, o][:].rearrange("p (t m j) -> p m j t", t=PACK, j=PACK)
             cut = P - VM[e][o]
             if cut > 0:
-                nc.scalar.copy(out=dst[:, :cut], in_=src[:, :cut])
+                for t in (0, 2):
+                    nc.scalar.copy(out=dst[:, :cut, :, t : t + 2], in_=src[:, :cut, :, t : t + 2])
             if cut < P:
                 nc.vector.tensor_copy(out=dst[:, cut:], in_=src[:, cut:])
 
@@ -155,10 +154,13 @@ def tile_moe_bdx_mlp_silu_kernel(tc, dy_words, dy_scales, a, w2, w1, gate, offs,
             nc.vector.scalar_tensor_tensor(out=factor[e][:], in0=factor[e][:], scalar=1.0, in1=room, op0=ALU.add, op1=ALU.mult)
 
         def first_product(e):
-            da[e] = ring.tile([P, C * PACK], BF16, name="da", tag="da", align_bytes=64)
+            if e == E - 1:
+                da[e] = w1_grouped[0][:, 0 : 0 + C * PACK]
+            else:
+                da[e] = ring.tile([P, C * PACK], BF16, name="da", tag="da", align_bytes=64)
             for h in range(C // P):
                 cols = slice(P * h, P * (h + 1))
-                acc = psum.tile([P, PACK, P], F32, name="acc", tag="acc", bufs=3)
+                acc = psum.tile([P, PACK, P], F32, name="acc", tag="acc", bufs=4)
                 for t in range(PACK):
                     for o in range(PASSES):
                         nc.tensor.matmul_mx(
@@ -180,7 +182,7 @@ def tile_moe_bdx_mlp_silu_kernel(tc, dy_words, dy_scales, a, w2, w1, gate, offs,
         def quantize_da(e):
             da_codes[e] = keep.tile([P, C], U32, name=f"da_codes{e}", align_bytes=64)
             da_scales[e] = keep.tile([P, C], U8, name=f"da_scales{e}", align_bytes=64)
-            nc.vector.quantize_mx(out=da_codes[e][:].bitcast(FP8X4), scales=da_scales[e][:], in_=da[e][:])
+            nc.vector.quantize_mx(out=da_codes[e][:].bitcast(FP8X4), scales=da_scales[e][:], in_=da[e][:, :])
 
         w1_grouped, w1_codes, w1_scales, dx = {}, {}, {}, {}
 
@@ -204,8 +206,14 @@ def tile_moe_bdx_mlp_silu_kernel(tc, dy_words, dy_scales, a, w2, w1, gate, offs,
 
         def second_layer(kt, pair):
             if pair == 0:
-                dx[kt] = ring.tile([P, S], F32, name="dx", tag="dx", bufs=3)
-            bank = psum.tile([P, 2 * C], F32, name="bank", tag="bank", bufs=5)
+                if kt < 1:
+                    host = w1_tile[kt]
+                elif kt + 1 < KT:
+                    host = w1_tile[kt + 1]
+                else:
+                    host = ring.tile([P, E * PACK * P], F32, name="w1_tile", tag="w1_tile", bufs=4)
+                dx[kt] = host[:, S : S + S]
+            bank = psum.tile([P, 2 * C], F32, name="bank", tag="bank", bufs=4)
             for n in range(2):
                 e = 2 * pair + n
                 nc.tensor.matmul_mx(
@@ -220,17 +228,21 @@ def tile_moe_bdx_mlp_silu_kernel(tc, dy_words, dy_scales, a, w2, w1, gate, offs,
             nc.scalar.copy(out=dx[kt][:, 2 * C * pair : 2 * C * (pair + 1)], in_=bank[:])
 
         def combine(kt):
-            if kt + 1 < KT:
+            if 2 <= kt + 1 < KT:
                 room = w1_grouped[kt + 1]
             else:
                 room = ring.tile([P, E * P * PACK], BF16, name="w1_grouped", tag="w1_grouped", bufs=4, align_bytes=64)
-            picked = [room[:, 2 * T * r : 2 * T * (r + 1)].bitcast(F32) for r in range(3)]
+            picked = [room[:, 2 * T * r : 2 * T * (r + 1)].bitcast(F32) for r in (0, 1, 2)]
             total = ring.tile([P, T], F32, name="total", tag="total")
-            for r in range(3):
-                nc.vector.tensor_copy(picked[r], dx[kt][:].indirect(pos_t[r][:]))
-            nc.vector.tensor_tensor(out=picked[0], in0=picked[0], in1=picked[1], op=ALU.add)
-            nc.vector.tensor_tensor(out=total[:], in0=picked[0], in1=picked[2], op=ALU.add)
-            nc.sync.dma_start(out=out[P * kt : P * (kt + 1), :], in_=total[:])
+            add = nc.gpsimd.tensor_tensor if kt < 0 else nc.vector.tensor_tensor
+            parts = 2 if kt == KT - 1 else 1
+            for part in range(parts):
+                cols = slice(T // parts * part, T // parts * (part + 1))
+                for r in range(3):
+                    nc.vector.tensor_copy(picked[r][:, cols], dx[kt].indirect(pos_t[r][:, cols.start // 16 : cols.stop // 16]))
+                add(out=picked[0][:, cols], in0=picked[0][:, cols], in1=picked[1][:, cols], op=ALU.add)
+                add(out=total[:, cols], in0=picked[0][:, cols], in1=picked[2][:, cols], op=ALU.add)
+                nc.sync.dma_start(out=out[P * kt : P * (kt + 1), cols], in_=total[:, cols])
 
         for e in range(1):
             gather_dy(e)
@@ -245,16 +257,25 @@ def tile_moe_bdx_mlp_silu_kernel(tc, dy_words, dy_scales, a, w2, w1, gate, offs,
             quantize_w2(e, 1)
             if e + 1 < E:
                 make_factor(e + 1)
+            if e == E - 1:
+                quantize_w1(0, (0, 1, 2, 3))
+                quantize_w1(0, (4, 5))
             first_product(e)
             if e + 1 < E:
                 gather_dy(e + 1)
             quantize_da(e)
-        for kt in range(2):
+        for kt in range(1, 1):
             quantize_w1(kt, (0, 1, 2, 3))
             quantize_w1(kt, (4, 5))
         for pair in range(3):
             second_layer(0, pair)
+        for kt in range(1, 2):
+            quantize_w1(kt, (0, 1, 2, 3))
+            quantize_w1(kt, (4, 5))
         for kt in range(KT):
+            if False:
+                for pair in range(3):
+                    second_layer(kt + 1, pair)
             if kt + 2 < KT:
                 quantize_w1(kt + 2, (0, 1, 2, 3))
                 quantize_w1(kt + 2, (4, 5))

@@ -21,8 +21,8 @@ P = 128
 PACK = 4
 PASSES = N // (P * PACK)
 KT = K // P
-VM = ((0,32),(0,32),(0,32),(0,32),(0,32),(0,64))
-W1_ENG = {}
+VM = ((0,16),(0,32),(0,48),(0,32),(0,32),(0,32))
+W1_ENG = {(1, 5): "v", (1, 4): "v"}
 W1_CHUNKS = ((0, 256), (256, 256), (512, 256))
 
 
@@ -134,10 +134,10 @@ def tile_moe_bdx_mlp_silu_kernel(tc, dy_words, dy_scales, a, w2, w1, gate, offs,
             dst = grouped[e, o][:].rearrange("p (t m j) -> p m j t", t=PACK, j=PACK)
             cut = P - VM[e][o]
             if cut > 0:
-                for t in (0, 2):
-                    nc.scalar.copy(out=dst[:, :cut, :, t : t + 2], in_=src[:, :cut, :, t : t + 2])
+                nc.scalar.copy(out=dst[:, :cut], in_=src[:, :cut])
             if cut < P:
-                nc.vector.tensor_copy(out=dst[:, cut:], in_=src[:, cut:])
+                for t in (0, 2):
+                    nc.vector.tensor_copy(out=dst[:, cut:, :, t : t + 2], in_=src[:, cut:, :, t : t + 2])
 
         def quantize_w2(e, o):
             codes[e, o] = ring.tile([P, H], U32, name="w2_codes", tag="w2_codes", bufs=4, align_bytes=64)
@@ -188,7 +188,7 @@ def tile_moe_bdx_mlp_silu_kernel(tc, dy_words, dy_scales, a, w2, w1, gate, offs,
 
         def quantize_w1(kt, experts):
             if experts[0] == 0:
-                w1_grouped[kt] = ring.tile([P, E * P * PACK], BF16, name="w1_grouped", tag="w1_grouped", bufs=4, align_bytes=64)
+                w1_grouped[kt] = ring.tile([P, E * P * PACK], BF16, name="w1_grouped", tag="w1_grouped", bufs=3, align_bytes=64)
                 w1_codes[kt] = ring.tile([P, E * P], U32, name="w1_codes", tag="w1_codes", bufs=3, align_bytes=64)
                 w1_scales[kt] = ring.tile([P, E * P], U8, name="w1_scales", tag="w1_scales", bufs=3, align_bytes=64)
             for e in experts:
@@ -212,7 +212,7 @@ def tile_moe_bdx_mlp_silu_kernel(tc, dy_words, dy_scales, a, w2, w1, gate, offs,
                     host = w1_tile[kt + 1]
                 else:
                     host = ring.tile([P, E * PACK * P], F32, name="w1_tile", tag="w1_tile", bufs=4)
-                dx[kt] = host[:, S : S + S]
+                dx[kt] = host[:, 512 : 512 + S]
             bank = psum.tile([P, 2 * C], F32, name="bank", tag="bank", bufs=4)
             for n in range(2):
                 e = 2 * pair + n
@@ -231,17 +231,18 @@ def tile_moe_bdx_mlp_silu_kernel(tc, dy_words, dy_scales, a, w2, w1, gate, offs,
             if 2 <= kt + 1 < KT:
                 room = w1_grouped[kt + 1]
             else:
-                room = ring.tile([P, E * P * PACK], BF16, name="w1_grouped", tag="w1_grouped", bufs=4, align_bytes=64)
-            picked = [room[:, 2 * T * r : 2 * T * (r + 1)].bitcast(F32) for r in (0, 1, 2)]
+                room = ring.tile([P, E * P * PACK], BF16, name="w1_grouped", tag="w1_grouped", bufs=3, align_bytes=64)
+            picked = [ring.tile([P, T], F32, name=f"picked{r}", tag=f"picked{r}", bufs=2) for r in range(2)]
+            picked.append(room[:, 2048 : 2048 + 2 * T].bitcast(F32))
             total = ring.tile([P, T], F32, name="total", tag="total")
-            add = nc.gpsimd.tensor_tensor if kt < 0 else nc.vector.tensor_tensor
+            add = nc.gpsimd.tensor_tensor if kt < 5 else nc.vector.tensor_tensor
             parts = 2 if kt == KT - 1 else 1
             for part in range(parts):
                 cols = slice(T // parts * part, T // parts * (part + 1))
                 for r in range(3):
                     nc.vector.tensor_copy(picked[r][:, cols], dx[kt].indirect(pos_t[r][:, cols.start // 16 : cols.stop // 16]))
-                add(out=picked[0][:, cols], in0=picked[0][:, cols], in1=picked[1][:, cols], op=ALU.add)
-                add(out=total[:, cols], in0=picked[0][:, cols], in1=picked[2][:, cols], op=ALU.add)
+                add(out=picked[1][:, cols], in0=picked[1][:, cols], in1=picked[2][:, cols], op=ALU.add)
+                add(out=total[:, cols], in0=picked[0][:, cols], in1=picked[1][:, cols], op=ALU.add)
                 nc.sync.dma_start(out=out[P * kt : P * (kt + 1), cols], in_=total[:, cols])
 
         for e in range(1):

@@ -1,11 +1,12 @@
 from contextlib import ExitStack
 
 import concourse.mybir as mybir
+from concourse.masks import make_identity
 
 K, T, E, C, H, N = 768, 512, 6, 256, 512, 1024
 S = E * C
 FLOPS = 2 * S * (N * H + H * K)
-BYTES = N * T + N * T // 32 + 4 * (H * S + E * N * H + E * H * K + 128 * S + K * T) + 2 * 128 * (S + 3 * T) // 16
+BYTES = N * T + N * T // 32 + 4 * (H * S + E * N * H + E * H * K + S + K * T) + 2 * 128 * (S + 3 * T) // 16
 
 F32 = mybir.dt.float32
 BF16 = mybir.dt.bfloat16
@@ -21,9 +22,10 @@ P = 128
 PACK = 4
 PASSES = N // (P * PACK)
 KT = K // P
-VM = ((0,16),(0,32),(0,48),(0,32),(0,32),(0,32))
-W1_ENG = {(1, 5): "v", (1, 4): "v"}
-W1_CHUNKS = ((0, 256), (256, 256), (512, 256))
+BLOCKS = S // P
+RUN = 4
+W2_VECTOR_COLS = 128
+W1_SCALAR_EXPERTS = 6
 
 
 def tile_moe_bdx_mlp_silu_kernel(tc, dy_words, dy_scales, a, w2, w1, gate, offs, pos1, pos2, pos3, out):
@@ -34,253 +36,197 @@ def tile_moe_bdx_mlp_silu_kernel(tc, dy_words, dy_scales, a, w2, w1, gate, offs,
         ring = ctx.enter_context(tc.tile_pool(name="ring", bufs=2))
         psum = ctx.enter_context(tc.psum_pool(name="psum", bufs=1))
 
+        def room(n, shape, name):
+            return keep.tile(shape, F32, name=name, tag=f"room{n}", align_bytes=64)
+
+        banks = [psum.tile([P, 512], F32, name=f"bank{b}") for b in range(8)]
+
         offs_t = lists.tile([P, S // 16], U16, name="offs_t")
         pos_t = [lists.tile([P, T // 16], U16, name=f"pos_t{r}") for r in range(3)]
         words = keep.tile([P, PASSES, T], I32, name="words", align_bytes=64)
         plane = keep.tile([P, T // 4], I32, name="plane", align_bytes=64)
+        ident = keep.tile([P, P], F32, name="ident")
+        gate_rows = keep.tile([P, P], F32, name="gate_rows")
+        neg_gate = keep.tile([P, BLOCKS], F32, name="neg_gate")
 
+        make_identity(nc, ident[:])
+        nc.gpsimd.memset(gate_rows[:], 0.0)
+        nc.gpsimd.dma_start(out=gate_rows[0:BLOCKS, :], in_=gate[0, :].rearrange("(b c) -> b c", c=P))
         nc.vector.memset(plane[:], 0)
-        nc.sync.dma_start(offs_t[:], offs)
+
+        a_rows = a.rearrange("(t p) s -> p t s", p=P)
+        a_t = [room(n, [P, PACK, 2 * C], f"a_t{n}") for n in range(3)]
         words_i32 = dy_words.rearrange("o p t d -> p o (t d)").bitcast(I32)
-        nc.sync.dma_start(out=words[:, 0, :], in_=words_i32[:, 0, :])
         scales_i32 = dy_scales.bitcast(I32)
+
+        nc.sync.dma_start(out=a_t[0][:, :, 0:C], in_=a_rows[:, :, 0:C])
+        nc.sync.dma_start(offs_t[:], offs)
+        nc.sync.dma_start(out=words[:, 0, :], in_=words_i32[:, 0, :])
+        nc.sync.dma_start(out=words[:, 1, :], in_=words_i32[:, 1, :])
         for q in range(4):
             nc.sync.dma_start(out=plane[32 * q : 32 * q + 8, :], in_=scales_i32[:, 4 * q : 4 * q + 4, :])
+        nc.sync.dma_start(out=a_t[0][:, :, C : 2 * C], in_=a_rows[:, :, C : 2 * C])
+        for n in (1, 2):
+            nc.sync.dma_start(out=a_t[n][:], in_=a_rows[:, :, 2 * C * n : 2 * C * (n + 1)])
+        factor = [room(3 + n, [P, 4, H], f"factor{n}") for n in range(3)]
 
-        a_rows = a.rearrange("(p j) s -> p j s", j=PACK)
-        a_t, gate_t, w2_raw, w1_raw = {}, {}, {}, {}
+        w2_raw = {}
+        for e in range(E):
+            for o in range(PASSES):
+                w2_raw[e, o] = room(6 + (PASSES * e + o) % 9, [P, PACK, H], f"w2_raw{e}_{o}")
+                nc.sync.dma_start(out=w2_raw[e, o][:], in_=w2[e, 512 * o : 512 * (o + 1), :].rearrange("(p j) i -> p j i", j=PACK))
 
-        def load_a(first, count):
-            tile = ring.tile([P, PACK, count * C], F32, name="a_t", tag="a_t", bufs=3)
-            nc.sync.dma_start(out=tile[:], in_=a_rows[:, :, C * first : C * (first + count)])
-            for n in range(count):
-                a_t[first + n] = tile[:, :, C * n : C * (n + 1)]
-
-        def load_gate(first, count):
-            tile = keep.tile([P, count * C], F32, name=f"gate{first}")
-            nc.sync.dma_start(out=tile[:], in_=gate[0:P, C * first : C * (first + count)])
-            for cols in (slice(0, 2 * C), slice(2 * C, count * C)):
-                nc.gpsimd.tensor_scalar(out=tile[:, cols], in0=tile[:, cols], scalar1=-0.5, scalar2=0.0, op0=ALU.mult, op1=ALU.add)
-            for n in range(count):
-                gate_t[first + n] = tile[:, C * n : C * (n + 1)]
-
-        def load_w2(e, o):
-            raw = ring.tile([P, PACK, H], F32, name="raw", tag="raw", bufs=5)
-            nc.sync.dma_start(out=raw[:], in_=w2[e, 512 * o : 512 * (o + 1), :].rearrange("(p j) i -> p j i", j=PACK))
-            w2_raw[e, o] = raw
-
-        def load_lists():
-            for r, pos in enumerate((pos1, pos2, pos3)):
-                nc.sync.dma_start(pos_t[r][:], pos)
-
-        w1_tile = {}
-
-        def load_w1(kt, experts):
-            if kt not in w1_tile:
-                w1_tile[kt] = ring.tile([P, E * PACK * P], F32, name="w1_tile", tag="w1_tile", bufs=4)
-            for e in experts:
-                w1_raw[kt, e] = w1_tile[kt][:, PACK * P * e : PACK * P * (e + 1)].rearrange("p (j k) -> p j k", j=PACK)
-                nc.sync.dma_start(out=w1_raw[kt, e], in_=w1[e].rearrange("(p j) k -> p j k", j=PACK)[:, :, P * kt : P * (kt + 1)])
-
-        load_a(0, 1)
-        nc.sync.dma_start(out=words[:, 1, :], in_=words_i32[:, 1, :])
-        load_w2(0, 0)
-        load_gate(0, 6)
-        load_a(1, 1)
-        load_w2(0, 1)
-        load_w2(1, 0)
-        load_a(2, 1)
-        load_w2(1, 1)
-        load_w2(2, 0)
-        load_a(3, 1)
-        load_w2(2, 1)
-        load_w2(3, 0)
-        load_a(4, 1)
-        load_w2(3, 1)
-        load_w2(4, 0)
-        load_a(5, 1)
-        load_w2(4, 1)
-        load_w1(0, range(0, 4))
-        load_w2(5, 0)
-        load_w2(5, 1)
-        load_w1(0, range(4, E))
-        load_lists()
-        for kt in range(1, KT):
-            load_w1(kt, range(E))
-
-        g_words, g_scales = {}, {}
-
-        def gather_dy(e):
-            g_words[e] = ring.tile([P, PASSES, C], U32, name="g_words", tag="g_words", bufs=4, align_bytes=64)
-            g_scales[e] = ring.tile([P, C], U8, name="g_scales", tag="g_scales", bufs=4, align_bytes=64)
+        g_words = keep.tile([P, PASSES, S], U32, name="g_words", align_bytes=64)
+        g_scales = keep.tile([P, S], U8, name="g_scales", align_bytes=64)
+        for e in range(E):
             slots = offs_t[:, 16 * e : 16 * (e + 1)]
             for o in range(PASSES):
-                nc.vector.tensor_copy(g_words[e][:, o, :], words[:, o, :].bitcast(U32).indirect(slots))
-            nc.vector.tensor_copy(g_scales[e][:], plane[:].bitcast(U8).indirect(slots))
+                nc.vector.tensor_copy(g_words[:, o, C * e : C * (e + 1)], words[:, o, :].bitcast(U32).indirect(slots))
+            nc.vector.tensor_copy(g_scales[:, C * e : C * (e + 1)], plane[:].bitcast(U8).indirect(slots))
 
-        da_codes, da_scales = {}, {}
+        def turn_a(b):
+            bank = banks[b % 2]
+            for t in range(PACK):
+                nc.tensor.transpose(bank[:, P * t : P * (t + 1)], a_t[b // 4][:, t, P * (b % 4) : P * (b % 4 + 1)], ident[:])
+            return bank
 
-        silu_neg, factor, codes, scales, grouped, da = {}, {}, {}, {}, {}, {}
+        for b in range(BLOCKS):
+            nc.scalar.activation(out=factor[b // 4][:, b % 4, :], in_=turn_a(b)[:], func=ACT.Sigmoid)
 
-        def activations(e):
-            silu_neg[e] = ring.tile([P, PACK, C], F32, name="silu_neg", tag="silu_neg", bufs=3)
-            factor[e] = ring.tile([P, PACK, C], F32, name="factor", tag="factor", bufs=3)
-            nc.scalar.activation(out=silu_neg[e][:], in_=a_t[e], func=ACT.Silu, scale=-1.0)
-            nc.scalar.activation(out=factor[e][:], in_=a_t[e], func=ACT.Tanh, scale=0.5)
+        nc.tensor.transpose(banks[7][:, 0:P], gate_rows[:], ident[:])
+        nc.vector.tensor_scalar(out=neg_gate[:], in0=banks[7][:, 0:BLOCKS], scalar1=-1.0, scalar2=None, op0=ALU.mult)
 
-        def cast_w2(e, o):
-            grouped[e, o] = ring.tile([P, PACK * H], BF16, name="w2_grouped", tag="w2_grouped", bufs=5, align_bytes=64)
-            src = w2_raw[e, o][:].rearrange("p j (m t) -> p m j t", t=PACK)
-            dst = grouped[e, o][:].rearrange("p (t m j) -> p m j t", t=PACK, j=PACK)
-            cut = P - VM[e][o]
-            if cut > 0:
-                nc.scalar.copy(out=dst[:, :cut], in_=src[:, :cut])
-            if cut < P:
-                for t in (0, 2):
-                    nc.vector.tensor_copy(out=dst[:, cut:, :, t : t + 2], in_=src[:, cut:, :, t : t + 2])
+        def make_factor(b):
+            silu_neg = ring.tile([P, H], F32, name="silu_neg", tag="silu_neg", bufs=3)
+            nc.scalar.activation(out=silu_neg[:], in_=turn_a(b)[:], func=ACT.Silu, scale=-1.0)
+            f = factor[b // 4][:, b % 4, :]
+            nc.vector.scalar_tensor_tensor(out=f, in0=silu_neg[:], scalar=1.0, in1=f, op0=ALU.subtract, op1=ALU.mult)
+
+        codes, scales, da_codes, da_scales = {}, {}, {}, {}
 
         def quantize_w2(e, o):
+            grouped = ring.tile([P, PACK * H], BF16, name="grouped", tag="grouped", bufs=5, align_bytes=64)
+            src = w2_raw[e, o][:].rearrange("p j (c i) -> p c j i", i=RUN)
+            dst = grouped[:].rearrange("p (c i j) -> p c j i", i=RUN, j=PACK)
+            cut = (H - W2_VECTOR_COLS) // RUN
+            nc.scalar.copy(out=dst[:, :cut], in_=src[:, :cut])
+            nc.vector.tensor_copy(out=dst[:, cut:], in_=src[:, cut:])
             codes[e, o] = ring.tile([P, H], U32, name="w2_codes", tag="w2_codes", bufs=4, align_bytes=64)
             scales[e, o] = ring.tile([P, H], U8, name="w2_scales", tag="w2_scales", bufs=4, align_bytes=64)
-            nc.vector.quantize_mx(out=codes[e, o][:].bitcast(FP8X4), scales=scales[e, o][:], in_=grouped[e, o][:])
-
-        def make_factor(e):
-            gate_e = gate_t[e].unsqueeze(1).to_broadcast([P, PACK, C])
-            if e > 0:
-                room = grouped[e - 1, 1][:].bitcast(F32).rearrange("p (j s) -> p j s", j=PACK)
-            else:
-                room = silu_neg[e][:]
-            nc.vector.scalar_tensor_tensor(out=room, in0=silu_neg[e][:], scalar=1.0, in1=gate_e, op0=ALU.subtract, op1=ALU.mult)
-            nc.vector.scalar_tensor_tensor(out=factor[e][:], in0=factor[e][:], scalar=1.0, in1=room, op0=ALU.add, op1=ALU.mult)
+            nc.vector.quantize_mx(out=codes[e, o][:].bitcast(FP8X4), scales=scales[e, o][:], in_=grouped[:])
 
         def first_product(e):
-            if e == E - 1:
-                da[e] = w1_grouped[0][:, 0 : 0 + C * PACK]
-            else:
-                da[e] = ring.tile([P, C * PACK], BF16, name="da", tag="da", align_bytes=64)
-            for h in range(C // P):
-                cols = slice(P * h, P * (h + 1))
-                acc = psum.tile([P, PACK, P], F32, name="acc", tag="acc", bufs=4)
-                for t in range(PACK):
-                    for o in range(PASSES):
-                        nc.tensor.matmul_mx(
-                            out=acc[:, t, :],
-                            lhsT=codes[e, o][:, P * t : P * (t + 1)].bitcast(FP8X4),
-                            lhsT_scale=scales[e, o][:, P * t : P * (t + 1)],
-                            rhs=g_words[e][:, o, cols].bitcast(FP8X4),
-                            rhs_scale=g_scales[e][4 * o : P, cols],
-                            start=(o == 0),
-                            stop=(o == PASSES - 1),
-                        )
-                nc.vector.tensor_tensor(
-                    out=da[e][:, PACK * P * h : PACK * P * (h + 1)].rearrange("p (c i j) -> p c j i", i=4, j=PACK),
-                    in0=acc[:].rearrange("p j (c i) -> p c j i", i=4),
-                    in1=factor[e][:, :, cols].rearrange("p j (c i) -> p c j i", i=4),
-                    op=ALU.mult,
+            turned = banks[5 + e % 2][:].rearrange("p (h u r) -> p h u r", h=2, u=2)
+            for h in range(2):
+                b = 2 * e + h
+                cols = slice(P * b, P * (b + 1))
+                acc = banks[2 + b % 3]
+                for o in range(PASSES):
+                    nc.tensor.matmul_mx(
+                        out=acc[:],
+                        lhsT=g_words[:, o, cols].bitcast(FP8X4),
+                        lhsT_scale=g_scales[4 * o : P, cols],
+                        rhs=codes[e, o][:].bitcast(FP8X4),
+                        rhs_scale=scales[e, o][:],
+                        start=(o == 0),
+                        stop=(o == PASSES - 1),
+                    )
+                da_rows = ring.tile([P, H], BF16, name="da_rows", tag="da_rows", bufs=3, align_bytes=64)
+                nc.vector.scalar_tensor_tensor(
+                    out=da_rows[:], in0=acc[:], scalar=neg_gate[:, b : b + 1], in1=factor[b // 4][:, b % 4, :], op0=ALU.mult, op1=ALU.mult
                 )
-
-        def quantize_da(e):
+                pairs = da_rows[:].bitcast(F32)
+                for u in range(2):
+                    nc.tensor.transpose(turned[:, h, u, :], pairs[:, u : H // 2 : 2], ident[:])
+            da = ring.tile([P, C * PACK], BF16, name="da", tag="da", bufs=2, align_bytes=64)
+            nc.scalar.copy(out=da[:].bitcast(F32).rearrange("p (h r u) -> p h r u", h=2, u=2), in_=turned.rearrange("p h u r -> p h r u"))
             da_codes[e] = keep.tile([P, C], U32, name=f"da_codes{e}", align_bytes=64)
             da_scales[e] = keep.tile([P, C], U8, name=f"da_scales{e}", align_bytes=64)
-            nc.vector.quantize_mx(out=da_codes[e][:].bitcast(FP8X4), scales=da_scales[e][:], in_=da[e][:, :])
+            nc.vector.quantize_mx(out=da_codes[e][:].bitcast(FP8X4), scales=da_scales[e][:], in_=da[:])
 
-        w1_grouped, w1_codes, w1_scales, dx = {}, {}, {}, {}
-
-        def quantize_w1(kt, experts):
-            if experts[0] == 0:
-                w1_grouped[kt] = ring.tile([P, E * P * PACK], BF16, name="w1_grouped", tag="w1_grouped", bufs=3, align_bytes=64)
-                w1_codes[kt] = ring.tile([P, E * P], U32, name="w1_codes", tag="w1_codes", bufs=3, align_bytes=64)
-                w1_scales[kt] = ring.tile([P, E * P], U8, name="w1_scales", tag="w1_scales", bufs=3, align_bytes=64)
-            for e in experts:
-                copy = {"v": nc.vector.tensor_copy, "g": nc.gpsimd.tensor_copy}.get(W1_ENG.get((kt, e)), nc.scalar.copy)
-                copy(
-                    out=w1_grouped[kt][:, PACK * P * e : PACK * P * (e + 1)].rearrange("p (c i j) -> p c j i", i=4, j=PACK),
-                    in_=w1_raw[kt, e].rearrange("p j (c i) -> p c j i", i=4),
-                )
-            cols = slice(P * experts[0], P * (experts[-1] + 1))
-            nc.vector.quantize_mx(
-                out=w1_codes[kt][:, cols].bitcast(FP8X4),
-                scales=w1_scales[kt][:, cols],
-                in_=w1_grouped[kt][:, PACK * cols.start : PACK * cols.stop],
-            )
-
-        def second_layer(kt, pair):
-            if pair == 0:
-                if kt < 1:
-                    host = w1_tile[kt]
-                elif kt + 1 < KT:
-                    host = w1_tile[kt + 1]
-                else:
-                    host = ring.tile([P, E * PACK * P], F32, name="w1_tile", tag="w1_tile", bufs=4)
-                dx[kt] = host[:, 512 : 512 + S]
-            bank = psum.tile([P, 2 * C], F32, name="bank", tag="bank", bufs=4)
-            for n in range(2):
-                e = 2 * pair + n
-                nc.tensor.matmul_mx(
-                    out=bank[:, C * n : C * (n + 1)],
-                    lhsT=w1_codes[kt][:, P * e : P * (e + 1)].bitcast(FP8X4),
-                    lhsT_scale=w1_scales[kt][:, P * e : P * (e + 1)],
-                    rhs=da_codes[e][:].bitcast(FP8X4),
-                    rhs_scale=da_scales[e][:],
-                    start=True,
-                    stop=True,
-                )
-            nc.scalar.copy(out=dx[kt][:, 2 * C * pair : 2 * C * (pair + 1)], in_=bank[:])
-
-        def combine(kt):
-            if 2 <= kt + 1 < KT:
-                room = w1_grouped[kt + 1]
-            else:
-                room = ring.tile([P, E * P * PACK], BF16, name="w1_grouped", tag="w1_grouped", bufs=3, align_bytes=64)
-            picked = [ring.tile([P, T], F32, name=f"picked{r}", tag=f"picked{r}", bufs=2) for r in range(2)]
-            picked.append(room[:, 2048 : 2048 + 2 * T].bitcast(F32))
-            total = ring.tile([P, T], F32, name="total", tag="total")
-            add = nc.gpsimd.tensor_tensor if kt < 5 else nc.vector.tensor_tensor
-            parts = 2 if kt == KT - 1 else 1
-            for part in range(parts):
-                cols = slice(T // parts * part, T // parts * (part + 1))
-                for r in range(3):
-                    nc.vector.tensor_copy(picked[r][:, cols], dx[kt].indirect(pos_t[r][:, cols.start // 16 : cols.stop // 16]))
-                add(out=picked[1][:, cols], in0=picked[1][:, cols], in1=picked[2][:, cols], op=ALU.add)
-                add(out=total[:, cols], in0=picked[0][:, cols], in1=picked[1][:, cols], op=ALU.add)
-                nc.sync.dma_start(out=out[P * kt : P * (kt + 1), cols], in_=total[:, cols])
-
-        for e in range(1):
-            gather_dy(e)
-        activations(0)
         make_factor(0)
+        make_factor(1)
         for e in range(E):
-            cast_w2(e, 0)
             quantize_w2(e, 0)
-            if e + 1 < E:
-                activations(e + 1)
-            cast_w2(e, 1)
             quantize_w2(e, 1)
             if e + 1 < E:
-                make_factor(e + 1)
-            if e == E - 1:
-                quantize_w1(0, (0, 1, 2, 3))
-                quantize_w1(0, (4, 5))
+                make_factor(2 * e + 2)
+                make_factor(2 * e + 3)
             first_product(e)
-            if e + 1 < E:
-                gather_dy(e + 1)
-            quantize_da(e)
-        for kt in range(1, 1):
-            quantize_w1(kt, (0, 1, 2, 3))
-            quantize_w1(kt, (4, 5))
-        for pair in range(3):
-            second_layer(0, pair)
-        for kt in range(1, 2):
-            quantize_w1(kt, (0, 1, 2, 3))
-            quantize_w1(kt, (4, 5))
+
+        w1_raw, w1_codes, w1_scales, dx = {}, {}, {}, {}
+        groups = ((0, 4), (4, 2))
+
+        def load_w1(kt):
+            for first, count in groups:
+                if first == 0:
+                    raw = room(9 + kt, [P, count, PACK, P], f"w1_raw{kt}")
+                else:
+                    raw = ring.tile([P, count, PACK, P], F32, name="w1_rest", tag="w1_rest", bufs=3)
+                w1_raw[kt, first] = raw
+                for n in range(count):
+                    nc.sync.dma_start(out=raw[:, n], in_=w1[first + n].rearrange("(p j) k -> p j k", j=PACK)[:, :, P * kt : P * (kt + 1)])
+
+        def quantize_w1(kt):
+            w1_codes[kt] = ring.tile([P, E * P], U32, name="w1_codes", tag="w1_codes", bufs=3, align_bytes=64)
+            w1_scales[kt] = ring.tile([P, E * P], U8, name="w1_scales", tag="w1_scales", bufs=3, align_bytes=64)
+            for first, count in groups:
+                grouped = ring.tile([P, count * P * PACK], BF16, name="grouped", tag="grouped", bufs=5, align_bytes=64)
+                src = w1_raw[kt, first][:].rearrange("p e j (c i) -> p e c j i", i=RUN)
+                dst = grouped[:].rearrange("p (e c i j) -> p e c j i", e=count, i=RUN, j=PACK)
+                for n in range(count):
+                    copy = nc.scalar.copy if first + n < W1_SCALAR_EXPERTS else nc.vector.tensor_copy
+                    copy(out=dst[:, n], in_=src[:, n])
+                cols = slice(P * first, P * (first + count))
+                nc.vector.quantize_mx(out=w1_codes[kt][:, cols].bitcast(FP8X4), scales=w1_scales[kt][:, cols], in_=grouped[:])
+
+        def second_product(kt):
+            dx[kt] = room({0: 0, 4: 1, 5: 2}.get(kt, 10 + kt), [P, S], f"dx{kt}")
+            for pair in range(E // 2):
+                bank = banks[(7, 0, 1, 2, 3, 4)[(3 * kt + pair) % 6]]
+                for n in range(2):
+                    e = 2 * pair + n
+                    nc.tensor.matmul_mx(
+                        out=bank[:, C * n : C * (n + 1)],
+                        lhsT=w1_codes[kt][:, P * e : P * (e + 1)].bitcast(FP8X4),
+                        lhsT_scale=w1_scales[kt][:, P * e : P * (e + 1)],
+                        rhs=da_codes[e][:].bitcast(FP8X4),
+                        rhs_scale=da_scales[e][:],
+                        start=True,
+                        stop=True,
+                    )
+                nc.scalar.copy(out=dx[kt][:, 2 * C * pair : 2 * C * (pair + 1)], in_=bank[:])
+
         for kt in range(KT):
-            if False:
-                for pair in range(3):
-                    second_layer(kt + 1, pair)
+            load_w1(kt)
+            if kt == 0:
+                for r, pos in enumerate((pos1, pos2, pos3)):
+                    nc.sync.dma_start(pos_t[r][:], pos)
+
+        totals = [room(3, [P, 4, T], "totals0"), room(4, [P, 2, T], "totals1")]
+        partial = room(5, [P, 2, 2, T], "partial")
+
+        def combine(kt):
+            total = totals[kt // 4][:, kt % 4, :]
+            first, second = partial[:, kt % 2, 0, :], partial[:, kt % 2, 1, :]
+            halves = [(slice(T // 2 * n, T // 2 * (n + 1)), slice(T // 32 * n, T // 32 * (n + 1))) for n in range(2)]
+            for cols, part in halves:
+                nc.vector.tensor_copy(first[:, cols], dx[kt][:].indirect(pos_t[0][:, part]))
+            for cols, part in halves:
+                nc.vector.tensor_tensor(second[:, cols], dx[kt][:].indirect(pos_t[1][:, part]), first[:, cols], ALU.add)
+            for cols, part in halves:
+                nc.vector.tensor_tensor(total[:, cols], dx[kt][:].indirect(pos_t[2][:, part]), second[:, cols], ALU.add)
+                if kt == KT - 1:
+                    nc.sync.dma_start(out=out[P * kt : P * (kt + 1), cols], in_=total[:, cols])
+            if kt < KT - 1:
+                nc.sync.dma_start(out=out[P * kt : P * (kt + 1), :], in_=total)
+
+        quantize_w1(0)
+        second_product(0)
+        quantize_w1(1)
+        for kt in range(KT):
             if kt + 2 < KT:
-                quantize_w1(kt + 2, (0, 1, 2, 3))
-                quantize_w1(kt + 2, (4, 5))
+                quantize_w1(kt + 2)
             if kt + 1 < KT:
-                for pair in range(3):
-                    second_layer(kt + 1, pair)
+                second_product(kt + 1)
             combine(kt)

@@ -23,7 +23,7 @@ PACK = 4
 PASSES = N // (P * PACK)
 KT = K // P
 BLOCKS = S // P
-RUN = 4
+RUN = 2
 W2_VECTOR_COLS = 128
 W1_SCALAR_EXPERTS = 6
 

@@ -24,8 +24,9 @@ PASSES = N // (P * PACK)
 KT = K // P
 BLOCKS = S // P
 RUN = 2
-W2_VECTOR_COLS = 128
-W1_SCALAR_EXPERTS = 6
+GATHER = 384
+W2_VECTOR_COLS = 256
+W1_SCALAR_EXPERTS = 5
 
 
 def tile_moe_bdx_mlp_silu_kernel(tc, dy_words, dy_scales, a, w2, w1, gate, offs, pos1, pos2, pos3, out):
@@ -59,58 +60,63 @@ def tile_moe_bdx_mlp_silu_kernel(tc, dy_words, dy_scales, a, w2, w1, gate, offs,
         words_i32 = dy_words.rearrange("o p t d -> p o (t d)").bitcast(I32)
         scales_i32 = dy_scales.bitcast(I32)
 
-        nc.sync.dma_start(out=a_t[0][:, :, 0:C], in_=a_rows[:, :, 0:C])
         nc.sync.dma_start(offs_t[:], offs)
         nc.sync.dma_start(out=words[:, 0, :], in_=words_i32[:, 0, :])
+        nc.sync.dma_start(out=a_t[0][:, :, 0:P], in_=a_rows[:, :, 0:P])
         nc.sync.dma_start(out=words[:, 1, :], in_=words_i32[:, 1, :])
         for q in range(4):
             nc.sync.dma_start(out=plane[32 * q : 32 * q + 8, :], in_=scales_i32[:, 4 * q : 4 * q + 4, :])
-        nc.sync.dma_start(out=a_t[0][:, :, C : 2 * C], in_=a_rows[:, :, C : 2 * C])
+        nc.sync.dma_start(out=a_t[0][:, :, P : 2 * C], in_=a_rows[:, :, P : 2 * C])
         for n in (1, 2):
             nc.sync.dma_start(out=a_t[n][:], in_=a_rows[:, :, 2 * C * n : 2 * C * (n + 1)])
-        factor = [room(3 + n, [P, 4, H], f"factor{n}") for n in range(3)]
+        sig = [room(3 + n, [P, 4, H], f"sig{n}") for n in range(3)]
+        silu_neg = [room(6 + n, [P, 4, H], f"silu_neg{n}") for n in range(3)]
 
         w2_raw = {}
         for e in range(E):
             for o in range(PASSES):
-                w2_raw[e, o] = room(6 + (PASSES * e + o) % 9, [P, PACK, H], f"w2_raw{e}_{o}")
+                w2_raw[e, o] = room((9, 10, 11, 12, 13, 14, 0, 1, 2)[(PASSES * e + o) % 9], [P, PACK, H], f"w2_raw{e}_{o}")
                 nc.sync.dma_start(out=w2_raw[e, o][:], in_=w2[e, 512 * o : 512 * (o + 1), :].rearrange("(p j) i -> p j i", j=PACK))
 
         g_words = keep.tile([P, PASSES, S], U32, name="g_words", align_bytes=64)
         g_scales = keep.tile([P, S], U8, name="g_scales", align_bytes=64)
-        for e in range(E):
-            slots = offs_t[:, 16 * e : 16 * (e + 1)]
+        for first in range(0, S, GATHER):
+            slots = offs_t[:, first // 16 : (first + GATHER) // 16]
             for o in range(PASSES):
-                nc.vector.tensor_copy(g_words[:, o, C * e : C * (e + 1)], words[:, o, :].bitcast(U32).indirect(slots))
-            nc.vector.tensor_copy(g_scales[:, C * e : C * (e + 1)], plane[:].bitcast(U8).indirect(slots))
-
-        def turn_a(b):
-            bank = banks[b % 2]
-            for t in range(PACK):
-                nc.tensor.transpose(bank[:, P * t : P * (t + 1)], a_t[b // 4][:, t, P * (b % 4) : P * (b % 4 + 1)], ident[:])
-            return bank
+                nc.vector.tensor_copy(g_words[:, o, first : first + GATHER], words[:, o, :].bitcast(U32).indirect(slots))
+            nc.vector.tensor_copy(g_scales[:, first : first + GATHER], plane[:].bitcast(U8).indirect(slots))
 
         for b in range(BLOCKS):
-            nc.scalar.activation(out=factor[b // 4][:, b % 4, :], in_=turn_a(b)[:], func=ACT.Sigmoid)
+            bank = banks[b % 4]
+            for t in range(PACK):
+                nc.tensor.transpose(bank[:, P * t : P * (t + 1)], a_t[b // 4][:, t, P * (b % 4) : P * (b % 4 + 1)], ident[:])
+            half = sig[b // 4][:, b % 4, :]
+            nc.scalar.activation(out=silu_neg[b // 4][:, b % 4, :], in_=bank[:], func=ACT.Silu, scale=-1.0)
+            nc.scalar.activation(out=half, in_=bank[:], func=ACT.Tanh, scale=0.5)
+            nc.gpsimd.tensor_scalar(out=half, in0=half, scalar1=0.5, scalar2=0.5, op0=ALU.mult, op1=ALU.add)
 
         nc.tensor.transpose(banks[7][:, 0:P], gate_rows[:], ident[:])
         nc.vector.tensor_scalar(out=neg_gate[:], in0=banks[7][:, 0:BLOCKS], scalar1=-1.0, scalar2=None, op0=ALU.mult)
 
-        def make_factor(b):
-            silu_neg = ring.tile([P, H], F32, name="silu_neg", tag="silu_neg", bufs=3)
-            nc.scalar.activation(out=silu_neg[:], in_=turn_a(b)[:], func=ACT.Silu, scale=-1.0)
-            f = factor[b // 4][:, b % 4, :]
-            nc.vector.scalar_tensor_tensor(out=f, in0=silu_neg[:], scalar=1.0, in1=f, op0=ALU.subtract, op1=ALU.mult)
+        codes, scales, da_codes, da_scales, staged, slope = {}, {}, {}, {}, {}, {}
 
-        codes, scales, da_codes, da_scales = {}, {}, {}, {}
+        def make_factor(e):
+            rows = slice(2 * (e % 2), 2 * (e % 2) + 2)
+            slope[e] = sig[0][:, rows, :] if e == 0 else staged[e - 1, 1][:].bitcast(F32).rearrange("p (h i) -> p h i", h=2)
+            nc.vector.scalar_tensor_tensor(
+                out=slope[e], in0=silu_neg[e // 2][:, rows, :], scalar=1.0, in1=sig[e // 2][:, rows, :], op0=ALU.subtract, op1=ALU.mult
+            )
 
         def quantize_w2(e, o):
-            grouped = ring.tile([P, PACK * H], BF16, name="grouped", tag="grouped", bufs=5, align_bytes=64)
+            grouped = ring.tile([P, PACK * H], BF16, name="grouped", tag="grouped", bufs=6, align_bytes=64)
+            staged[e, o] = grouped
             src = w2_raw[e, o][:].rearrange("p j (c i) -> p c j i", i=RUN)
             dst = grouped[:].rearrange("p (c i j) -> p c j i", i=RUN, j=PACK)
-            cut = (H - W2_VECTOR_COLS) // RUN
-            nc.scalar.copy(out=dst[:, :cut], in_=src[:, :cut])
-            nc.vector.tensor_copy(out=dst[:, cut:], in_=src[:, cut:])
+            cut = (H - (H if e == 0 else W2_VECTOR_COLS if o == 1 and e >= 3 else 0)) // RUN
+            if cut > 0:
+                nc.scalar.copy(out=dst[:, :cut], in_=src[:, :cut])
+            if cut < H // RUN:
+                nc.vector.tensor_copy(out=dst[:, cut:], in_=src[:, cut:])
             codes[e, o] = ring.tile([P, H], U32, name="w2_codes", tag="w2_codes", bufs=4, align_bytes=64)
             scales[e, o] = ring.tile([P, H], U8, name="w2_scales", tag="w2_scales", bufs=4, align_bytes=64)
             nc.vector.quantize_mx(out=codes[e, o][:].bitcast(FP8X4), scales=scales[e, o][:], in_=grouped[:])
@@ -133,34 +139,41 @@ def tile_moe_bdx_mlp_silu_kernel(tc, dy_words, dy_scales, a, w2, w1, gate, offs,
                     )
                 da_rows = ring.tile([P, H], BF16, name="da_rows", tag="da_rows", bufs=3, align_bytes=64)
                 nc.vector.scalar_tensor_tensor(
-                    out=da_rows[:], in0=acc[:], scalar=neg_gate[:, b : b + 1], in1=factor[b // 4][:, b % 4, :], op0=ALU.mult, op1=ALU.mult
+                    out=da_rows[:], in0=acc[:], scalar=neg_gate[:, b : b + 1], in1=slope[e][:, h, :], op0=ALU.mult, op1=ALU.mult
                 )
                 pairs = da_rows[:].bitcast(F32)
                 for u in range(2):
                     nc.tensor.transpose(turned[:, h, u, :], pairs[:, u : H // 2 : 2], ident[:])
-            da = ring.tile([P, C * PACK], BF16, name="da", tag="da", bufs=2, align_bytes=64)
-            nc.scalar.copy(out=da[:].bitcast(F32).rearrange("p (h r u) -> p h r u", h=2, u=2), in_=turned.rearrange("p h u r -> p h r u"))
+            return turned
+
+        def quantize_da(e, turned):
+            if e + 1 < E:
+                da = w2_raw[e + 1, 1][:, 0, :].bitcast(BF16)
+            else:
+                da = keep.tile([P, C * PACK], BF16, name="da", align_bytes=64)[:]
+            nc.scalar.copy(out=da.bitcast(F32).rearrange("p (h r u) -> p h r u", h=2, u=2), in_=turned.rearrange("p h u r -> p h r u"))
             da_codes[e] = keep.tile([P, C], U32, name=f"da_codes{e}", align_bytes=64)
             da_scales[e] = keep.tile([P, C], U8, name=f"da_scales{e}", align_bytes=64)
-            nc.vector.quantize_mx(out=da_codes[e][:].bitcast(FP8X4), scales=da_scales[e][:], in_=da[:])
+            nc.vector.quantize_mx(out=da_codes[e][:].bitcast(FP8X4), scales=da_scales[e][:], in_=da)
 
         make_factor(0)
-        make_factor(1)
         for e in range(E):
             quantize_w2(e, 0)
             quantize_w2(e, 1)
+            if e > 0:
+                quantize_da(e - 1, turned)
             if e + 1 < E:
-                make_factor(2 * e + 2)
-                make_factor(2 * e + 3)
-            first_product(e)
+                make_factor(e + 1)
+            turned = first_product(e)
+        quantize_da(E - 1, turned)
 
         w1_raw, w1_codes, w1_scales, dx = {}, {}, {}, {}
-        groups = ((0, 4), (4, 2))
+        groups = ((4, 2), (0, 4))
 
         def load_w1(kt):
             for first, count in groups:
                 if first == 0:
-                    raw = room(9 + kt, [P, count, PACK, P], f"w1_raw{kt}")
+                    raw = room((12, 13, 14, 0, 1, 2)[kt], [P, count, PACK, P], f"w1_raw{kt}")
                 else:
                     raw = ring.tile([P, count, PACK, P], F32, name="w1_rest", tag="w1_rest", bufs=3)
                 w1_raw[kt, first] = raw
@@ -171,7 +184,7 @@ def tile_moe_bdx_mlp_silu_kernel(tc, dy_words, dy_scales, a, w2, w1, gate, offs,
             w1_codes[kt] = ring.tile([P, E * P], U32, name="w1_codes", tag="w1_codes", bufs=3, align_bytes=64)
             w1_scales[kt] = ring.tile([P, E * P], U8, name="w1_scales", tag="w1_scales", bufs=3, align_bytes=64)
             for first, count in groups:
-                grouped = ring.tile([P, count * P * PACK], BF16, name="grouped", tag="grouped", bufs=5, align_bytes=64)
+                grouped = ring.tile([P, count * P * PACK], BF16, name="grouped", tag="grouped", bufs=6, align_bytes=64)
                 src = w1_raw[kt, first][:].rearrange("p e j (c i) -> p e c j i", i=RUN)
                 dst = grouped[:].rearrange("p (e c i j) -> p e c j i", e=count, i=RUN, j=PACK)
                 for n in range(count):
@@ -181,7 +194,7 @@ def tile_moe_bdx_mlp_silu_kernel(tc, dy_words, dy_scales, a, w2, w1, gate, offs,
                 nc.vector.quantize_mx(out=w1_codes[kt][:, cols].bitcast(FP8X4), scales=w1_scales[kt][:, cols], in_=grouped[:])
 
         def second_product(kt):
-            dx[kt] = room({0: 0, 4: 1, 5: 2}.get(kt, 10 + kt), [P, S], f"dx{kt}")
+            dx[kt] = room((6, 14, 0, 1, 7, 8)[kt], [P, S], f"dx{kt}")
             for pair in range(E // 2):
                 bank = banks[(7, 0, 1, 2, 3, 4)[(3 * kt + pair) % 6]]
                 for n in range(2):

@@ -25,8 +25,8 @@ KT = K // P
 BLOCKS = S // P
 RUN = 2
 GATHER = 384
-W2_VECTOR_COLS = 256
-W1_SCALAR_EXPERTS = 5
+W2_GPSIMD_COLS = 128
+EARLY_EXPERTS = 4
 
 
 def tile_moe_bdx_mlp_silu_kernel(tc, dy_words, dy_scales, a, w2, w1, gate, offs, pos1, pos2, pos3, out):
@@ -70,7 +70,11 @@ def tile_moe_bdx_mlp_silu_kernel(tc, dy_words, dy_scales, a, w2, w1, gate, offs,
         for n in (1, 2):
             nc.sync.dma_start(out=a_t[n][:], in_=a_rows[:, :, 2 * C * n : 2 * C * (n + 1)])
         sig = [room(3 + n, [P, 4, H], f"sig{n}") for n in range(3)]
-        silu_neg = [room(6 + n, [P, 4, H], f"silu_neg{n}") for n in range(3)]
+        first_two = room(6, [P, 4 * H], "first_two")
+        third = keep.tile([P, 2 * H], F32, name="third", align_bytes=64)
+        wide = {e: room(n, [P, 4 * H], f"wide{e}") for e, n in ((3, 7), (4, 8), (5, 15))}
+        silu_neg = [first_two[:, : 2 * H], first_two[:, 2 * H :], third[:]] + [wide[e][:, 2 * H :] for e in (3, 4, 5)]
+        silu_neg = [rows.rearrange("p (h i) -> p h i", h=2) for rows in silu_neg]
 
         w2_raw = {}
         for e in range(E):
@@ -91,35 +95,54 @@ def tile_moe_bdx_mlp_silu_kernel(tc, dy_words, dy_scales, a, w2, w1, gate, offs,
             for t in range(PACK):
                 nc.tensor.transpose(bank[:, P * t : P * (t + 1)], a_t[b // 4][:, t, P * (b % 4) : P * (b % 4 + 1)], ident[:])
             half = sig[b // 4][:, b % 4, :]
-            nc.scalar.activation(out=silu_neg[b // 4][:, b % 4, :], in_=bank[:], func=ACT.Silu, scale=-1.0)
+            nc.scalar.activation(out=silu_neg[b // 2][:, b % 2, :], in_=bank[:], func=ACT.Silu, scale=-1.0)
             nc.scalar.activation(out=half, in_=bank[:], func=ACT.Tanh, scale=0.5)
-            nc.gpsimd.tensor_scalar(out=half, in0=half, scalar1=0.5, scalar2=0.5, op0=ALU.mult, op1=ALU.add)
+            if b < 2 * EARLY_EXPERTS:
+                nc.gpsimd.tensor_scalar(out=half, in0=half, scalar1=0.5, scalar2=0.5, op0=ALU.mult, op1=ALU.add)
 
         nc.tensor.transpose(banks[7][:, 0:P], gate_rows[:], ident[:])
         nc.vector.tensor_scalar(out=neg_gate[:], in0=banks[7][:, 0:BLOCKS], scalar1=-1.0, scalar2=None, op0=ALU.mult)
 
         codes, scales, da_codes, da_scales, staged, slope = {}, {}, {}, {}, {}, {}
 
-        def make_factor(e):
-            rows = slice(2 * (e % 2), 2 * (e % 2) + 2)
-            slope[e] = sig[0][:, rows, :] if e == 0 else staged[e - 1, 1][:].bitcast(F32).rearrange("p (h i) -> p h i", h=2)
-            nc.vector.scalar_tensor_tensor(
-                out=slope[e], in0=silu_neg[e // 2][:, rows, :], scalar=1.0, in1=sig[e // 2][:, rows, :], op0=ALU.subtract, op1=ALU.mult
+        def of_expert(tiles, e):
+            return tiles[e // 2][:, 2 * (e % 2) : 2 * (e % 2) + 2, :]
+
+        sigmoid = {e: of_expert(sig, e) for e in range(EARLY_EXPERTS)}
+
+        def gpsimd_cast(dst, src):
+            nc.gpsimd.tensor_scalar(
+                out=dst.rearrange("p (c j) -> p c j", j=PACK), in0=src.rearrange("p j c -> p c j"), scalar1=1.0, scalar2=0.0, op0=ALU.mult, op1=ALU.add
             )
 
+        def make_factor(e):
+            slope[e] = sigmoid[0] if e == 0 else staged[e - 1, 1].bitcast(F32).rearrange("p (h i) -> p h i", h=2)
+            nc.vector.scalar_tensor_tensor(out=slope[e], in0=silu_neg[e], scalar=1.0, in1=sigmoid[e], op0=ALU.subtract, op1=ALU.mult)
+            late = EARLY_EXPERTS + e - 1
+            if e > 0 and late < E:
+                sigmoid[late] = silu_neg[e]
+                nc.gpsimd.tensor_scalar(out=sigmoid[late], in0=of_expert(sig, late), scalar1=0.5, scalar2=0.5, op0=ALU.mult, op1=ALU.add)
+
         def quantize_w2(e, o):
-            grouped = ring.tile([P, PACK * H], BF16, name="grouped", tag="grouped", bufs=6, align_bytes=64)
+            shared = o == 1 and e >= 3
+            if shared:
+                grouped = wide[e][:, H // 2 : H // 2 + 2 * H].bitcast(BF16)
+            else:
+                grouped = ring.tile([P, PACK * H], BF16, name="grouped", tag="grouped", bufs=6, align_bytes=64)[:]
             staged[e, o] = grouped
             src = w2_raw[e, o][:].rearrange("p j (c i) -> p c j i", i=RUN)
-            dst = grouped[:].rearrange("p (c i j) -> p c j i", i=RUN, j=PACK)
-            cut = (H - (H if e == 0 else W2_VECTOR_COLS if o == 1 and e >= 3 else 0)) // RUN
+            dst = grouped.rearrange("p (c i j) -> p c j i", i=RUN, j=PACK)
+            end = H - W2_GPSIMD_COLS if shared else H
+            cut = 0 if e == 0 else H // 2 if o == 1 else H
             if cut > 0:
-                nc.scalar.copy(out=dst[:, :cut], in_=src[:, :cut])
-            if cut < H // RUN:
-                nc.vector.tensor_copy(out=dst[:, cut:], in_=src[:, cut:])
+                nc.scalar.copy(out=dst[:, : cut // RUN], in_=src[:, : cut // RUN])
+            if cut < end:
+                nc.vector.tensor_copy(out=dst[:, cut // RUN : end // RUN], in_=src[:, cut // RUN : end // RUN])
+            if end < H:
+                gpsimd_cast(grouped[:, PACK * end :], w2_raw[e, o][:, :, end:])
             codes[e, o] = ring.tile([P, H], U32, name="w2_codes", tag="w2_codes", bufs=4, align_bytes=64)
             scales[e, o] = ring.tile([P, H], U8, name="w2_scales", tag="w2_scales", bufs=4, align_bytes=64)
-            nc.vector.quantize_mx(out=codes[e, o][:].bitcast(FP8X4), scales=scales[e, o][:], in_=grouped[:])
+            nc.vector.quantize_mx(out=codes[e, o][:].bitcast(FP8X4), scales=scales[e, o][:], in_=grouped)
 
         def first_product(e):
             turned = banks[5 + e % 2][:].rearrange("p (h u r) -> p h u r", h=2, u=2)
@@ -146,11 +169,13 @@ def tile_moe_bdx_mlp_silu_kernel(tc, dy_words, dy_scales, a, w2, w1, gate, offs,
                     nc.tensor.transpose(turned[:, h, u, :], pairs[:, u : H // 2 : 2], ident[:])
             return turned
 
+        last_da = keep.tile([P, (P + C) * PACK], BF16, name="last_da", align_bytes=64)
+
         def quantize_da(e, turned):
             if e + 1 < E:
                 da = w2_raw[e + 1, 1][:, 0, :].bitcast(BF16)
             else:
-                da = keep.tile([P, C * PACK], BF16, name="da", align_bytes=64)[:]
+                da = last_da[:, P * PACK :]
             nc.scalar.copy(out=da.bitcast(F32).rearrange("p (h r u) -> p h r u", h=2, u=2), in_=turned.rearrange("p h u r -> p h r u"))
             da_codes[e] = keep.tile([P, C], U32, name=f"da_codes{e}", align_bytes=64)
             da_scales[e] = keep.tile([P, C], U8, name=f"da_scales{e}", align_bytes=64)
@@ -168,33 +193,59 @@ def tile_moe_bdx_mlp_silu_kernel(tc, dy_words, dy_scales, a, w2, w1, gate, offs,
         quantize_da(E - 1, turned)
 
         w1_raw, w1_codes, w1_scales, dx = {}, {}, {}, {}
-        groups = ((4, 2), (0, 4))
+        LAST = E - 1
 
-        def load_w1(kt):
-            for first, count in groups:
-                if first == 0:
-                    raw = room((12, 13, 14, 0, 1, 2)[kt], [P, count, PACK, P], f"w1_raw{kt}")
-                else:
-                    raw = ring.tile([P, count, PACK, P], F32, name="w1_rest", tag="w1_rest", bufs=3)
-                w1_raw[kt, first] = raw
-                for n in range(count):
-                    nc.sync.dma_start(out=raw[:, n], in_=w1[first + n].rearrange("(p j) k -> p j k", j=PACK)[:, :, P * kt : P * (kt + 1)])
+        def load_w1(kt, first, count):
+            if first == 0:
+                raw = room((12, 13, 14, 0, 1, 2)[kt], [P, count, PACK, P], f"w1_raw{kt}")
+            else:
+                raw = ring.tile([P, count, PACK, P], F32, name="w1_one", tag=f"w1_one{first}", bufs=4)
+            w1_raw[kt, first] = raw
+            for n in range(count):
+                nc.sync.dma_start(out=raw[:, n], in_=w1[first + n].rearrange("(p j) k -> p j k", j=PACK)[:, :, P * kt : P * (kt + 1)])
+
+        load_w1(0, LAST, 1)
+        load_w1(1, LAST, 1)
+        for kt in range(KT):
+            if kt + 2 < KT:
+                load_w1(kt + 2, LAST, 1)
+            load_w1(kt, LAST - 1, 1)
+            load_w1(kt, 0, 4)
+            if kt == 0:
+                for r, pos in enumerate((pos1, pos2, pos3)):
+                    nc.sync.dma_start(pos_t[r][:], pos)
+
+        pair_stage = (wide[LAST][:, 0:T].bitcast(BF16), last_da[:, 0 : 2 * P * PACK])
+        four_stage = {}
+
+        def interleave(copy, dst, raw):
+            count = raw.shape[1]
+            copy(
+                out=dst.rearrange("p (e c i j) -> p e c j i", e=count, i=RUN, j=PACK),
+                in_=raw.rearrange("p e j (c i) -> p e c j i", i=RUN),
+            )
 
         def quantize_w1(kt):
             w1_codes[kt] = ring.tile([P, E * P], U32, name="w1_codes", tag="w1_codes", bufs=3, align_bytes=64)
             w1_scales[kt] = ring.tile([P, E * P], U8, name="w1_scales", tag="w1_scales", bufs=3, align_bytes=64)
-            for first, count in groups:
-                grouped = ring.tile([P, count * P * PACK], BF16, name="grouped", tag="grouped", bufs=6, align_bytes=64)
-                src = w1_raw[kt, first][:].rearrange("p e j (c i) -> p e c j i", i=RUN)
-                dst = grouped[:].rearrange("p (e c i j) -> p e c j i", e=count, i=RUN, j=PACK)
-                for n in range(count):
-                    copy = nc.scalar.copy if first + n < W1_SCALAR_EXPERTS else nc.vector.tensor_copy
-                    copy(out=dst[:, n], in_=src[:, n])
-                cols = slice(P * first, P * (first + count))
-                nc.vector.quantize_mx(out=w1_codes[kt][:, cols].bitcast(FP8X4), scales=w1_scales[kt][:, cols], in_=grouped[:])
+            width = P * PACK
+            if kt < 2:
+                pair = ring.tile([P, 2 * width], BF16, name="grouped", tag="grouped", bufs=6, align_bytes=64)[:]
+                four = ring.tile([P, 4 * width], BF16, name="grouped", tag="grouped", bufs=6, align_bytes=64)[:]
+                interleave(nc.vector.tensor_copy, pair[:, width:], w1_raw[kt, LAST][:])
+            else:
+                pair = pair_stage[kt % 2]
+                four = room(1 + kt, [P, 2 * width], f"four_stage{kt}")[:].bitcast(BF16)
+                gpsimd_cast(pair[:, width:], w1_raw[kt, LAST][:, 0])
+            four_stage[kt] = four
+            interleave(nc.vector.tensor_copy if kt < 3 else nc.scalar.copy, pair[:, :width], w1_raw[kt, LAST - 1][:])
+            nc.vector.quantize_mx(out=w1_codes[kt][:, 4 * P :].bitcast(FP8X4), scales=w1_scales[kt][:, 4 * P :], in_=pair)
+            for n in (0, 2):
+                interleave(nc.vector.tensor_copy if (kt, n) == (0, 2) else nc.scalar.copy, four[:, width * n : width * (n + 2)], w1_raw[kt, 0][:, n : n + 2])
+            nc.vector.quantize_mx(out=w1_codes[kt][:, : 4 * P].bitcast(FP8X4), scales=w1_scales[kt][:, : 4 * P], in_=four)
 
         def second_product(kt):
-            dx[kt] = room((6, 14, 0, 1, 7, 8)[kt], [P, S], f"dx{kt}")
+            dx[kt] = room((10, 14, 0, 1, 7, 9)[kt], [P, S], f"dx{kt}")
             for pair in range(E // 2):
                 bank = banks[(7, 0, 1, 2, 3, 4)[(3 * kt + pair) % 6]]
                 for n in range(2):
@@ -210,24 +261,21 @@ def tile_moe_bdx_mlp_silu_kernel(tc, dy_words, dy_scales, a, w2, w1, gate, offs,
                     )
                 nc.scalar.copy(out=dx[kt][:, 2 * C * pair : 2 * C * (pair + 1)], in_=bank[:])
 
-        for kt in range(KT):
-            load_w1(kt)
-            if kt == 0:
-                for r, pos in enumerate((pos1, pos2, pos3)):
-                    nc.sync.dma_start(pos_t[r][:], pos)
-
-        totals = [room(3, [P, 4, T], "totals0"), room(4, [P, 2, T], "totals1")]
-        partial = room(5, [P, 2, 2, T], "partial")
+        firsts = room(8, [P, 2, T], "firsts")
+        late = room(11, [P, 2, 2, T], "late")
 
         def combine(kt):
-            total = totals[kt // 4][:, kt % 4, :]
-            first, second = partial[:, kt % 2, 0, :], partial[:, kt % 2, 1, :]
-            halves = [(slice(T // 2 * n, T // 2 * (n + 1)), slice(T // 32 * n, T // 32 * (n + 1))) for n in range(2)]
-            for cols, part in halves:
+            first = firsts[:, kt % 2, :]
+            if kt + 2 < KT:
+                second, total, parts = pair_stage[kt % 2].bitcast(F32), four_stage[kt + 2].bitcast(F32)[:, 0:T], 1
+            else:
+                second, total, parts = late[:, kt % 2, 0, :], late[:, kt % 2, 1, :], 2
+            pieces = [(slice(T // parts * n, T // parts * (n + 1)), slice(T // 16 // parts * n, T // 16 // parts * (n + 1))) for n in range(parts)]
+            for cols, part in pieces:
                 nc.vector.tensor_copy(first[:, cols], dx[kt][:].indirect(pos_t[0][:, part]))
-            for cols, part in halves:
+            for cols, part in pieces:
                 nc.vector.tensor_tensor(second[:, cols], dx[kt][:].indirect(pos_t[1][:, part]), first[:, cols], ALU.add)
-            for cols, part in halves:
+            for cols, part in pieces:
                 nc.vector.tensor_tensor(total[:, cols], dx[kt][:].indirect(pos_t[2][:, part]), second[:, cols], ALU.add)
                 if kt == KT - 1:
                     nc.sync.dma_start(out=out[P * kt : P * (kt + 1), cols], in_=total[:, cols])

@@ -23,7 +23,9 @@ PACK = 4
 PASSES = N // (P * PACK)
 KT = K // P
 BLOCKS = S // P
-RUN = 2
+SCALAR_RUN = 2
+VECTOR_RUN = 4
+W2_VECTOR_COLS = 128
 GATHER = 384
 W2_GPSIMD_COLS = 128
 EARLY_EXPERTS = 4
@@ -110,6 +112,18 @@ def tile_moe_bdx_mlp_silu_kernel(tc, dy_words, dy_scales, a, w2, w1, gate, offs,
 
         sigmoid = {e: of_expert(sig, e) for e in range(EARLY_EXPERTS)}
 
+        def interleave(copy, run, dst, raw):
+            copy(
+                out=dst.rearrange("p (e c i j) -> p e c j i", e=raw.shape[1], i=run, j=PACK),
+                in_=raw.rearrange("p e j (c i) -> p e c j i", i=run),
+            )
+
+        def scalar_cast(dst, raw):
+            interleave(nc.scalar.copy, SCALAR_RUN, dst, raw)
+
+        def vector_cast(dst, raw):
+            interleave(nc.vector.tensor_copy, VECTOR_RUN, dst, raw)
+
         def gpsimd_cast(dst, src):
             nc.gpsimd.tensor_scalar(
                 out=dst.rearrange("p (c j) -> p c j", j=PACK), in0=src.rearrange("p j c -> p c j"), scalar1=1.0, scalar2=0.0, op0=ALU.mult, op1=ALU.add
@@ -130,14 +144,13 @@ def tile_moe_bdx_mlp_silu_kernel(tc, dy_words, dy_scales, a, w2, w1, gate, offs,
             else:
                 grouped = ring.tile([P, PACK * H], BF16, name="grouped", tag="grouped", bufs=6, align_bytes=64)[:]
             staged[e, o] = grouped
-            src = w2_raw[e, o][:].rearrange("p j (c i) -> p c j i", i=RUN)
-            dst = grouped.rearrange("p (c i j) -> p c j i", i=RUN, j=PACK)
+            raw = w2_raw[e, o][:].unsqueeze(1)
             end = H - W2_GPSIMD_COLS if shared else H
-            cut = 0 if e == 0 else H // 2 if o == 1 else H
+            cut = 0 if e == 0 else end - W2_VECTOR_COLS if (e, o) in ((2, 1), (E - 1, 1)) else end
             if cut > 0:
-                nc.scalar.copy(out=dst[:, : cut // RUN], in_=src[:, : cut // RUN])
+                scalar_cast(grouped[:, : PACK * cut], raw[:, :, :, :cut])
             if cut < end:
-                nc.vector.tensor_copy(out=dst[:, cut // RUN : end // RUN], in_=src[:, cut // RUN : end // RUN])
+                vector_cast(grouped[:, PACK * cut : PACK * end], raw[:, :, :, cut:end])
             if end < H:
                 gpsimd_cast(grouped[:, PACK * end :], w2_raw[e, o][:, :, end:])
             codes[e, o] = ring.tile([P, H], U32, name="w2_codes", tag="w2_codes", bufs=4, align_bytes=64)
@@ -218,13 +231,6 @@ def tile_moe_bdx_mlp_silu_kernel(tc, dy_words, dy_scales, a, w2, w1, gate, offs,
         pair_stage = (wide[LAST][:, 0:T].bitcast(BF16), last_da[:, 0 : 2 * P * PACK])
         four_stage = {}
 
-        def interleave(copy, dst, raw):
-            count = raw.shape[1]
-            copy(
-                out=dst.rearrange("p (e c i j) -> p e c j i", e=count, i=RUN, j=PACK),
-                in_=raw.rearrange("p e j (c i) -> p e c j i", i=RUN),
-            )
-
         def quantize_w1(kt):
             w1_codes[kt] = ring.tile([P, E * P], U32, name="w1_codes", tag="w1_codes", bufs=3, align_bytes=64)
             w1_scales[kt] = ring.tile([P, E * P], U8, name="w1_scales", tag="w1_scales", bufs=3, align_bytes=64)
@@ -232,16 +238,16 @@ def tile_moe_bdx_mlp_silu_kernel(tc, dy_words, dy_scales, a, w2, w1, gate, offs,
             if kt < 2:
                 pair = ring.tile([P, 2 * width], BF16, name="grouped", tag="grouped", bufs=6, align_bytes=64)[:]
                 four = ring.tile([P, 4 * width], BF16, name="grouped", tag="grouped", bufs=6, align_bytes=64)[:]
-                interleave(nc.vector.tensor_copy, pair[:, width:], w1_raw[kt, LAST][:])
+                vector_cast(pair[:, width:], w1_raw[kt, LAST][:])
             else:
                 pair = pair_stage[kt % 2]
                 four = room(1 + kt, [P, 2 * width], f"four_stage{kt}")[:].bitcast(BF16)
                 gpsimd_cast(pair[:, width:], w1_raw[kt, LAST][:, 0])
             four_stage[kt] = four
-            interleave(nc.vector.tensor_copy if kt < 3 else nc.scalar.copy, pair[:, :width], w1_raw[kt, LAST - 1][:])
+            (vector_cast if kt < 3 else scalar_cast)(pair[:, :width], w1_raw[kt, LAST - 1][:])
             nc.vector.quantize_mx(out=w1_codes[kt][:, 4 * P :].bitcast(FP8X4), scales=w1_scales[kt][:, 4 * P :], in_=pair)
             for n in (0, 2):
-                interleave(nc.vector.tensor_copy if (kt, n) == (0, 2) else nc.scalar.copy, four[:, width * n : width * (n + 2)], w1_raw[kt, 0][:, n : n + 2])
+                (vector_cast if (kt, n) == (0, 2) else scalar_cast)(four[:, width * n : width * (n + 2)], w1_raw[kt, 0][:, n : n + 2])
             nc.vector.quantize_mx(out=w1_codes[kt][:, : 4 * P].bitcast(FP8X4), scales=w1_scales[kt][:, : 4 * P], in_=four)
 
         def second_product(kt):

@@ -25,10 +25,38 @@ KT = K // P
 BLOCKS = S // P
 SCALAR_RUN = 2
 VECTOR_RUN = 4
-W2_VECTOR_COLS = 128
 GATHER = 384
-W2_GPSIMD_COLS = 128
-EARLY_EXPERTS = 4
+ROOMS = 11
+STAGE = PACK * H
+STAGGER = True
+P00 = 384
+P01 = 0
+V1 = 384
+V4 = 0
+V5 = 0
+P4 = 128
+P5 = 192
+A2_FIRST = False
+VS = 256
+SPLIT = 5
+FORCED = 3
+VA0 = 0
+VA1 = 2
+VP = 0
+ST3 = 2
+TURN = (5, 5, 5, 1, 5, 7)
+DEFER = 3
+HOLD = False
+
+
+def w2_shares(e, o):
+    if e == 0:
+        return (P00, 0, H - P00) if o == 0 else (P01, 0, H - P01)
+    if o == 1:
+        return (0, VS, H - VS) if e >= SPLIT else (0, 0, H)
+    if e >= 4:
+        return (P4, V4, H - P4 - V4) if e == 4 else (P5, V5, H - P5 - V5)
+    return (0, V1, H - V1)
 
 
 def tile_moe_bdx_mlp_silu_kernel(tc, dy_words, dy_scales, a, w2, w1, gate, offs, pos1, pos2, pos3, out):
@@ -39,9 +67,6 @@ def tile_moe_bdx_mlp_silu_kernel(tc, dy_words, dy_scales, a, w2, w1, gate, offs,
         ring = ctx.enter_context(tc.tile_pool(name="ring", bufs=2))
         psum = ctx.enter_context(tc.psum_pool(name="psum", bufs=1))
 
-        def room(n, shape, name):
-            return keep.tile(shape, F32, name=name, tag=f"room{n}", align_bytes=64)
-
         banks = [psum.tile([P, 512], F32, name=f"bank{b}") for b in range(8)]
 
         offs_t = lists.tile([P, S // 16], U16, name="offs_t")
@@ -51,6 +76,9 @@ def tile_moe_bdx_mlp_silu_kernel(tc, dy_words, dy_scales, a, w2, w1, gate, offs,
         ident = keep.tile([P, P], F32, name="ident")
         gate_rows = keep.tile([P, P], F32, name="gate_rows")
         neg_gate = keep.tile([P, BLOCKS], F32, name="neg_gate")
+        stage = [keep.tile([P, 2 * STAGE - PACK * P5 if n == 4 else STAGE], BF16, name=f"stage{n}", align_bytes=64)[:] for n in range(KT + 1)]
+        behind = stage[4][:, STAGE - PACK * P5 :]
+        stage[4] = stage[4][:, :STAGE]
 
         make_identity(nc, ident[:])
         nc.gpsimd.memset(gate_rows[:], 0.0)
@@ -58,65 +86,120 @@ def tile_moe_bdx_mlp_silu_kernel(tc, dy_words, dy_scales, a, w2, w1, gate, offs,
         nc.vector.memset(plane[:], 0)
 
         a_rows = a.rearrange("(t p) s -> p t s", p=P)
-        a_t = [room(n, [P, PACK, 2 * C], f"a_t{n}") for n in range(3)]
         words_i32 = dy_words.rearrange("o p t d -> p o (t d)").bitcast(I32)
         scales_i32 = dy_scales.bitcast(I32)
+        a_t, w2_raw, w1_raw = {}, {}, {}
+
+        def room(n, shape):
+            return keep.tile(shape, F32, name=f"raw{n}", tag=f"room{n % ROOMS}", align_bytes=64)
+
+        def load_a(e):
+            a_t[e] = keep.tile([P, PACK, C], F32, name=f"a_t{e}", tag=f"a{e % 3}", align_bytes=64)
+            nc.sync.dma_start(out=a_t[e][:], in_=a_rows[:, :, C * e : C * (e + 1)])
+
+        def load_w2(e, o):
+            w2_raw[e, o] = room(PASSES * e + o, [P, PACK, H])
+            nc.sync.dma_start(out=w2_raw[e, o][:], in_=w2[e, 512 * o : 512 * (o + 1), :].rearrange("(p j) i -> p j i", j=PACK))
 
         nc.sync.dma_start(offs_t[:], offs)
         nc.sync.dma_start(out=words[:, 0, :], in_=words_i32[:, 0, :])
-        nc.sync.dma_start(out=a_t[0][:, :, 0:P], in_=a_rows[:, :, 0:P])
+        load_a(0)
         nc.sync.dma_start(out=words[:, 1, :], in_=words_i32[:, 1, :])
+        load_a(1)
+        if A2_FIRST:
+            load_a(2)
         for q in range(4):
             nc.sync.dma_start(out=plane[32 * q : 32 * q + 8, :], in_=scales_i32[:, 4 * q : 4 * q + 4, :])
-        nc.sync.dma_start(out=a_t[0][:, :, P : 2 * C], in_=a_rows[:, :, P : 2 * C])
-        for n in (1, 2):
-            nc.sync.dma_start(out=a_t[n][:], in_=a_rows[:, :, 2 * C * n : 2 * C * (n + 1)])
-        sig = [room(3 + n, [P, 4, H], f"sig{n}") for n in range(3)]
-        first_two = room(6, [P, 4 * H], "first_two")
-        third = keep.tile([P, 2 * H], F32, name="third", align_bytes=64)
-        wide = {e: room(n, [P, 4 * H], f"wide{e}") for e, n in ((3, 7), (4, 8), (5, 15))}
-        silu_neg = [first_two[:, : 2 * H], first_two[:, 2 * H :], third[:]] + [wide[e][:, 2 * H :] for e in (3, 4, 5)]
-        silu_neg = [rows.rearrange("p (h i) -> p h i", h=2) for rows in silu_neg]
-
-        w2_raw = {}
         for e in range(E):
-            for o in range(PASSES):
-                w2_raw[e, o] = room((9, 10, 11, 12, 13, 14, 0, 1, 2)[(PASSES * e + o) % 9], [P, PACK, H], f"w2_raw{e}_{o}")
-                nc.sync.dma_start(out=w2_raw[e, o][:], in_=w2[e, 512 * o : 512 * (o + 1), :].rearrange("(p j) i -> p j i", j=PACK))
+            load_w2(e, 0)
+            if e == 0 and not A2_FIRST:
+                load_a(2)
+            load_w2(e, 1)
+            if e + 3 < E:
+                load_a(e + 3)
+            if e == 2:
+                for r, pos in enumerate((pos1, pos2, pos3)):
+                    nc.sync.dma_start(pos_t[r][:], pos)
+
+        def early_expert(kt):
+            return 2 if kt % 2 == 0 else 5
+
+        def late_expert(kt):
+            return 5 if kt % 2 == 0 else 2
+
+        units = []
+        for kt in range(KT):
+            if not STAGGER:
+                units.extend((e, kt, 1) for e in (early_expert(kt), 0, 1, 3, 4, late_expert(kt)))
+            elif kt == 0:
+                units.extend([(2, 0, 1), (0, 0, 1), (1, 0, 1), (3, 0, 2), (4, 0, 2), (5, 0, 2)])
+            else:
+                units.extend((late_expert(kt) - 2 + n, kt, min(2, KT - kt)) for n in range(3))
+        used, filled, current = PASSES * E, 4, None
+        for e, kt, strips in units:
+            if filled + strips > 4:
+                current = room(used, [P, 4 * PACK * P])
+                used, filled = used + 1, 0
+            raw = current[:, PACK * P * filled : PACK * P * (filled + strips)].rearrange("p (j k) -> p j k", j=PACK)
+            filled = filled + strips
+            nc.sync.dma_start(out=raw, in_=w1[e].rearrange("(p j) k -> p j k", j=PACK)[:, :, P * kt : P * (kt + strips)])
+            for n in range(strips):
+                w1_raw[e, kt + n] = raw[:, :, P * n : P * (n + 1)]
 
         g_words = keep.tile([P, PASSES, S], U32, name="g_words", align_bytes=64)
         g_scales = keep.tile([P, S], U8, name="g_scales", align_bytes=64)
+        for o in range(PASSES):
+            for first in range(0, S, GATHER):
+                slots = offs_t[:, first // 16 : (first + GATHER) // 16]
+                nc.vector.tensor_copy(g_words[:, o, first : first + GATHER], words[:, o, :].bitcast(U32).indirect(slots))
         for first in range(0, S, GATHER):
             slots = offs_t[:, first // 16 : (first + GATHER) // 16]
-            for o in range(PASSES):
-                nc.vector.tensor_copy(g_words[:, o, first : first + GATHER], words[:, o, :].bitcast(U32).indirect(slots))
             nc.vector.tensor_copy(g_scales[:, first : first + GATHER], plane[:].bitcast(U8).indirect(slots))
 
-        for b in range(BLOCKS):
-            bank = banks[b % 4]
-            for t in range(PACK):
-                nc.tensor.transpose(bank[:, P * t : P * (t + 1)], a_t[b // 4][:, t, P * (b % 4) : P * (b % 4 + 1)], ident[:])
-            half = sig[b // 4][:, b % 4, :]
-            nc.scalar.activation(out=silu_neg[b // 2][:, b % 2, :], in_=bank[:], func=ACT.Silu, scale=-1.0)
-            nc.scalar.activation(out=half, in_=bank[:], func=ACT.Tanh, scale=0.5)
-            if b < 2 * EARLY_EXPERTS:
-                nc.gpsimd.tensor_scalar(out=half, in0=half, scalar1=0.5, scalar2=0.5, op0=ALU.mult, op1=ALU.add)
+        silu_neg, tanh_half, sigmoid, codes, scales, da_codes, da_scales, slope = {}, {}, {}, {}, {}, {}, {}, {}
 
-        nc.tensor.transpose(banks[7][:, 0:P], gate_rows[:], ident[:])
-        nc.vector.tensor_scalar(out=neg_gate[:], in0=banks[7][:, 0:BLOCKS], scalar1=-1.0, scalar2=None, op0=ALU.mult)
+        def act_room(n, shape, name):
+            return keep.tile(shape, F32, name=name, tag=f"act{n}", align_bytes=64)
 
-        codes, scales, da_codes, da_scales, staged, slope = {}, {}, {}, {}, {}, {}
+        wide = keep.tile([P, 4 * H - 2 * P4], F32, name="wide", align_bytes=64)
 
-        def of_expert(tiles, e):
-            return tiles[e // 2][:, 2 * (e % 2) : 2 * (e % 2) + 2, :]
+        def activations(e):
+            silu_neg[e] = act_room(e % 4, [P, 2, H], f"silu_neg{e}")[:] if e + 1 < E else wide[:, : 2 * H].rearrange("p (h i) -> p h i", h=2)
+            tanh_half[e] = act_room(4 + e % 4, [P, 2, H], f"tanh_half{e}")
+            turned_a = [banks[(0, 1, 4, 6)[(2 * e + h) % 4]] for h in range(2)]
+            for h in range(2):
+                for t in range(PACK):
+                    nc.tensor.transpose(turned_a[h][:, P * t : P * (t + 1)], a_t[e][:, t, P * h : P * (h + 1)], ident[:])
+            steps = [(silu_neg[e], ACT.Silu, -1.0), (tanh_half[e], ACT.Tanh, 0.5)]
+            for dst, func, scale in steps if e == 0 else reversed(steps):
+                for h in range(2):
+                    nc.scalar.activation(out=dst[:, h, :], in_=turned_a[h][:], func=func, scale=scale)
 
-        sigmoid = {e: of_expert(sig, e) for e in range(EARLY_EXPERTS)}
+        def w2_stage(e, o):
+            if (e, o) == (4, 0):
+                return wide[:, 2 * H - 2 * P4 :].bitcast(BF16)
+            if (e, o) == (5, 0):
+                return behind
+            return stage[(1, 3)[e % 2] if o == 0 else (ST3, 4, KT)[e % 3]]
+
+        def make_sigmoid(e):
+            src = tanh_half[e][:].rearrange("p h i -> p (h i)")
+            sigmoid[e] = src if e < 3 else silu_neg[e - 2][:].rearrange("p h i -> p (h i)")
+            nc.gpsimd.tensor_scalar(out=sigmoid[e], in0=src, scalar1=0.5, scalar2=0.5, op0=ALU.mult, op1=ALU.add)
+
+        def make_slope(e):
+            slope[e] = sigmoid[0] if e == 0 else w2_stage(*((e - 1, 1) if e < 4 else (3, e - 4))).bitcast(F32)
+            nc.vector.scalar_tensor_tensor(
+                out=slope[e],
+                in0=silu_neg[e][:].rearrange("p h i -> p (h i)"),
+                scalar=1.0,
+                in1=sigmoid[e],
+                op0=ALU.subtract,
+                op1=ALU.mult,
+            )
 
         def interleave(copy, run, dst, raw):
-            copy(
-                out=dst.rearrange("p (e c i j) -> p e c j i", e=raw.shape[1], i=run, j=PACK),
-                in_=raw.rearrange("p e j (c i) -> p e c j i", i=run),
-            )
+            copy(out=dst.rearrange("p (c i j) -> p c j i", i=run, j=PACK), in_=raw.rearrange("p j (c i) -> p c j i", i=run))
 
         def scalar_cast(dst, raw):
             interleave(nc.scalar.copy, SCALAR_RUN, dst, raw)
@@ -124,176 +207,163 @@ def tile_moe_bdx_mlp_silu_kernel(tc, dy_words, dy_scales, a, w2, w1, gate, offs,
         def vector_cast(dst, raw):
             interleave(nc.vector.tensor_copy, VECTOR_RUN, dst, raw)
 
-        def gpsimd_cast(dst, src):
+        def gpsimd_cast(dst, raw):
             nc.gpsimd.tensor_scalar(
-                out=dst.rearrange("p (c j) -> p c j", j=PACK), in0=src.rearrange("p j c -> p c j"), scalar1=1.0, scalar2=0.0, op0=ALU.mult, op1=ALU.add
+                out=dst.rearrange("p (c j) -> p c j", j=PACK), in0=raw.rearrange("p j c -> p c j"), scalar1=1.0, scalar2=0.0, op0=ALU.mult, op1=ALU.add
             )
 
-        def make_factor(e):
-            slope[e] = sigmoid[0] if e == 0 else staged[e - 1, 1].bitcast(F32).rearrange("p (h i) -> p h i", h=2)
-            nc.vector.scalar_tensor_tensor(out=slope[e], in0=silu_neg[e], scalar=1.0, in1=sigmoid[e], op0=ALU.subtract, op1=ALU.mult)
-            late = EARLY_EXPERTS + e - 1
-            if e > 0 and late < E:
-                sigmoid[late] = silu_neg[e]
-                nc.gpsimd.tensor_scalar(out=sigmoid[late], in0=of_expert(sig, late), scalar1=0.5, scalar2=0.5, op0=ALU.mult, op1=ALU.add)
+        def cast_w2(e, o):
+            first = 0
+            for cast, count in zip((gpsimd_cast, vector_cast, scalar_cast), w2_shares(e, o)):
+                if count > 0:
+                    cast(w2_stage(e, o)[:, PACK * first : PACK * (first + count)], w2_raw[e, o][:, :, first : first + count])
+                first = first + count
 
         def quantize_w2(e, o):
-            shared = o == 1 and e >= 3
-            if shared:
-                grouped = wide[e][:, H // 2 : H // 2 + 2 * H].bitcast(BF16)
-            else:
-                grouped = ring.tile([P, PACK * H], BF16, name="grouped", tag="grouped", bufs=6, align_bytes=64)[:]
-            staged[e, o] = grouped
-            raw = w2_raw[e, o][:].unsqueeze(1)
-            end = H - W2_GPSIMD_COLS if shared else H
-            cut = 0 if e == 0 else end - W2_VECTOR_COLS if (e, o) in ((2, 1), (E - 1, 1)) else end
-            if cut > 0:
-                scalar_cast(grouped[:, : PACK * cut], raw[:, :, :, :cut])
-            if cut < end:
-                vector_cast(grouped[:, PACK * cut : PACK * end], raw[:, :, :, cut:end])
-            if end < H:
-                gpsimd_cast(grouped[:, PACK * end :], w2_raw[e, o][:, :, end:])
             codes[e, o] = ring.tile([P, H], U32, name="w2_codes", tag="w2_codes", bufs=4, align_bytes=64)
             scales[e, o] = ring.tile([P, H], U8, name="w2_scales", tag="w2_scales", bufs=4, align_bytes=64)
-            nc.vector.quantize_mx(out=codes[e, o][:].bitcast(FP8X4), scales=scales[e, o][:], in_=grouped)
+            nc.vector.quantize_mx(out=codes[e, o][:].bitcast(FP8X4), scales=scales[e, o][:], in_=w2_stage(e, o)[:])
+
+        turned = [banks[b][:].rearrange("p (h u r) -> p h u r", h=2, u=2) for b in TURN]
 
         def first_product(e):
-            turned = banks[5 + e % 2][:].rearrange("p (h u r) -> p h u r", h=2, u=2)
             for h in range(2):
                 b = 2 * e + h
                 cols = slice(P * b, P * (b + 1))
-                acc = banks[2 + b % 3]
-                for o in range(PASSES):
+                acc = banks[2 + h]
+                order = (1, 0) if e == 0 else (0, 1)
+                for o in order:
                     nc.tensor.matmul_mx(
                         out=acc[:],
                         lhsT=g_words[:, o, cols].bitcast(FP8X4),
                         lhsT_scale=g_scales[4 * o : P, cols],
                         rhs=codes[e, o][:].bitcast(FP8X4),
                         rhs_scale=scales[e, o][:],
-                        start=(o == 0),
-                        stop=(o == PASSES - 1),
+                        start=(o == order[0]),
+                        stop=(o == order[1]),
                     )
                 da_rows = ring.tile([P, H], BF16, name="da_rows", tag="da_rows", bufs=3, align_bytes=64)
                 nc.vector.scalar_tensor_tensor(
-                    out=da_rows[:], in0=acc[:], scalar=neg_gate[:, b : b + 1], in1=slope[e][:, h, :], op0=ALU.mult, op1=ALU.mult
+                    out=da_rows[:], in0=acc[:], scalar=neg_gate[:, b : b + 1], in1=slope[e][:, H * h : H * (h + 1)], op0=ALU.mult, op1=ALU.mult
                 )
                 pairs = da_rows[:].bitcast(F32)
                 for u in range(2):
-                    nc.tensor.transpose(turned[:, h, u, :], pairs[:, u : H // 2 : 2], ident[:])
-            return turned
+                    nc.tensor.transpose(turned[e][:, h, u, :], pairs[:, u : H // 2 : 2], ident[:])
 
-        last_da = keep.tile([P, (P + C) * PACK], BF16, name="last_da", align_bytes=64)
+        last_da = keep.tile([P, 2, PACK * C], BF16, name="last_da", align_bytes=64)
 
-        def quantize_da(e, turned):
-            if e + 1 < E:
-                da = w2_raw[e + 1, 1][:, 0, :].bitcast(BF16)
+        def quantize_da(e):
+            if e + 1 == E:
+                da = stage[1][:, STAGE // 2 :] if HOLD else last_da[:, 0, :]
             else:
-                da = last_da[:, P * PACK :]
-            nc.scalar.copy(out=da.bitcast(F32).rearrange("p (h r u) -> p h r u", h=2, u=2), in_=turned.rearrange("p h u r -> p h r u"))
+                da = (w2_raw[e + 1, 1][:, 0, :] if e < DEFER else w2_raw[E - 1, 1][:, e - DEFER, :]).bitcast(BF16)
+            nc.scalar.copy(out=da.bitcast(F32).rearrange("p (h r u) -> p h r u", h=2, u=2), in_=turned[e].rearrange("p h u r -> p h r u"))
             da_codes[e] = keep.tile([P, C], U32, name=f"da_codes{e}", align_bytes=64)
             da_scales[e] = keep.tile([P, C], U8, name=f"da_scales{e}", align_bytes=64)
             nc.vector.quantize_mx(out=da_codes[e][:].bitcast(FP8X4), scales=da_scales[e][:], in_=da)
 
-        make_factor(0)
+        activations(0)
+        nc.tensor.transpose(banks[7][:, 0:P], gate_rows[:], ident[:])
+        nc.vector.tensor_scalar(out=neg_gate[:], in0=banks[7][:, 0:BLOCKS], scalar1=-1.0, scalar2=None, op0=ALU.mult)
+        activations(1)
+        make_sigmoid(0)
+        cast_w2(0, 0)
+        make_sigmoid(1)
+        make_slope(0)
+        quantize_w2(0, 0)
+        activations(2)
+        make_sigmoid(2)
         for e in range(E):
-            quantize_w2(e, 0)
+            cast_w2(e, 1)
             quantize_w2(e, 1)
-            if e > 0:
-                quantize_da(e - 1, turned)
+            if 0 < e <= DEFER:
+                quantize_da(e - 1)
+            if e < 4:
+                make_slope(e + 1 if e < 3 else 5)
+            if e + 3 < E:
+                activations(e + 3)
+                make_sigmoid(e + 3)
+            first_product(e)
             if e + 1 < E:
-                make_factor(e + 1)
-            turned = first_product(e)
-        quantize_da(E - 1, turned)
+                cast_w2(e + 1, 0)
+                quantize_w2(e + 1, 0)
+            if e == 2:
+                make_slope(4)
+        for e in range(DEFER, E):
+            quantize_da(e)
 
-        w1_raw, w1_codes, w1_scales, dx = {}, {}, {}, {}
-        LAST = E - 1
+        w1_codes, w1_scales, dx = {}, {}, {}
+        piece = PACK * P
+        FOUR = (0, 1, 3, 4)
 
-        def load_w1(kt, first, count):
-            if first == 0:
-                raw = room((12, 13, 14, 0, 1, 2)[kt], [P, count, PACK, P], f"w1_raw{kt}")
-            else:
-                raw = ring.tile([P, count, PACK, P], F32, name="w1_one", tag=f"w1_one{first}", bufs=4)
-            w1_raw[kt, first] = raw
-            for n in range(count):
-                nc.sync.dma_start(out=raw[:, n], in_=w1[first + n].rearrange("(p j) k -> p j k", j=PACK)[:, :, P * kt : P * (kt + 1)])
+        def upper(n):
+            return stage[n % (KT + 1)][:, STAGE // 2 :]
 
-        load_w1(0, LAST, 1)
-        load_w1(1, LAST, 1)
-        for kt in range(KT):
-            if kt + 2 < KT:
-                load_w1(kt + 2, LAST, 1)
-            load_w1(kt, LAST - 1, 1)
-            load_w1(kt, 0, 4)
-            if kt == 0:
-                for r, pos in enumerate((pos1, pos2, pos3)):
-                    nc.sync.dma_start(pos_t[r][:], pos)
+        def products(kt, bank, experts, first):
+            for n, e in enumerate(experts):
+                cols = slice(P * (first + n), P * (first + n + 1))
+                nc.tensor.matmul_mx(
+                    out=bank[:, C * n : C * (n + 1)],
+                    lhsT=w1_codes[kt][:, cols].bitcast(FP8X4),
+                    lhsT_scale=w1_scales[kt][:, cols],
+                    rhs=da_codes[e][:].bitcast(FP8X4),
+                    rhs_scale=da_scales[e][:],
+                    start=True,
+                    stop=True,
+                )
 
-        pair_stage = (wide[LAST][:, 0:T].bitcast(BF16), last_da[:, 0 : 2 * P * PACK])
-        four_stage = {}
+        def strip_banks(kt):
+            return [banks[b] for b in ((4, 6, 0), (1, 5, 2))[kt % 2]]
 
-        def quantize_w1(kt):
+        def four_experts(kt):
             w1_codes[kt] = ring.tile([P, E * P], U32, name="w1_codes", tag="w1_codes", bufs=3, align_bytes=64)
             w1_scales[kt] = ring.tile([P, E * P], U8, name="w1_scales", tag="w1_scales", bufs=3, align_bytes=64)
-            width = P * PACK
-            if kt < 2:
-                pair = ring.tile([P, 2 * width], BF16, name="grouped", tag="grouped", bufs=6, align_bytes=64)[:]
-                four = ring.tile([P, 4 * width], BF16, name="grouped", tag="grouped", bufs=6, align_bytes=64)[:]
-                vector_cast(pair[:, width:], w1_raw[kt, LAST][:])
+            dx[kt] = act_room(kt, [P, S], f"dx{kt}")
+            order = FOUR if kt % 2 == 0 else FOUR[2:] + FOUR[:2]
+            for e in order:
+                n = FOUR.index(e)
+                cut = P if order.index(e) < (VA0, VA1, 0, 0, 0, 0)[kt] else VP if e == order[0] else 0
+                if cut > 0:
+                    vector_cast(stage[kt][:, piece * n : piece * n + PACK * cut], w1_raw[e, kt][:, :, :cut])
+                if cut < P:
+                    scalar_cast(stage[kt][:, piece * n + PACK * cut : piece * (n + 1)], w1_raw[e, kt][:, :, cut:])
+            nc.vector.quantize_mx(out=w1_codes[kt][:, : 4 * P].bitcast(FP8X4), scales=w1_scales[kt][:, : 4 * P], in_=stage[kt][:])
+            for n in range(2):
+                products(kt, strip_banks(kt)[n], FOUR[2 * n : 2 * n + 2], 2 * n)
+                nc.scalar.copy(out=dx[kt][:, C * FOUR[2 * n] : C * (FOUR[2 * n] + 2)], in_=strip_banks(kt)[n][:])
+
+        def two_experts(kt):
+            staged = upper(kt - 1)
+            for e, cast in ((early_expert(kt), vector_cast if kt == 1 else gpsimd_cast), (late_expert(kt), scalar_cast)):
+                n = (2, 5).index(e)
+                cast(staged[:, piece * n : piece * (n + 1)], w1_raw[e, kt])
+            nc.vector.quantize_mx(out=w1_codes[kt][:, 4 * P :].bitcast(FP8X4), scales=w1_scales[kt][:, 4 * P :], in_=staged)
+            products(kt, strip_banks(kt)[2], (2, 5), 4)
+            nc.scalar.copy(
+                out=dx[kt][:].rearrange("p (g e c) -> p g e c", g=2, e=3)[:, :, 2, :], in_=strip_banks(kt)[2][:].rearrange("p (g c) -> p g c", g=2)
+            )
+
+        four_experts(0)
+        two_experts(0)
+        for kt in range(KT):
+            first = stage[kt][:, : STAGE // 2].bitcast(F32)
+            second = upper(kt + 1).bitcast(F32)
+            total = upper(kt).bitcast(F32)
+            pieces = [(slice(T // 2 * n, T // 2 * (n + 1)), slice(T // 32 * n, T // 32 * (n + 1))) for n in range(2)]
+            if kt + 1 < KT:
+                nc.vector.tensor_copy(first, dx[kt][:].indirect(pos_t[0][:]))
             else:
-                pair = pair_stage[kt % 2]
-                four = room(1 + kt, [P, 2 * width], f"four_stage{kt}")[:].bitcast(BF16)
-                gpsimd_cast(pair[:, width:], w1_raw[kt, LAST][:, 0])
-            four_stage[kt] = four
-            (vector_cast if kt < 3 else scalar_cast)(pair[:, :width], w1_raw[kt, LAST - 1][:])
-            nc.vector.quantize_mx(out=w1_codes[kt][:, 4 * P :].bitcast(FP8X4), scales=w1_scales[kt][:, 4 * P :], in_=pair)
-            for n in (0, 2):
-                (vector_cast if (kt, n) == (0, 2) else scalar_cast)(four[:, width * n : width * (n + 2)], w1_raw[kt, 0][:, n : n + 2])
-            nc.vector.quantize_mx(out=w1_codes[kt][:, : 4 * P].bitcast(FP8X4), scales=w1_scales[kt][:, : 4 * P], in_=four)
-
-        def second_product(kt):
-            dx[kt] = room((10, 14, 0, 1, 7, 9)[kt], [P, S], f"dx{kt}")
-            for pair in range(E // 2):
-                bank = banks[(7, 0, 1, 2, 3, 4)[(3 * kt + pair) % 6]]
-                for n in range(2):
-                    e = 2 * pair + n
-                    nc.tensor.matmul_mx(
-                        out=bank[:, C * n : C * (n + 1)],
-                        lhsT=w1_codes[kt][:, P * e : P * (e + 1)].bitcast(FP8X4),
-                        lhsT_scale=w1_scales[kt][:, P * e : P * (e + 1)],
-                        rhs=da_codes[e][:].bitcast(FP8X4),
-                        rhs_scale=da_scales[e][:],
-                        start=True,
-                        stop=True,
-                    )
-                nc.scalar.copy(out=dx[kt][:, 2 * C * pair : 2 * C * (pair + 1)], in_=bank[:])
-
-        firsts = room(8, [P, 2, T], "firsts")
-        late = room(11, [P, 2, 2, T], "late")
-
-        def combine(kt):
-            first = firsts[:, kt % 2, :]
-            if kt + 2 < KT:
-                second, total, parts = pair_stage[kt % 2].bitcast(F32), four_stage[kt + 2].bitcast(F32)[:, 0:T], 1
-            else:
-                second, total, parts = late[:, kt % 2, 0, :], late[:, kt % 2, 1, :], 2
-            pieces = [(slice(T // parts * n, T // parts * (n + 1)), slice(T // 16 // parts * n, T // 16 // parts * (n + 1))) for n in range(parts)]
-            for cols, part in pieces:
-                nc.vector.tensor_copy(first[:, cols], dx[kt][:].indirect(pos_t[0][:, part]))
+                for cols, part in pieces:
+                    nc.vector.tensor_copy(first[:, cols], dx[kt][:].indirect(pos_t[0][:, part]))
+            if kt + 1 < KT:
+                four_experts(kt + 1)
             for cols, part in pieces:
                 nc.vector.tensor_tensor(second[:, cols], dx[kt][:].indirect(pos_t[1][:, part]), first[:, cols], ALU.add)
+            if kt + 1 < KT:
+                two_experts(kt + 1)
             for cols, part in pieces:
                 nc.vector.tensor_tensor(total[:, cols], dx[kt][:].indirect(pos_t[2][:, part]), second[:, cols], ALU.add)
-                if kt == KT - 1:
+                if kt + 1 == KT:
                     nc.sync.dma_start(out=out[P * kt : P * (kt + 1), cols], in_=total[:, cols])
-            if kt < KT - 1:
-                nc.sync.dma_start(out=out[P * kt : P * (kt + 1), :], in_=total)
-
-        quantize_w1(0)
-        second_product(0)
-        quantize_w1(1)
-        for kt in range(KT):
-            if kt + 2 < KT:
-                quantize_w1(kt + 2)
             if kt + 1 < KT:
-                second_product(kt + 1)
-            combine(kt)
+                nc.sync.dma_start(out=out[P * kt : P * (kt + 1), :], in_=total)

@@ -25,38 +25,45 @@ KT = K // P
 BLOCKS = S // P
 SCALAR_RUN = 2
 VECTOR_RUN = 4
-GATHER = 384
-ROOMS = 11
+GATHER = 1536
+WINDOW = 2048
+FIRST_BLOCK = True
+ROOMS = 6
+W1_SPOTS = 12
+LAST_DA = 6
+HX = 1
+HOLD_FROM = 2
 STAGE = PACK * H
-STAGGER = True
-P00 = 384
-P01 = 0
-V1 = 384
+STAGGER = False
+P00 = 128
+V01 = 0
+V00 = 384
+V10 = 384
+V11 = 256
+SIG = 2
+V1 = 64
 V4 = 0
 V5 = 0
-P4 = 128
+P4 = 96
+LATE0 = 1
 P5 = 192
 A2_FIRST = False
-VS = 256
+VS = 128
 SPLIT = 5
 FORCED = 3
 VA0 = 0
-VA1 = 2
-VP = 0
+VA1 = 0
+ON_VECTOR = ((0, 0), (0, 1), (1, 1), (3, 1))
 ST3 = 2
-TURN = (5, 5, 5, 1, 5, 7)
-DEFER = 3
+TURN = (5, 5, 5, 5, 5, 7)
+DEFER = 5
 HOLD = False
 
 
 def w2_shares(e, o):
-    if e == 0:
-        return (P00, 0, H - P00) if o == 0 else (P01, 0, H - P01)
-    if o == 1:
-        return (0, VS, H - VS) if e >= SPLIT else (0, 0, H)
-    if e >= 4:
-        return (P4, V4, H - P4 - V4) if e == 4 else (P5, V5, H - P5 - V5)
-    return (0, V1, H - V1)
+    gpsimd = {(0, 0): P00, (E - 1, 0): P4}.get((e, o), 0)
+    vector = {(0, 0): V00, (0, 1): V01, (1, 0): V10, (1, 1): V11, (E - 1, 0): V5, (E - 1, 1): VS}.get((e, o), V1 if o == 0 else 0)
+    return gpsimd, vector, H - gpsimd - vector
 
 
 def tile_moe_bdx_mlp_silu_kernel(tc, dy_words, dy_scales, a, w2, w1, gate, offs, pos1, pos2, pos3, out):
@@ -71,19 +78,20 @@ def tile_moe_bdx_mlp_silu_kernel(tc, dy_words, dy_scales, a, w2, w1, gate, offs,
 
         offs_t = lists.tile([P, S // 16], U16, name="offs_t")
         pos_t = [lists.tile([P, T // 16], U16, name=f"pos_t{r}") for r in range(3)]
-        words = keep.tile([P, PASSES, T], I32, name="words", align_bytes=64)
-        plane = keep.tile([P, T // 4], I32, name="plane", align_bytes=64)
+        words = keep.tile([P, T + WINDOW], I32, name="words", align_bytes=64)
+        plane = keep.tile([P, WINDOW // 4], I32, name="plane", align_bytes=64)
         ident = keep.tile([P, P], F32, name="ident")
         gate_rows = keep.tile([P, P], F32, name="gate_rows")
         neg_gate = keep.tile([P, BLOCKS], F32, name="neg_gate")
-        stage = [keep.tile([P, 2 * STAGE - PACK * P5 if n == 4 else STAGE], BF16, name=f"stage{n}", align_bytes=64)[:] for n in range(KT + 1)]
-        behind = stage[4][:, STAGE - PACK * P5 :]
-        stage[4] = stage[4][:, :STAGE]
+        stage = [keep.tile([P, STAGE + STAGE // 2 if n in (2, 4, KT) else STAGE], BF16, name=f"stage{n}", align_bytes=64) for n in range(KT + 1)]
+        first_pairs = keep.tile([P, STAGE], BF16, name="first_pairs", align_bytes=64)
+        thirds = {n: stage[n][:].bitcast(F32).rearrange("p (a i) -> p a i", i=H) for n in (2, 4, KT)}
+        stage = [tile[:, :STAGE] for tile in stage]
 
         make_identity(nc, ident[:])
         nc.gpsimd.memset(gate_rows[:], 0.0)
-        nc.gpsimd.dma_start(out=gate_rows[0:BLOCKS, :], in_=gate[0, :].rearrange("(b c) -> b c", c=P))
         nc.vector.memset(plane[:], 0)
+        nc.vector.memset(words[:, 2 * T :], 0)
 
         a_rows = a.rearrange("(t p) s -> p t s", p=P)
         words_i32 = dy_words.rearrange("o p t d -> p o (t d)").bitcast(I32)
@@ -93,65 +101,39 @@ def tile_moe_bdx_mlp_silu_kernel(tc, dy_words, dy_scales, a, w2, w1, gate, offs,
         def room(n, shape):
             return keep.tile(shape, F32, name=f"raw{n}", tag=f"room{n % ROOMS}", align_bytes=64)
 
-        def load_a(e):
-            a_t[e] = keep.tile([P, PACK, C], F32, name=f"a_t{e}", tag=f"a{e % 3}", align_bytes=64)
-            nc.sync.dma_start(out=a_t[e][:], in_=a_rows[:, :, C * e : C * (e + 1)])
+        def load_a(pair, pieces):
+            tile = keep.tile([P, PACK, 2 * C], F32, name=f"a_t{pair}", tag=f"a{pair % 2}", align_bytes=64)
+            for n in range(2):
+                a_t[2 * pair + n] = tile[:, :, C * n : C * (n + 1)]
+            return [(tile[:, :, first:last], a_rows[:, :, 2 * C * pair + first : 2 * C * pair + last]) for first, last in pieces]
 
         def load_w2(e, o):
             w2_raw[e, o] = room(PASSES * e + o, [P, PACK, H])
             nc.sync.dma_start(out=w2_raw[e, o][:], in_=w2[e, 512 * o : 512 * (o + 1), :].rearrange("(p j) i -> p j i", j=PACK))
 
         nc.sync.dma_start(offs_t[:], offs)
-        nc.sync.dma_start(out=words[:, 0, :], in_=words_i32[:, 0, :])
-        load_a(0)
-        nc.sync.dma_start(out=words[:, 1, :], in_=words_i32[:, 1, :])
-        load_a(1)
-        if A2_FIRST:
-            load_a(2)
+        nc.sync.dma_start(out=words[:, T : 2 * T], in_=words_i32[:, 0, :])
+        for part in load_a(0, ((0, P), (P, C), (C, 2 * C))):
+            nc.sync.dma_start(*part)
+        nc.sync.dma_start(out=words[:, :T], in_=words_i32[:, 1, :])
         for q in range(4):
-            nc.sync.dma_start(out=plane[32 * q : 32 * q + 8, :], in_=scales_i32[:, 4 * q : 4 * q + 4, :])
+            nc.sync.dma_start(out=plane[32 * q : 32 * q + 8, : T // 4], in_=scales_i32[:, 4 * q : 4 * q + 4, :])
+        nc.sync.dma_start(*load_a(1, ((0, 2 * C),))[0])
+        nc.sync.dma_start(out=gate_rows[0:BLOCKS, :], in_=gate[0, :].rearrange("(b c) -> b c", c=P))
         for e in range(E):
             load_w2(e, 0)
-            if e == 0 and not A2_FIRST:
-                load_a(2)
             load_w2(e, 1)
-            if e + 3 < E:
-                load_a(e + 3)
-            if e == 2:
-                for r, pos in enumerate((pos1, pos2, pos3)):
-                    nc.sync.dma_start(pos_t[r][:], pos)
-
-        def early_expert(kt):
-            return 2 if kt % 2 == 0 else 5
-
-        def late_expert(kt):
-            return 5 if kt % 2 == 0 else 2
-
-        units = []
-        for kt in range(KT):
-            if not STAGGER:
-                units.extend((e, kt, 1) for e in (early_expert(kt), 0, 1, 3, 4, late_expert(kt)))
-            elif kt == 0:
-                units.extend([(2, 0, 1), (0, 0, 1), (1, 0, 1), (3, 0, 2), (4, 0, 2), (5, 0, 2)])
-            else:
-                units.extend((late_expert(kt) - 2 + n, kt, min(2, KT - kt)) for n in range(3))
-        used, filled, current = PASSES * E, 4, None
-        for e, kt, strips in units:
-            if filled + strips > 4:
-                current = room(used, [P, 4 * PACK * P])
-                used, filled = used + 1, 0
-            raw = current[:, PACK * P * filled : PACK * P * (filled + strips)].rearrange("p (j k) -> p j k", j=PACK)
-            filled = filled + strips
-            nc.sync.dma_start(out=raw, in_=w1[e].rearrange("(p j) k -> p j k", j=PACK)[:, :, P * kt : P * (kt + strips)])
-            for n in range(strips):
-                w1_raw[e, kt + n] = raw[:, :, P * n : P * (n + 1)]
+            if e == 0:
+                nc.sync.dma_start(*load_a(2, ((0, 2 * C),))[0])
+            if e >= 3:
+                nc.sync.dma_start(pos_t[e - 3][:], (pos1, pos2, pos3)[e - 3])
 
         g_words = keep.tile([P, PASSES, S], U32, name="g_words", align_bytes=64)
         g_scales = keep.tile([P, S], U8, name="g_scales", align_bytes=64)
         for o in range(PASSES):
             for first in range(0, S, GATHER):
                 slots = offs_t[:, first // 16 : (first + GATHER) // 16]
-                nc.vector.tensor_copy(g_words[:, o, first : first + GATHER], words[:, o, :].bitcast(U32).indirect(slots))
+                nc.vector.tensor_copy(g_words[:, o, first : first + GATHER], words[:, T * (1 - o) : T * (1 - o) + WINDOW].bitcast(U32).indirect(slots))
         for first in range(0, S, GATHER):
             slots = offs_t[:, first // 16 : (first + GATHER) // 16]
             nc.vector.tensor_copy(g_scales[:, first : first + GATHER], plane[:].bitcast(U8).indirect(slots))
@@ -161,10 +143,10 @@ def tile_moe_bdx_mlp_silu_kernel(tc, dy_words, dy_scales, a, w2, w1, gate, offs,
         def act_room(n, shape, name):
             return keep.tile(shape, F32, name=name, tag=f"act{n}", align_bytes=64)
 
-        wide = keep.tile([P, 4 * H - 2 * P4], F32, name="wide", align_bytes=64)
+        wide = {e: keep.tile([P, 4 * H - 2 * P4], F32, name=f"wide{e}", align_bytes=64) for e in range(7 - SIG, E)}
 
         def activations(e):
-            silu_neg[e] = act_room(e % 4, [P, 2, H], f"silu_neg{e}")[:] if e + 1 < E else wide[:, : 2 * H].rearrange("p (h i) -> p h i", h=2)
+            silu_neg[e] = act_room(e % 4, [P, 2, H], f"silu_neg{e}")[:] if e + SIG < 7 else wide[e][:, : 2 * H].rearrange("p (h i) -> p h i", h=2)
             tanh_half[e] = act_room(4 + e % 4, [P, 2, H], f"tanh_half{e}")
             turned_a = [banks[(0, 1, 4, 6)[(2 * e + h) % 4]] for h in range(2)]
             for h in range(2):
@@ -176,24 +158,22 @@ def tile_moe_bdx_mlp_silu_kernel(tc, dy_words, dy_scales, a, w2, w1, gate, offs,
                     nc.scalar.activation(out=dst[:, h, :], in_=turned_a[h][:], func=func, scale=scale)
 
         def w2_stage(e, o):
-            if (e, o) == (4, 0):
-                return wide[:, 2 * H - 2 * P4 :].bitcast(BF16)
-            if (e, o) == (5, 0):
-                return behind
-            return stage[(1, 3)[e % 2] if o == 0 else (ST3, 4, KT)[e % 3]]
+            if e + SIG > 6 and o == 0:
+                return wide[e][:, 2 * H - 2 * P4 :].bitcast(BF16)
+            return stage[(1, 3)[e % 2] if o == 0 else (2, 4, KT)[e % 3]]
 
         def make_sigmoid(e):
             src = tanh_half[e][:].rearrange("p h i -> p (h i)")
-            sigmoid[e] = src if e < 3 else silu_neg[e - 2][:].rearrange("p h i -> p (h i)")
+            sigmoid[e] = src if e < SIG else silu_neg[e - SIG + 1][:].rearrange("p h i -> p (h i)")
             nc.gpsimd.tensor_scalar(out=sigmoid[e], in0=src, scalar1=0.5, scalar2=0.5, op0=ALU.mult, op1=ALU.add)
 
         def make_slope(e):
-            slope[e] = sigmoid[0] if e == 0 else w2_stage(*((e - 1, 1) if e < 4 else (3, e - 4))).bitcast(F32)
+            slope[e] = first_pairs[:].bitcast(F32).rearrange("p (h i) -> p h i", h=2) if e == 0 else thirds[(2, 4, KT)[(e - 1) % 3]][:, 0:3:2, :]
             nc.vector.scalar_tensor_tensor(
                 out=slope[e],
-                in0=silu_neg[e][:].rearrange("p h i -> p (h i)"),
+                in0=silu_neg[e][:],
                 scalar=1.0,
-                in1=sigmoid[e],
+                in1=sigmoid[e].rearrange("p (h i) -> p h i", h=2),
                 op0=ALU.subtract,
                 op1=ALU.mult,
             )
@@ -231,7 +211,7 @@ def tile_moe_bdx_mlp_silu_kernel(tc, dy_words, dy_scales, a, w2, w1, gate, offs,
                 b = 2 * e + h
                 cols = slice(P * b, P * (b + 1))
                 acc = banks[2 + h]
-                order = (1, 0) if e == 0 else (0, 1)
+                order = (1, 0) if e < LATE0 else (0, 1)
                 for o in order:
                     nc.tensor.matmul_mx(
                         out=acc[:],
@@ -244,19 +224,16 @@ def tile_moe_bdx_mlp_silu_kernel(tc, dy_words, dy_scales, a, w2, w1, gate, offs,
                     )
                 da_rows = ring.tile([P, H], BF16, name="da_rows", tag="da_rows", bufs=3, align_bytes=64)
                 nc.vector.scalar_tensor_tensor(
-                    out=da_rows[:], in0=acc[:], scalar=neg_gate[:, b : b + 1], in1=slope[e][:, H * h : H * (h + 1)], op0=ALU.mult, op1=ALU.mult
+                    out=da_rows[:], in0=acc[:], scalar=neg_gate[:, b : b + 1], in1=slope[e][:, h, :], op0=ALU.mult, op1=ALU.mult
                 )
                 pairs = da_rows[:].bitcast(F32)
                 for u in range(2):
                     nc.tensor.transpose(turned[e][:, h, u, :], pairs[:, u : H // 2 : 2], ident[:])
 
-        last_da = keep.tile([P, 2, PACK * C], BF16, name="last_da", align_bytes=64)
+        last_da = []
 
         def quantize_da(e):
-            if e + 1 == E:
-                da = stage[1][:, STAGE // 2 :] if HOLD else last_da[:, 0, :]
-            else:
-                da = (w2_raw[e + 1, 1][:, 0, :] if e < DEFER else w2_raw[E - 1, 1][:, e - DEFER, :]).bitcast(BF16)
+            da = w2_stage(e + 1, 1)[:, STAGE // 2 :] if e + 2 < E else stage[3][:, : STAGE // 2] if e + 1 < E else last_da[0][:]
             nc.scalar.copy(out=da.bitcast(F32).rearrange("p (h r u) -> p h r u", h=2, u=2), in_=turned[e].rearrange("p h u r -> p h r u"))
             da_codes[e] = keep.tile([P, C], U32, name=f"da_codes{e}", align_bytes=64)
             da_scales[e] = keep.tile([P, C], U8, name=f"da_scales{e}", align_bytes=64)
@@ -272,25 +249,46 @@ def tile_moe_bdx_mlp_silu_kernel(tc, dy_words, dy_scales, a, w2, w1, gate, offs,
         make_slope(0)
         quantize_w2(0, 0)
         activations(2)
-        make_sigmoid(2)
+        activations(3)
         for e in range(E):
             cast_w2(e, 1)
             quantize_w2(e, 1)
-            if 0 < e <= DEFER:
+            if e + 1 < E:
+                make_slope(e + 1)
+            if e > 0:
                 quantize_da(e - 1)
-            if e < 4:
-                make_slope(e + 1 if e < 3 else 5)
-            if e + 3 < E:
-                activations(e + 3)
-                make_sigmoid(e + 3)
+            if e == 0:
+                activations(4)
+                activations(5)
+            if e + SIG < E:
+                make_sigmoid(e + SIG)
             first_product(e)
             if e + 1 < E:
                 cast_w2(e + 1, 0)
                 quantize_w2(e + 1, 0)
-            if e == 2:
-                make_slope(4)
-        for e in range(DEFER, E):
-            quantize_da(e)
+
+        def early_expert(kt):
+            return 2 if kt % 2 == 0 else 5
+
+        def late_expert(kt):
+            return 5 if kt % 2 == 0 else 2
+
+        units = []
+        for kt in range(KT):
+            if not STAGGER:
+                units.extend((e, kt, 1) for e in (early_expert(kt), 0, 1, 3, 4, late_expert(kt)))
+            elif kt == 0:
+                units.extend([(2, 0, 1), (0, 0, 1), (1, 0, 1), (3, 0, 2), (4, 0, 2), (5, 0, 2)])
+            else:
+                units.extend((late_expert(kt) - 2 + n, kt, min(2, KT - kt)) for n in range(3))
+        spots = [f"w1_{n}" for n in range(W1_SPOTS)]
+        for u, (e, kt, strips) in enumerate(units):
+            raw = keep.tile([P, PACK, P * strips], F32, name=f"w1_raw{e}_{kt}", tag="last" if u == LAST_DA else f"act{kt - 1}" if kt >= HOLD_FROM and e == HX else spots[u % len(spots)], align_bytes=64)
+            nc.sync.dma_start(out=raw[:], in_=w1[e].rearrange("(p j) k -> p j k", j=PACK)[:, :, P * kt : P * (kt + strips)])
+            for n in range(strips):
+                w1_raw[e, kt + n] = raw[:, :, P * n : P * (n + 1)]
+            if u == LAST_DA:
+                last_da.append(keep.tile([P, PACK * C], BF16, name="last_da", tag="last", align_bytes=64))
 
         w1_codes, w1_scales, dx = {}, {}, {}
         piece = PACK * P
@@ -315,40 +313,53 @@ def tile_moe_bdx_mlp_silu_kernel(tc, dy_words, dy_scales, a, w2, w1, gate, offs,
         def strip_banks(kt):
             return [banks[b] for b in ((4, 6, 0), (1, 5, 2))[kt % 2]]
 
+        def cast_four(kt, experts=FOUR):
+            for e in experts:
+                n = FOUR.index(e)
+                cast = vector_cast if (e, kt) in ON_VECTOR else scalar_cast
+                cast(stage[kt][:, piece * n : piece * (n + 1)], w1_raw[e, kt])
+
+        def two_stage(kt):
+            return first_pairs[:, STAGE // 2 * kt : STAGE // 2 * (kt + 1)] if kt < 2 else upper(kt - 1)
+
+        def cast_two(kt, experts=None):
+            for e in experts or (early_expert(kt), late_expert(kt)):
+                n = (2, 5).index(e)
+                cast = gpsimd_cast if kt > 1 and e == early_expert(kt) else scalar_cast
+                cast(two_stage(kt)[:, piece * n : piece * (n + 1)], w1_raw[e, kt])
+
         def four_experts(kt):
             w1_codes[kt] = ring.tile([P, E * P], U32, name="w1_codes", tag="w1_codes", bufs=3, align_bytes=64)
             w1_scales[kt] = ring.tile([P, E * P], U8, name="w1_scales", tag="w1_scales", bufs=3, align_bytes=64)
             dx[kt] = act_room(kt, [P, S], f"dx{kt}")
-            order = FOUR if kt % 2 == 0 else FOUR[2:] + FOUR[:2]
-            for e in order:
-                n = FOUR.index(e)
-                cut = P if order.index(e) < (VA0, VA1, 0, 0, 0, 0)[kt] else VP if e == order[0] else 0
-                if cut > 0:
-                    vector_cast(stage[kt][:, piece * n : piece * n + PACK * cut], w1_raw[e, kt][:, :, :cut])
-                if cut < P:
-                    scalar_cast(stage[kt][:, piece * n + PACK * cut : piece * (n + 1)], w1_raw[e, kt][:, :, cut:])
+            if kt > 0:
+                cast_four(kt, FOUR[max(LAST_DA - E, 0) :] if kt == 1 else FOUR)
             nc.vector.quantize_mx(out=w1_codes[kt][:, : 4 * P].bitcast(FP8X4), scales=w1_scales[kt][:, : 4 * P], in_=stage[kt][:])
             for n in range(2):
                 products(kt, strip_banks(kt)[n], FOUR[2 * n : 2 * n + 2], 2 * n)
                 nc.scalar.copy(out=dx[kt][:, C * FOUR[2 * n] : C * (FOUR[2 * n] + 2)], in_=strip_banks(kt)[n][:])
 
         def two_experts(kt):
-            staged = upper(kt - 1)
-            for e, cast in ((early_expert(kt), vector_cast if kt == 1 else gpsimd_cast), (late_expert(kt), scalar_cast)):
-                n = (2, 5).index(e)
-                cast(staged[:, piece * n : piece * (n + 1)], w1_raw[e, kt])
+            staged = two_stage(kt)
+            if kt > 0:
+                cast_two(kt, (late_expert(kt),) if kt == 1 else None)
             nc.vector.quantize_mx(out=w1_codes[kt][:, 4 * P :].bitcast(FP8X4), scales=w1_scales[kt][:, 4 * P :], in_=staged)
             products(kt, strip_banks(kt)[2], (2, 5), 4)
             nc.scalar.copy(
                 out=dx[kt][:].rearrange("p (g e c) -> p g e c", g=2, e=3)[:, :, 2, :], in_=strip_banks(kt)[2][:].rearrange("p (g c) -> p g c", g=2)
             )
 
+        cast_four(0)
+        cast_two(0)
+        cast_two(1, (early_expert(1),))
+        cast_four(1, FOUR[: max(LAST_DA - E, 0)])
+        quantize_da(E - 1)
         four_experts(0)
         two_experts(0)
         for kt in range(KT):
             first = stage[kt][:, : STAGE // 2].bitcast(F32)
             second = upper(kt + 1).bitcast(F32)
-            total = upper(kt).bitcast(F32)
+            total = (two_stage(1) if kt == 0 else upper(kt)).bitcast(F32)
             pieces = [(slice(T // 2 * n, T // 2 * (n + 1)), slice(T // 32 * n, T // 32 * (n + 1))) for n in range(2)]
             if kt + 1 < KT:
                 nc.vector.tensor_copy(first, dx[kt][:].indirect(pos_t[0][:]))

@@ -35,13 +35,13 @@ HX = 1
 HOLD_FROM = 2
 STAGE = PACK * H
 STAGGER = False
-P00 = 128
-V01 = 0
-V00 = 384
+P00 = 256
+V01 = 128
+V00 = 256
 V10 = 384
 V11 = 256
 SIG = 2
-V1 = 64
+V1 = 320
 V4 = 0
 V5 = 0
 P4 = 96
@@ -53,7 +53,7 @@ SPLIT = 5
 FORCED = 3
 VA0 = 0
 VA1 = 0
-ON_VECTOR = ((0, 0), (0, 1), (1, 1), (3, 1))
+ON_VECTOR = ((0, 0), (1, 0), (0, 1), (1, 1), (3, 1), (3, 2), (3, 3), (3, 4), (3, 5))
 ST3 = 2
 TURN = (5, 5, 5, 5, 5, 7)
 DEFER = 5

@@ -25,23 +25,24 @@ KT = K // P
 BLOCKS = S // P
 SCALAR_RUN = 2
 VECTOR_RUN = 4
-GATHER = 1536
-WINDOW = 2048
+GATHER = 384
+WINDOW = 512
 FIRST_BLOCK = True
 ROOMS = 6
-W1_SPOTS = 12
-LAST_DA = 6
-HX = 1
+W1_SPOTS = 5
+LAST_DA = 4
+HX = 0
+WHOLE = True
 HOLD_FROM = 2
 STAGE = PACK * H
-STAGGER = False
+STAGGER = True
 P00 = 256
-V01 = 128
+V01 = 0
 V00 = 256
 V10 = 384
 V11 = 256
 SIG = 2
-V1 = 320
+V1 = 128
 V4 = 0
 V5 = 0
 P4 = 96
@@ -53,9 +54,9 @@ SPLIT = 5
 FORCED = 3
 VA0 = 0
 VA1 = 0
-ON_VECTOR = ((0, 0), (1, 0), (0, 1), (1, 1), (3, 1), (3, 2), (3, 3), (3, 4), (3, 5))
+ON_VECTOR = ((0, 0), (1, 0), (0, 1), (1, 1), (0, 2), (1, 2), (4, 3))
 ST3 = 2
-TURN = (5, 5, 5, 5, 5, 7)
+TURN = (5, 7, 5, 7, 5, 7)
 DEFER = 5
 HOLD = False
 
@@ -90,8 +91,8 @@ def tile_moe_bdx_mlp_silu_kernel(tc, dy_words, dy_scales, a, w2, w1, gate, offs,
 
         make_identity(nc, ident[:])
         nc.gpsimd.memset(gate_rows[:], 0.0)
+        nc.gpsimd.dma_start(out=gate_rows[0:BLOCKS, :], in_=gate[0, :].rearrange("(b c) -> b c", c=P))
         nc.vector.memset(plane[:], 0)
-        nc.vector.memset(words[:, 2 * T :], 0)
 
         a_rows = a.rearrange("(t p) s -> p t s", p=P)
         words_i32 = dy_words.rearrange("o p t d -> p o (t d)").bitcast(I32)
@@ -119,7 +120,6 @@ def tile_moe_bdx_mlp_silu_kernel(tc, dy_words, dy_scales, a, w2, w1, gate, offs,
         for q in range(4):
             nc.sync.dma_start(out=plane[32 * q : 32 * q + 8, : T // 4], in_=scales_i32[:, 4 * q : 4 * q + 4, :])
         nc.sync.dma_start(*load_a(1, ((0, 2 * C),))[0])
-        nc.sync.dma_start(out=gate_rows[0:BLOCKS, :], in_=gate[0, :].rearrange("(b c) -> b c", c=P))
         for e in range(E):
             load_w2(e, 0)
             load_w2(e, 1)
@@ -233,7 +233,7 @@ def tile_moe_bdx_mlp_silu_kernel(tc, dy_words, dy_scales, a, w2, w1, gate, offs,
         last_da = []
 
         def quantize_da(e):
-            da = w2_stage(e + 1, 1)[:, STAGE // 2 :] if e + 2 < E else stage[3][:, : STAGE // 2] if e + 1 < E else last_da[0][:]
+            da = tanh_half[e + 3][:, 0, :].bitcast(BF16) if e < 3 else (w2_raw[E - 1, 1][:, 0, :].bitcast(BF16), stage[3][:, : STAGE // 2], last_da[0][:] if last_da else None)[e - 3]
             nc.scalar.copy(out=da.bitcast(F32).rearrange("p (h r u) -> p h r u", h=2, u=2), in_=turned[e].rearrange("p h u r -> p h r u"))
             da_codes[e] = keep.tile([P, C], U32, name=f"da_codes{e}", align_bytes=64)
             da_scales[e] = keep.tile([P, C], U8, name=f"da_scales{e}", align_bytes=64)
@@ -253,9 +253,11 @@ def tile_moe_bdx_mlp_silu_kernel(tc, dy_words, dy_scales, a, w2, w1, gate, offs,
         for e in range(E):
             cast_w2(e, 1)
             quantize_w2(e, 1)
+            if e > 1:
+                quantize_da(e - 2)
             if e + 1 < E:
                 make_slope(e + 1)
-            if e > 0:
+            else:
                 quantize_da(e - 1)
             if e == 0:
                 activations(4)
@@ -281,9 +283,16 @@ def tile_moe_bdx_mlp_silu_kernel(tc, dy_words, dy_scales, a, w2, w1, gate, offs,
                 units.extend([(2, 0, 1), (0, 0, 1), (1, 0, 1), (3, 0, 2), (4, 0, 2), (5, 0, 2)])
             else:
                 units.extend((late_expert(kt) - 2 + n, kt, min(2, KT - kt)) for n in range(3))
-        spots = [f"w1_{n}" for n in range(W1_SPOTS)]
+        spots = [f"w1_{n}" for n in range(W1_SPOTS)] + ["a0", "a1"]
+        taken = 0
         for u, (e, kt, strips) in enumerate(units):
-            raw = keep.tile([P, PACK, P * strips], F32, name=f"w1_raw{e}_{kt}", tag="last" if u == LAST_DA else f"act{kt - 1}" if kt >= HOLD_FROM and e == HX else spots[u % len(spots)], align_bytes=64)
+            if u == LAST_DA:
+                tag = "last"
+            elif kt >= HOLD_FROM and e % 3 == HX:
+                tag = f"act{kt - 1}"
+            else:
+                tag, taken = spots[taken % len(spots)], taken + 1
+            raw = keep.tile([P, PACK, P * strips], F32, name=f"w1_raw{e}_{kt}", tag=tag, align_bytes=64)
             nc.sync.dma_start(out=raw[:], in_=w1[e].rearrange("(p j) k -> p j k", j=PACK)[:, :, P * kt : P * (kt + strips)])
             for n in range(strips):
                 w1_raw[e, kt + n] = raw[:, :, P * n : P * (n + 1)]
@@ -313,9 +322,12 @@ def tile_moe_bdx_mlp_silu_kernel(tc, dy_words, dy_scales, a, w2, w1, gate, offs,
         def strip_banks(kt):
             return [banks[b] for b in ((4, 6, 0), (1, 5, 2))[kt % 2]]
 
+        done = set()
+
         def cast_four(kt, experts=FOUR):
             for e in experts:
                 n = FOUR.index(e)
+                done.add((e, kt))
                 cast = vector_cast if (e, kt) in ON_VECTOR else scalar_cast
                 cast(stage[kt][:, piece * n : piece * (n + 1)], w1_raw[e, kt])
 
@@ -333,7 +345,9 @@ def tile_moe_bdx_mlp_silu_kernel(tc, dy_words, dy_scales, a, w2, w1, gate, offs,
             w1_scales[kt] = ring.tile([P, E * P], U8, name="w1_scales", tag="w1_scales", bufs=3, align_bytes=64)
             dx[kt] = act_room(kt, [P, S], f"dx{kt}")
             if kt > 0:
-                cast_four(kt, FOUR[max(LAST_DA - E, 0) :] if kt == 1 else FOUR)
+                cast_four(kt, tuple(e for e in FOUR if (e, kt) not in done))
+            if kt > 1 and kt + 1 < KT:
+                cast_four(kt + 1, (late_expert(kt) - 2,))
             nc.vector.quantize_mx(out=w1_codes[kt][:, : 4 * P].bitcast(FP8X4), scales=w1_scales[kt][:, : 4 * P], in_=stage[kt][:])
             for n in range(2):
                 products(kt, strip_banks(kt)[n], FOUR[2 * n : 2 * n + 2], 2 * n)
@@ -352,7 +366,7 @@ def tile_moe_bdx_mlp_silu_kernel(tc, dy_words, dy_scales, a, w2, w1, gate, offs,
         cast_four(0)
         cast_two(0)
         cast_two(1, (early_expert(1),))
-        cast_four(1, FOUR[: max(LAST_DA - E, 0)])
+        cast_four(1, FOUR[2:])
         quantize_da(E - 1)
         four_experts(0)
         two_experts(0)
@@ -360,7 +374,8 @@ def tile_moe_bdx_mlp_silu_kernel(tc, dy_words, dy_scales, a, w2, w1, gate, offs,
             first = stage[kt][:, : STAGE // 2].bitcast(F32)
             second = upper(kt + 1).bitcast(F32)
             total = (two_stage(1) if kt == 0 else upper(kt)).bitcast(F32)
-            pieces = [(slice(T // 2 * n, T // 2 * (n + 1)), slice(T // 32 * n, T // 32 * (n + 1))) for n in range(2)]
+            parts = 2 if kt + 1 == KT or not WHOLE else 1
+            pieces = [(slice(T // parts * n, T // parts * (n + 1)), slice(T // 16 // parts * n, T // 16 // parts * (n + 1))) for n in range(parts)]
             if kt + 1 < KT:
                 nc.vector.tensor_copy(first, dx[kt][:].indirect(pos_t[0][:]))
             else:

@@ -29,13 +29,14 @@ GATHER = 384
 WINDOW = 512
 FIRST_BLOCK = True
 ROOMS = 6
-W1_SPOTS = 5
-LAST_DA = 4
-HX = 0
-WHOLE = True
+W1_SPOTS = 12
+LAST_DA = 5
+HX = 1
+HL = 5
+WHOLE = False
 HOLD_FROM = 2
 STAGE = PACK * H
-STAGGER = True
+STAGGER = False
 P00 = 256
 V01 = 0
 V00 = 256
@@ -49,12 +50,13 @@ P4 = 96
 LATE0 = 1
 P5 = 192
 A2_FIRST = False
+V41 = 0
 VS = 128
 SPLIT = 5
 FORCED = 3
 VA0 = 0
 VA1 = 0
-ON_VECTOR = ((0, 0), (1, 0), (0, 1), (1, 1), (0, 2), (1, 2), (4, 3))
+ON_VECTOR = ((0, 0), (1, 0), (0, 1), (1, 1), (3, 1), (4, 1), (0, 2), (0, 3))
 ST3 = 2
 TURN = (5, 7, 5, 7, 5, 7)
 DEFER = 5
@@ -63,7 +65,7 @@ HOLD = False
 
 def w2_shares(e, o):
     gpsimd = {(0, 0): P00, (E - 1, 0): P4}.get((e, o), 0)
-    vector = {(0, 0): V00, (0, 1): V01, (1, 0): V10, (1, 1): V11, (E - 1, 0): V5, (E - 1, 1): VS}.get((e, o), V1 if o == 0 else 0)
+    vector = {(0, 0): V00, (0, 1): V01, (1, 0): V10, (1, 1): V11, (E - 1, 0): V5, (E - 1, 1): VS, (E - 2, 1): V41}.get((e, o), V1 if o == 0 else 0)
     return gpsimd, vector, H - gpsimd - vector
 
 
@@ -288,7 +290,7 @@ def tile_moe_bdx_mlp_silu_kernel(tc, dy_words, dy_scales, a, w2, w1, gate, offs,
         for u, (e, kt, strips) in enumerate(units):
             if u == LAST_DA:
                 tag = "last"
-            elif kt >= HOLD_FROM and e % 3 == HX:
+            elif kt >= HOLD_FROM and e == late_expert(kt):
                 tag = f"act{kt - 1}"
             else:
                 tag, taken = spots[taken % len(spots)], taken + 1
@@ -346,8 +348,6 @@ def tile_moe_bdx_mlp_silu_kernel(tc, dy_words, dy_scales, a, w2, w1, gate, offs,
             dx[kt] = act_room(kt, [P, S], f"dx{kt}")
             if kt > 0:
                 cast_four(kt, tuple(e for e in FOUR if (e, kt) not in done))
-            if kt > 1 and kt + 1 < KT:
-                cast_four(kt + 1, (late_expert(kt) - 2,))
             nc.vector.quantize_mx(out=w1_codes[kt][:, : 4 * P].bitcast(FP8X4), scales=w1_scales[kt][:, : 4 * P], in_=stage[kt][:])
             for n in range(2):
                 products(kt, strip_banks(kt)[n], FOUR[2 * n : 2 * n + 2], 2 * n)
@@ -366,23 +366,19 @@ def tile_moe_bdx_mlp_silu_kernel(tc, dy_words, dy_scales, a, w2, w1, gate, offs,
         cast_four(0)
         cast_two(0)
         cast_two(1, (early_expert(1),))
-        cast_four(1, FOUR[2:])
         quantize_da(E - 1)
         four_experts(0)
         two_experts(0)
         for kt in range(KT):
-            first = stage[kt][:, : STAGE // 2].bitcast(F32)
-            second = upper(kt + 1).bitcast(F32)
+            first = stage[kt + 1][:, : STAGE // 2].bitcast(F32)
+            second = stage[kt][:, : STAGE // 2].bitcast(F32)
+            if kt + 1 < KT:
+                four_experts(kt + 1)
             total = (two_stage(1) if kt == 0 else upper(kt)).bitcast(F32)
             parts = 2 if kt + 1 == KT or not WHOLE else 1
             pieces = [(slice(T // parts * n, T // parts * (n + 1)), slice(T // 16 // parts * n, T // 16 // parts * (n + 1))) for n in range(parts)]
-            if kt + 1 < KT:
-                nc.vector.tensor_copy(first, dx[kt][:].indirect(pos_t[0][:]))
-            else:
-                for cols, part in pieces:
-                    nc.vector.tensor_copy(first[:, cols], dx[kt][:].indirect(pos_t[0][:, part]))
-            if kt + 1 < KT:
-                four_experts(kt + 1)
+            for cols, part in pieces:
+                nc.vector.tensor_copy(first[:, cols], dx[kt][:].indirect(pos_t[0][:, part]))
             for cols, part in pieces:
                 nc.vector.tensor_tensor(second[:, cols], dx[kt][:].indirect(pos_t[1][:, part]), first[:, cols], ALU.add)
             if kt + 1 < KT:

@@ -21,51 +21,33 @@ ALU = mybir.AluOpType
 P = 128
 PACK = 4
 PASSES = N // (P * PACK)
-KT = K // P
+STRIPS = K // P
 BLOCKS = S // P
+STAGE = PACK * H
+HALF_STAGE = STAGE // 2
+PIECE = PACK * P
+LIST_ROWS = 16
+GATHER = 384
 SCALAR_RUN = 2
 VECTOR_RUN = 4
-GATHER = 384
-WINDOW = 512
-FIRST_BLOCK = True
-ROOMS = 6
-W1_SPOTS = 12
-LAST_DA = 5
-HX = 1
-HL = 5
-WHOLE = False
-HOLD_FROM = 2
-STAGE = PACK * H
-STAGGER = False
-P00 = 256
-V01 = 0
-V00 = 256
-V10 = 384
-V11 = 256
-SIG = 2
-V1 = 128
-V4 = 0
-V5 = 0
-P4 = 96
-LATE0 = 1
-P5 = 192
-A2_FIRST = False
-V41 = 0
-VS = 128
-SPLIT = 5
-FORCED = 3
-VA0 = 0
-VA1 = 0
-ON_VECTOR = ((0, 0), (1, 0), (0, 1), (1, 1), (3, 1), (4, 1), (0, 2), (0, 3))
-ST3 = 2
-TURN = (5, 7, 5, 7, 5, 7)
-DEFER = 5
-HOLD = False
+W2_ROOMS = 6
+ACT_SETS = 4
+FOUR = (0, 1, 3, 4)
+EARLY, LATE = 2, 5
+LAST_GPSIMD_COLS = 96
 
 
 def w2_shares(e, o):
-    gpsimd = {(0, 0): P00, (E - 1, 0): P4}.get((e, o), 0)
-    vector = {(0, 0): V00, (0, 1): V01, (1, 0): V10, (1, 1): V11, (E - 1, 0): V5, (E - 1, 1): VS, (E - 2, 1): V41}.get((e, o), V1 if o == 0 else 0)
+    quarter = H // 4
+    gpsimd = {(0, 0): 2 * quarter, (E - 1, 0): LAST_GPSIMD_COLS}.get((e, o), 0)
+    if e == 0:
+        vector = (0, 2 * quarter)[o]
+    elif e == 1:
+        vector = (3 * quarter, 2 * quarter)[o]
+    elif e < E - 1:
+        vector = (quarter, 0)[o]
+    else:
+        vector = (0, quarter)[o]
     return gpsimd, vector, H - gpsimd - vector
 
 
@@ -79,17 +61,19 @@ def tile_moe_bdx_mlp_silu_kernel(tc, dy_words, dy_scales, a, w2, w1, gate, offs,
 
         banks = [psum.tile([P, 512], F32, name=f"bank{b}") for b in range(8)]
 
-        offs_t = lists.tile([P, S // 16], U16, name="offs_t")
-        pos_t = [lists.tile([P, T // 16], U16, name=f"pos_t{r}") for r in range(3)]
-        words = keep.tile([P, T + WINDOW], I32, name="words", align_bytes=64)
-        plane = keep.tile([P, WINDOW // 4], I32, name="plane", align_bytes=64)
+        offs_t = lists.tile([P, S // LIST_ROWS], U16, name="offs_t")
+        pos_t = [lists.tile([P, T // LIST_ROWS], U16, name=f"pos_t{r}") for r in range(3)]
+        words = keep.tile([P, PASSES, T], I32, name="words", align_bytes=64)
+        plane = keep.tile([P, T // 4], I32, name="plane", align_bytes=64)
         ident = keep.tile([P, P], F32, name="ident")
         gate_rows = keep.tile([P, P], F32, name="gate_rows")
         neg_gate = keep.tile([P, BLOCKS], F32, name="neg_gate")
-        stage = [keep.tile([P, STAGE + STAGE // 2 if n in (2, 4, KT) else STAGE], BF16, name=f"stage{n}", align_bytes=64) for n in range(KT + 1)]
-        first_pairs = keep.tile([P, STAGE], BF16, name="first_pairs", align_bytes=64)
-        thirds = {n: stage[n][:].bitcast(F32).rearrange("p (a i) -> p a i", i=H) for n in (2, 4, KT)}
-        stage = [tile[:, :STAGE] for tile in stage]
+
+        pass_one = (2, 4, STRIPS)
+        whole = [keep.tile([P, STAGE + (HALF_STAGE if n in pass_one else 0)], BF16, name=f"stage{n}", align_bytes=64) for n in range(STRIPS + 1)]
+        spare_stage = keep.tile([P, STAGE], BF16, name="spare_stage", align_bytes=64)
+        outer_thirds = {n: whole[n][:].bitcast(F32).rearrange("p (m i) -> p m i", i=H)[:, 0:3:2, :] for n in pass_one}
+        stage = [tile[:, :STAGE] for tile in whole]
 
         make_identity(nc, ident[:])
         nc.gpsimd.memset(gate_rows[:], 0.0)
@@ -99,86 +83,45 @@ def tile_moe_bdx_mlp_silu_kernel(tc, dy_words, dy_scales, a, w2, w1, gate, offs,
         a_rows = a.rearrange("(t p) s -> p t s", p=P)
         words_i32 = dy_words.rearrange("o p t d -> p o (t d)").bitcast(I32)
         scales_i32 = dy_scales.bitcast(I32)
-        a_t, w2_raw, w1_raw = {}, {}, {}
+        a_pairs, w2_raw = {}, {}
 
-        def room(n, shape):
-            return keep.tile(shape, F32, name=f"raw{n}", tag=f"room{n % ROOMS}", align_bytes=64)
-
-        def load_a(pair, pieces):
-            tile = keep.tile([P, PACK, 2 * C], F32, name=f"a_t{pair}", tag=f"a{pair % 2}", align_bytes=64)
-            for n in range(2):
-                a_t[2 * pair + n] = tile[:, :, C * n : C * (n + 1)]
-            return [(tile[:, :, first:last], a_rows[:, :, 2 * C * pair + first : 2 * C * pair + last]) for first, last in pieces]
+        def load_a(pair, first, last):
+            if first == 0:
+                a_pairs[pair] = keep.tile([P, PACK, 2 * C], F32, name=f"a_pair{pair}", tag=f"a{pair % 2}", align_bytes=64)
+            nc.sync.dma_start(a_pairs[pair][:, :, first:last], a_rows[:, :, 2 * C * pair + first : 2 * C * pair + last])
 
         def load_w2(e, o):
-            w2_raw[e, o] = room(PASSES * e + o, [P, PACK, H])
+            n = PASSES * e + o
+            w2_raw[e, o] = keep.tile([P, PACK, H], F32, name=f"w2_raw{n}", tag=f"room{n % W2_ROOMS}", align_bytes=64)
             nc.sync.dma_start(out=w2_raw[e, o][:], in_=w2[e, 512 * o : 512 * (o + 1), :].rearrange("(p j) i -> p j i", j=PACK))
 
         nc.sync.dma_start(offs_t[:], offs)
-        nc.sync.dma_start(out=words[:, T : 2 * T], in_=words_i32[:, 0, :])
-        for part in load_a(0, ((0, P), (P, C), (C, 2 * C))):
-            nc.sync.dma_start(*part)
-        nc.sync.dma_start(out=words[:, :T], in_=words_i32[:, 1, :])
+        nc.sync.dma_start(out=words[:, 0, :], in_=words_i32[:, 0, :])
+        for first, last in ((0, P), (P, C), (C, 2 * C)):
+            load_a(0, first, last)
+        nc.sync.dma_start(out=words[:, 1, :], in_=words_i32[:, 1, :])
         for q in range(4):
-            nc.sync.dma_start(out=plane[32 * q : 32 * q + 8, : T // 4], in_=scales_i32[:, 4 * q : 4 * q + 4, :])
-        nc.sync.dma_start(*load_a(1, ((0, 2 * C),))[0])
-        for e in range(E):
+            nc.sync.dma_start(out=plane[32 * q : 32 * q + 4 * PASSES, :], in_=scales_i32[:, 4 * q : 4 * q + 4, :])
+        load_a(1, 0, C)
+        load_w2(0, 0)
+        load_a(1, C, 2 * C)
+        load_w2(0, 1)
+        load_a(2, 0, 2 * C)
+        for e in range(1, E):
             load_w2(e, 0)
             load_w2(e, 1)
-            if e == 0:
-                nc.sync.dma_start(*load_a(2, ((0, 2 * C),))[0])
-            if e >= 3:
-                nc.sync.dma_start(pos_t[e - 3][:], (pos1, pos2, pos3)[e - 3])
+            if e >= E - 3:
+                nc.sync.dma_start(pos_t[e - (E - 3)][:], (pos1, pos2, pos3)[e - (E - 3)])
 
         g_words = keep.tile([P, PASSES, S], U32, name="g_words", align_bytes=64)
         g_scales = keep.tile([P, S], U8, name="g_scales", align_bytes=64)
         for o in range(PASSES):
             for first in range(0, S, GATHER):
-                slots = offs_t[:, first // 16 : (first + GATHER) // 16]
-                nc.vector.tensor_copy(g_words[:, o, first : first + GATHER], words[:, T * (1 - o) : T * (1 - o) + WINDOW].bitcast(U32).indirect(slots))
+                slots = offs_t[:, first // LIST_ROWS : (first + GATHER) // LIST_ROWS]
+                nc.vector.tensor_copy(g_words[:, o, first : first + GATHER], words[:, o, :].bitcast(U32).indirect(slots))
         for first in range(0, S, GATHER):
-            slots = offs_t[:, first // 16 : (first + GATHER) // 16]
+            slots = offs_t[:, first // LIST_ROWS : (first + GATHER) // LIST_ROWS]
             nc.vector.tensor_copy(g_scales[:, first : first + GATHER], plane[:].bitcast(U8).indirect(slots))
-
-        silu_neg, tanh_half, sigmoid, codes, scales, da_codes, da_scales, slope = {}, {}, {}, {}, {}, {}, {}, {}
-
-        def act_room(n, shape, name):
-            return keep.tile(shape, F32, name=name, tag=f"act{n}", align_bytes=64)
-
-        wide = {e: keep.tile([P, 4 * H - 2 * P4], F32, name=f"wide{e}", align_bytes=64) for e in range(7 - SIG, E)}
-
-        def activations(e):
-            silu_neg[e] = act_room(e % 4, [P, 2, H], f"silu_neg{e}")[:] if e + SIG < 7 else wide[e][:, : 2 * H].rearrange("p (h i) -> p h i", h=2)
-            tanh_half[e] = act_room(4 + e % 4, [P, 2, H], f"tanh_half{e}")
-            turned_a = [banks[(0, 1, 4, 6)[(2 * e + h) % 4]] for h in range(2)]
-            for h in range(2):
-                for t in range(PACK):
-                    nc.tensor.transpose(turned_a[h][:, P * t : P * (t + 1)], a_t[e][:, t, P * h : P * (h + 1)], ident[:])
-            steps = [(silu_neg[e], ACT.Silu, -1.0), (tanh_half[e], ACT.Tanh, 0.5)]
-            for dst, func, scale in steps if e == 0 else reversed(steps):
-                for h in range(2):
-                    nc.scalar.activation(out=dst[:, h, :], in_=turned_a[h][:], func=func, scale=scale)
-
-        def w2_stage(e, o):
-            if e + SIG > 6 and o == 0:
-                return wide[e][:, 2 * H - 2 * P4 :].bitcast(BF16)
-            return stage[(1, 3)[e % 2] if o == 0 else (2, 4, KT)[e % 3]]
-
-        def make_sigmoid(e):
-            src = tanh_half[e][:].rearrange("p h i -> p (h i)")
-            sigmoid[e] = src if e < SIG else silu_neg[e - SIG + 1][:].rearrange("p h i -> p (h i)")
-            nc.gpsimd.tensor_scalar(out=sigmoid[e], in0=src, scalar1=0.5, scalar2=0.5, op0=ALU.mult, op1=ALU.add)
-
-        def make_slope(e):
-            slope[e] = first_pairs[:].bitcast(F32).rearrange("p (h i) -> p h i", h=2) if e == 0 else thirds[(2, 4, KT)[(e - 1) % 3]][:, 0:3:2, :]
-            nc.vector.scalar_tensor_tensor(
-                out=slope[e],
-                in0=silu_neg[e][:],
-                scalar=1.0,
-                in1=sigmoid[e].rearrange("p (h i) -> p h i", h=2),
-                op0=ALU.subtract,
-                op1=ALU.mult,
-            )
 
         def interleave(copy, run, dst, raw):
             copy(out=dst.rearrange("p (c i j) -> p c j i", i=run, j=PACK), in_=raw.rearrange("p j (c i) -> p c j i", i=run))
@@ -194,6 +137,54 @@ def tile_moe_bdx_mlp_silu_kernel(tc, dy_words, dy_scales, a, w2, w1, gate, offs,
                 out=dst.rearrange("p (c j) -> p c j", j=PACK), in0=raw.rearrange("p j c -> p c j"), scalar1=1.0, scalar2=0.0, op0=ALU.mult, op1=ALU.add
             )
 
+        silu_neg, tanh_half, sigmoid, slope, w2_codes, w2_scales, da_codes, da_scales = {}, {}, {}, {}, {}, {}, {}, {}
+
+        def act_room(n, shape, name):
+            return keep.tile(shape, F32, name=name, tag=f"act{n}", align_bytes=64)
+
+        overlap = 2 * LAST_GPSIMD_COLS
+        last_silu = keep.tile([P, 4 * H - overlap], F32, name="last_silu", align_bytes=64)
+
+        def activations(e):
+            if e + 1 < E:
+                silu_neg[e] = act_room(e % ACT_SETS, [P, 2, H], f"silu_neg{e}")[:]
+            else:
+                silu_neg[e] = last_silu[:, : 2 * H].rearrange("p (h i) -> p h i", h=2)
+            tanh_half[e] = act_room(ACT_SETS + e % ACT_SETS, [P, 2, H], f"tanh_half{e}")
+            turned_a = [banks[(0, 1, 4, 6)[(2 * e + h) % 4]] for h in range(2)]
+            for h in range(2):
+                first = C * (e % 2) + P * h
+                for t in range(PACK):
+                    nc.tensor.transpose(turned_a[h][:, P * t : P * (t + 1)], a_pairs[e // 2][:, t, first : first + P], ident[:])
+            steps = [(silu_neg[e], ACT.Silu, -1.0), (tanh_half[e], ACT.Tanh, 0.5)]
+            for dst, func, scale in steps if e == 0 else reversed(steps):
+                for h in range(2):
+                    nc.scalar.activation(out=dst[:, h, :], in_=turned_a[h][:], func=func, scale=scale)
+
+        def make_sigmoid(e):
+            src = tanh_half[e][:].rearrange("p h i -> p (h i)")
+            sigmoid[e] = src if e < 2 else silu_neg[e - 1].rearrange("p h i -> p (h i)")
+            nc.gpsimd.tensor_scalar(out=sigmoid[e], in0=src, scalar1=0.5, scalar2=0.5, op0=ALU.mult, op1=ALU.add)
+
+        def make_slope(e):
+            if e == 0:
+                slope[e] = spare_stage[:].bitcast(F32).rearrange("p (h i) -> p h i", h=2)
+            else:
+                slope[e] = outer_thirds[pass_one[(e - 1) % 3]]
+            nc.vector.scalar_tensor_tensor(
+                out=slope[e],
+                in0=silu_neg[e],
+                scalar=1.0,
+                in1=sigmoid[e].rearrange("p (h i) -> p h i", h=2),
+                op0=ALU.subtract,
+                op1=ALU.mult,
+            )
+
+        def w2_stage(e, o):
+            if (e, o) == (E - 1, 0):
+                return last_silu[:, 2 * H - overlap :].bitcast(BF16)
+            return stage[(1, 3)[e % 2] if o == 0 else pass_one[e % 3]]
+
         def cast_w2(e, o):
             first = 0
             for cast, count in zip((gpsimd_cast, vector_cast, scalar_cast), w2_shares(e, o)):
@@ -202,25 +193,25 @@ def tile_moe_bdx_mlp_silu_kernel(tc, dy_words, dy_scales, a, w2, w1, gate, offs,
                 first = first + count
 
         def quantize_w2(e, o):
-            codes[e, o] = ring.tile([P, H], U32, name="w2_codes", tag="w2_codes", bufs=4, align_bytes=64)
-            scales[e, o] = ring.tile([P, H], U8, name="w2_scales", tag="w2_scales", bufs=4, align_bytes=64)
-            nc.vector.quantize_mx(out=codes[e, o][:].bitcast(FP8X4), scales=scales[e, o][:], in_=w2_stage(e, o)[:])
+            w2_codes[e, o] = ring.tile([P, H], U32, name="w2_codes", tag="w2_codes", bufs=4, align_bytes=64)
+            w2_scales[e, o] = ring.tile([P, H], U8, name="w2_scales", tag="w2_scales", bufs=4, align_bytes=64)
+            nc.vector.quantize_mx(out=w2_codes[e, o][:].bitcast(FP8X4), scales=w2_scales[e, o][:], in_=w2_stage(e, o))
 
-        turned = [banks[b][:].rearrange("p (h u r) -> p h u r", h=2, u=2) for b in TURN]
+        turned_da = [banks[(5, 7)[e % 2]][:].rearrange("p (h u r) -> p h u r", h=2, u=2) for e in range(E)]
 
         def first_product(e):
+            order = (1, 0) if e == 0 else (0, 1)
             for h in range(2):
                 b = 2 * e + h
                 cols = slice(P * b, P * (b + 1))
                 acc = banks[2 + h]
-                order = (1, 0) if e < LATE0 else (0, 1)
                 for o in order:
                     nc.tensor.matmul_mx(
                         out=acc[:],
                         lhsT=g_words[:, o, cols].bitcast(FP8X4),
                         lhsT_scale=g_scales[4 * o : P, cols],
-                        rhs=codes[e, o][:].bitcast(FP8X4),
-                        rhs_scale=scales[e, o][:],
+                        rhs=w2_codes[e, o][:].bitcast(FP8X4),
+                        rhs_scale=w2_scales[e, o][:],
                         start=(o == order[0]),
                         stop=(o == order[1]),
                     )
@@ -230,20 +221,20 @@ def tile_moe_bdx_mlp_silu_kernel(tc, dy_words, dy_scales, a, w2, w1, gate, offs,
                 )
                 pairs = da_rows[:].bitcast(F32)
                 for u in range(2):
-                    nc.tensor.transpose(turned[e][:, h, u, :], pairs[:, u : H // 2 : 2], ident[:])
+                    nc.tensor.transpose(turned_da[e][:, h, u, :], pairs[:, u : H // 2 : 2], ident[:])
 
-        last_da = []
-
-        def quantize_da(e):
-            da = tanh_half[e + 3][:, 0, :].bitcast(BF16) if e < 3 else (w2_raw[E - 1, 1][:, 0, :].bitcast(BF16), stage[3][:, : STAGE // 2], last_da[0][:] if last_da else None)[e - 3]
-            nc.scalar.copy(out=da.bitcast(F32).rearrange("p (h r u) -> p h r u", h=2, u=2), in_=turned[e].rearrange("p h u r -> p h r u"))
+        def quantize_da(e, staged):
+            nc.scalar.copy(out=staged.bitcast(F32).rearrange("p (h r u) -> p h r u", h=2, u=2), in_=turned_da[e].rearrange("p h u r -> p h r u"))
             da_codes[e] = keep.tile([P, C], U32, name=f"da_codes{e}", align_bytes=64)
             da_scales[e] = keep.tile([P, C], U8, name=f"da_scales{e}", align_bytes=64)
-            nc.vector.quantize_mx(out=da_codes[e][:].bitcast(FP8X4), scales=da_scales[e][:], in_=da)
+            nc.vector.quantize_mx(out=da_codes[e][:].bitcast(FP8X4), scales=da_scales[e][:], in_=staged)
+
+        def da_stage(e):
+            if e + 3 < E:
+                return tanh_half[e + 3][:, 0, :].bitcast(BF16)
+            return w2_raw[E - 1, 1][:, 0, :].bitcast(BF16)
 
         activations(0)
-        nc.tensor.transpose(banks[7][:, 0:P], gate_rows[:], ident[:])
-        nc.vector.tensor_scalar(out=neg_gate[:], in0=banks[7][:, 0:BLOCKS], scalar1=-1.0, scalar2=None, op0=ALU.mult)
         activations(1)
         make_sigmoid(0)
         cast_w2(0, 0)
@@ -251,62 +242,51 @@ def tile_moe_bdx_mlp_silu_kernel(tc, dy_words, dy_scales, a, w2, w1, gate, offs,
         make_slope(0)
         quantize_w2(0, 0)
         activations(2)
+        nc.tensor.transpose(banks[1][:, 0:P], gate_rows[:], ident[:])
+        nc.vector.tensor_scalar(out=neg_gate[:], in0=banks[1][:, 0:BLOCKS], scalar1=-1.0, scalar2=None, op0=ALU.mult)
         activations(3)
         for e in range(E):
             cast_w2(e, 1)
             quantize_w2(e, 1)
-            if e > 1:
-                quantize_da(e - 2)
+            if e >= 2:
+                quantize_da(e - 2, da_stage(e - 2))
             if e + 1 < E:
                 make_slope(e + 1)
             else:
-                quantize_da(e - 1)
+                quantize_da(e - 1, stage[3][:, :HALF_STAGE])
             if e == 0:
                 activations(4)
                 activations(5)
-            if e + SIG < E:
-                make_sigmoid(e + SIG)
+            if e + 2 < E:
+                make_sigmoid(e + 2)
             first_product(e)
             if e + 1 < E:
                 cast_w2(e + 1, 0)
                 quantize_w2(e + 1, 0)
 
-        def early_expert(kt):
-            return 2 if kt % 2 == 0 else 5
+        w1_raw, w1_pair = {}, {}
 
-        def late_expert(kt):
-            return 5 if kt % 2 == 0 else 2
+        def load_w1(raw, e, kt):
+            nc.sync.dma_start(out=raw, in_=w1[e].rearrange("(p j) k -> p j k", j=PACK)[:, :, P * kt : P * (kt + 1)])
+            w1_raw[e, kt] = raw
 
-        units = []
-        for kt in range(KT):
-            if not STAGGER:
-                units.extend((e, kt, 1) for e in (early_expert(kt), 0, 1, 3, 4, late_expert(kt)))
-            elif kt == 0:
-                units.extend([(2, 0, 1), (0, 0, 1), (1, 0, 1), (3, 0, 2), (4, 0, 2), (5, 0, 2)])
-            else:
-                units.extend((late_expert(kt) - 2 + n, kt, min(2, KT - kt)) for n in range(3))
-        spots = [f"w1_{n}" for n in range(W1_SPOTS)] + ["a0", "a1"]
-        taken = 0
-        for u, (e, kt, strips) in enumerate(units):
-            if u == LAST_DA:
-                tag = "last"
-            elif kt >= HOLD_FROM and e == late_expert(kt):
-                tag = f"act{kt - 1}"
-            else:
-                tag, taken = spots[taken % len(spots)], taken + 1
-            raw = keep.tile([P, PACK, P * strips], F32, name=f"w1_raw{e}_{kt}", tag=tag, align_bytes=64)
-            nc.sync.dma_start(out=raw[:], in_=w1[e].rearrange("(p j) k -> p j k", j=PACK)[:, :, P * kt : P * (kt + strips)])
-            for n in range(strips):
-                w1_raw[e, kt + n] = raw[:, :, P * n : P * (n + 1)]
-            if u == LAST_DA:
-                last_da.append(keep.tile([P, PACK * C], BF16, name="last_da", tag="last", align_bytes=64))
+        def load_pair(n, kt, tag):
+            w1_pair[n, kt] = keep.tile([P, 2, PACK, P], F32, name=f"w1_pair{kt}_{n}", tag=tag, align_bytes=64)
+            for m in range(2):
+                load_w1(w1_pair[n, kt][:, m], FOUR[2 * n + m], kt)
+
+        first_pair_rooms = ("a1", "room0", "room2", "room3", "a1", "a0")
+        for kt in range(STRIPS):
+            load_w1(keep.tile([P, PACK, P], F32, name=f"w1_early{kt}", align_bytes=64)[:], EARLY, kt)
+            load_pair(0, kt, first_pair_rooms[kt])
+            load_pair(1, kt, ("a0", "room1")[kt] if kt < 2 else f"act{kt - 1}")
+            load_w1(keep.tile([P, PACK, P], F32, name=f"w1_late{kt}", tag=f"late{kt}", align_bytes=64)[:], LATE, kt)
+        last_da = keep.tile([P, PACK * C], BF16, name="last_da", tag="late0", align_bytes=64)
 
         w1_codes, w1_scales, dx = {}, {}, {}
-        piece = PACK * P
-        FOUR = (0, 1, 3, 4)
 
-        def upper(n):
-            return stage[n % (KT + 1)][:, STAGE // 2 :]
+        def strip_banks(kt):
+            return [banks[b] for b in ((4, 6, 0), (1, 5, 2))[kt % 2]]
 
         def products(kt, bank, experts, first):
             for n, e in enumerate(experts):
@@ -321,71 +301,82 @@ def tile_moe_bdx_mlp_silu_kernel(tc, dy_words, dy_scales, a, w2, w1, gate, offs,
                     stop=True,
                 )
 
-        def strip_banks(kt):
-            return [banks[b] for b in ((4, 6, 0), (1, 5, 2))[kt % 2]]
-
-        done = set()
-
-        def cast_four(kt, experts=FOUR):
-            for e in experts:
-                n = FOUR.index(e)
-                done.add((e, kt))
-                cast = vector_cast if (e, kt) in ON_VECTOR else scalar_cast
-                cast(stage[kt][:, piece * n : piece * (n + 1)], w1_raw[e, kt])
+        def cast_four(kt):
+            if kt < 2:
+                for m, e in enumerate(FOUR):
+                    cast = vector_cast if kt == 1 or m < 2 else scalar_cast
+                    cast(stage[kt][:, PIECE * m : PIECE * (m + 1)], w1_raw[e, kt])
+            else:
+                for n in range(2):
+                    nc.scalar.copy(
+                        out=stage[kt][:, HALF_STAGE * n : HALF_STAGE * (n + 1)].rearrange("p (m c i j) -> p m c j i", m=2, i=SCALAR_RUN, j=PACK),
+                        in_=w1_pair[n, kt][:].rearrange("p m j (c i) -> p m c j i", i=SCALAR_RUN),
+                    )
 
         def two_stage(kt):
-            return first_pairs[:, STAGE // 2 * kt : STAGE // 2 * (kt + 1)] if kt < 2 else upper(kt - 1)
+            if kt == 0:
+                return spare_stage[:, :HALF_STAGE]
+            return (stage[1][:, :HALF_STAGE], spare_stage[:, HALF_STAGE:])[kt % 2]
 
-        def cast_two(kt, experts=None):
-            for e in experts or (early_expert(kt), late_expert(kt)):
-                n = (2, 5).index(e)
-                cast = gpsimd_cast if kt > 1 and e == early_expert(kt) else scalar_cast
-                cast(two_stage(kt)[:, piece * n : piece * (n + 1)], w1_raw[e, kt])
+        def cast_early(kt):
+            (gpsimd_cast if kt >= 2 else scalar_cast)(two_stage(kt)[:, :PIECE], w1_raw[EARLY, kt])
+
+        def cast_late(kt):
+            (vector_cast if kt == 1 else scalar_cast)(two_stage(kt)[:, PIECE:], w1_raw[LATE, kt])
 
         def four_experts(kt):
             w1_codes[kt] = ring.tile([P, E * P], U32, name="w1_codes", tag="w1_codes", bufs=3, align_bytes=64)
             w1_scales[kt] = ring.tile([P, E * P], U8, name="w1_scales", tag="w1_scales", bufs=3, align_bytes=64)
             dx[kt] = act_room(kt, [P, S], f"dx{kt}")
             if kt > 0:
-                cast_four(kt, tuple(e for e in FOUR if (e, kt) not in done))
-            nc.vector.quantize_mx(out=w1_codes[kt][:, : 4 * P].bitcast(FP8X4), scales=w1_scales[kt][:, : 4 * P], in_=stage[kt][:])
+                cast_four(kt)
+            nc.vector.quantize_mx(out=w1_codes[kt][:, : 4 * P].bitcast(FP8X4), scales=w1_scales[kt][:, : 4 * P], in_=stage[kt])
             for n in range(2):
                 products(kt, strip_banks(kt)[n], FOUR[2 * n : 2 * n + 2], 2 * n)
                 nc.scalar.copy(out=dx[kt][:, C * FOUR[2 * n] : C * (FOUR[2 * n] + 2)], in_=strip_banks(kt)[n][:])
 
         def two_experts(kt):
-            staged = two_stage(kt)
-            if kt > 0:
-                cast_two(kt, (late_expert(kt),) if kt == 1 else None)
-            nc.vector.quantize_mx(out=w1_codes[kt][:, 4 * P :].bitcast(FP8X4), scales=w1_scales[kt][:, 4 * P :], in_=staged)
-            products(kt, strip_banks(kt)[2], (2, 5), 4)
+            if kt >= 2:
+                cast_early(kt)
+            if kt >= 1:
+                cast_late(kt)
+            nc.vector.quantize_mx(out=w1_codes[kt][:, 4 * P :].bitcast(FP8X4), scales=w1_scales[kt][:, 4 * P :], in_=two_stage(kt))
+            products(kt, strip_banks(kt)[2], (EARLY, LATE), 4)
             nc.scalar.copy(
-                out=dx[kt][:].rearrange("p (g e c) -> p g e c", g=2, e=3)[:, :, 2, :], in_=strip_banks(kt)[2][:].rearrange("p (g c) -> p g c", g=2)
+                out=dx[kt][:].rearrange("p (g m c) -> p g m c", g=2, m=3)[:, :, 2, :], in_=strip_banks(kt)[2][:].rearrange("p (g c) -> p g c", g=2)
             )
 
+        def token_parts(parts):
+            width = T // parts
+            return [(slice(width * n, width * (n + 1)), slice(width * n // LIST_ROWS, width * (n + 1) // LIST_ROWS)) for n in range(parts)]
+
+        def third_gather(kt, parts):
+            total = stage[(kt + 2) % (STRIPS + 1)][:, :HALF_STAGE].bitcast(F32)
+            rows = slice(P * kt, P * (kt + 1))
+            for cols, part in token_parts(parts):
+                nc.vector.tensor_tensor(total[:, cols], dx[kt][:].indirect(pos_t[2][:, part]), two_stage(kt + 1).bitcast(F32)[:, cols], ALU.add)
+                if kt + 1 == STRIPS:
+                    nc.sync.dma_start(out=out[rows, cols], in_=total[:, cols])
+            if kt + 1 < STRIPS:
+                nc.sync.dma_start(out=out[rows, :], in_=total)
+
         cast_four(0)
-        cast_two(0)
-        cast_two(1, (early_expert(1),))
-        quantize_da(E - 1)
+        cast_early(0)
+        cast_late(0)
+        cast_early(1)
+        quantize_da(E - 1, last_da[:])
         four_experts(0)
         two_experts(0)
-        for kt in range(KT):
-            first = stage[kt + 1][:, : STAGE // 2].bitcast(F32)
-            second = stage[kt][:, : STAGE // 2].bitcast(F32)
-            if kt + 1 < KT:
+        for kt in range(STRIPS):
+            first_sum = stage[kt + 1][:, HALF_STAGE:].bitcast(F32)
+            second_sum = two_stage(kt + 1).bitcast(F32)
+            if kt + 1 < STRIPS:
                 four_experts(kt + 1)
-            total = (two_stage(1) if kt == 0 else upper(kt)).bitcast(F32)
-            parts = 2 if kt + 1 == KT or not WHOLE else 1
-            pieces = [(slice(T // parts * n, T // parts * (n + 1)), slice(T // 16 // parts * n, T // 16 // parts * (n + 1))) for n in range(parts)]
-            for cols, part in pieces:
-                nc.vector.tensor_copy(first[:, cols], dx[kt][:].indirect(pos_t[0][:, part]))
-            for cols, part in pieces:
-                nc.vector.tensor_tensor(second[:, cols], dx[kt][:].indirect(pos_t[1][:, part]), first[:, cols], ALU.add)
-            if kt + 1 < KT:
                 two_experts(kt + 1)
-            for cols, part in pieces:
-                nc.vector.tensor_tensor(total[:, cols], dx[kt][:].indirect(pos_t[2][:, part]), second[:, cols], ALU.add)
-                if kt + 1 == KT:
-                    nc.sync.dma_start(out=out[P * kt : P * (kt + 1), cols], in_=total[:, cols])
-            if kt + 1 < KT:
-                nc.sync.dma_start(out=out[P * kt : P * (kt + 1), :], in_=total)
+            if kt > 0:
+                third_gather(kt - 1, 1 if kt + 1 < STRIPS else 2)
+            for cols, part in token_parts(2):
+                nc.vector.tensor_copy(first_sum[:, cols], dx[kt][:].indirect(pos_t[0][:, part]))
+            for cols, part in token_parts(2):
+                nc.vector.tensor_tensor(second_sum[:, cols], dx[kt][:].indirect(pos_t[1][:, part]), first_sum[:, cols], ALU.add)
+        third_gather(STRIPS - 1, 2)

@@ -23,32 +23,22 @@ PACK = 4
 PASSES = N // (P * PACK)
 STRIPS = K // P
 BLOCKS = S // P
-STAGE = PACK * H
-HALF_STAGE = STAGE // 2
+PAIRS = E // 2
 PIECE = PACK * P
 LIST_ROWS = 16
 GATHER = 384
 SCALAR_RUN = 2
 VECTOR_RUN = 4
-W2_ROOMS = 6
-ACT_SETS = 4
-FOUR = (0, 1, 3, 4)
-EARLY, LATE = 2, 5
-LAST_GPSIMD_COLS = 96
+ROOMS = 9
+HEAD = 5
 
 
-def w2_shares(e, o):
-    quarter = H // 4
-    gpsimd = {(0, 0): 2 * quarter, (E - 1, 0): LAST_GPSIMD_COLS}.get((e, o), 0)
+def w2_vector_cols(e, o):
     if e == 0:
-        vector = (0, 2 * quarter)[o]
-    elif e == 1:
-        vector = (3 * quarter, 2 * quarter)[o]
-    elif e < E - 1:
-        vector = (quarter, 0)[o]
-    else:
-        vector = (0, quarter)[o]
-    return gpsimd, vector, H - gpsimd - vector
+        return (0, H // 2)[o]
+    if (e, o) == (E - 1, PASSES - 1):
+        return H // 2
+    return 3 * H // 8
 
 
 def tile_moe_bdx_mlp_silu_kernel(tc, dy_words, dy_scales, a, w2, w1, gate, offs, pos1, pos2, pos3, out):
@@ -69,12 +59,6 @@ def tile_moe_bdx_mlp_silu_kernel(tc, dy_words, dy_scales, a, w2, w1, gate, offs,
         gate_rows = keep.tile([P, P], F32, name="gate_rows")
         neg_gate = keep.tile([P, BLOCKS], F32, name="neg_gate")
 
-        pass_one = (2, 4, STRIPS)
-        whole = [keep.tile([P, STAGE + (HALF_STAGE if n in pass_one else 0)], BF16, name=f"stage{n}", align_bytes=64) for n in range(STRIPS + 1)]
-        spare_stage = keep.tile([P, STAGE], BF16, name="spare_stage", align_bytes=64)
-        outer_thirds = {n: whole[n][:].bitcast(F32).rearrange("p (m i) -> p m i", i=H)[:, 0:3:2, :] for n in pass_one}
-        stage = [tile[:, :STAGE] for tile in whole]
-
         make_identity(nc, ident[:])
         nc.gpsimd.memset(gate_rows[:], 0.0)
         nc.gpsimd.dma_start(out=gate_rows[0:BLOCKS, :], in_=gate[0, :].rearrange("(b c) -> b c", c=P))
@@ -83,33 +67,33 @@ def tile_moe_bdx_mlp_silu_kernel(tc, dy_words, dy_scales, a, w2, w1, gate, offs,
         a_rows = a.rearrange("(t p) s -> p t s", p=P)
         words_i32 = dy_words.rearrange("o p t d -> p o (t d)").bitcast(I32)
         scales_i32 = dy_scales.bitcast(I32)
-        a_pairs, w2_raw = {}, {}
+        a_tiles = [keep.tile([P, PACK, C], F32, name=f"a{e}", tag=f"a{e}", align_bytes=64) for e in range(E)]
+        w2_raw = {}
 
-        def load_a(pair, first, last):
-            if first == 0:
-                a_pairs[pair] = keep.tile([P, PACK, 2 * C], F32, name=f"a_pair{pair}", tag=f"a{pair % 2}", align_bytes=64)
-            nc.sync.dma_start(a_pairs[pair][:, :, first:last], a_rows[:, :, 2 * C * pair + first : 2 * C * pair + last])
+        def load_a(e, first=0, last=C):
+            nc.sync.dma_start(a_tiles[e][:, :, first:last], a_rows[:, :, C * e + first : C * e + last])
 
         def load_w2(e, o):
             n = PASSES * e + o
-            w2_raw[e, o] = keep.tile([P, PACK, H], F32, name=f"w2_raw{n}", tag=f"room{n % W2_ROOMS}", align_bytes=64)
+            w2_raw[e, o] = keep.tile([P, PACK, H], F32, name=f"w2_raw{n}", tag=f"room{n % ROOMS}", align_bytes=64)
             nc.sync.dma_start(out=w2_raw[e, o][:], in_=w2[e, 512 * o : 512 * (o + 1), :].rearrange("(p j) i -> p j i", j=PACK))
 
         nc.sync.dma_start(offs_t[:], offs)
         nc.sync.dma_start(out=words[:, 0, :], in_=words_i32[:, 0, :])
-        for first, last in ((0, P), (P, C), (C, 2 * C)):
-            load_a(0, first, last)
+        load_a(0, 0, P)
+        load_a(0, P, C)
+        load_a(1)
         nc.sync.dma_start(out=words[:, 1, :], in_=words_i32[:, 1, :])
+        load_a(2)
+        load_a(3)
         for q in range(4):
             nc.sync.dma_start(out=plane[32 * q : 32 * q + 4 * PASSES, :], in_=scales_i32[:, 4 * q : 4 * q + 4, :])
-        load_a(1, 0, C)
-        load_w2(0, 0)
-        load_a(1, C, 2 * C)
-        load_w2(0, 1)
-        load_a(2, 0, 2 * C)
-        for e in range(1, E):
+        load_a(4)
+        for e in range(E):
             load_w2(e, 0)
             load_w2(e, 1)
+            if e == 0:
+                load_a(5)
             if e >= E - 3:
                 nc.sync.dma_start(pos_t[e - (E - 3)][:], (pos1, pos2, pos3)[e - (E - 3)])
 
@@ -132,88 +116,57 @@ def tile_moe_bdx_mlp_silu_kernel(tc, dy_words, dy_scales, a, w2, w1, gate, offs,
         def vector_cast(dst, raw):
             interleave(nc.vector.tensor_copy, VECTOR_RUN, dst, raw)
 
-        def gpsimd_cast(dst, raw):
-            nc.gpsimd.tensor_scalar(
-                out=dst.rearrange("p (c j) -> p c j", j=PACK), in0=raw.rearrange("p j c -> p c j"), scalar1=1.0, scalar2=0.0, op0=ALU.mult, op1=ALU.add
-            )
+        sigmoid = [keep.tile([P, 2, H], F32, name=f"sigmoid{e}", tag=f"s{e}", align_bytes=64) for e in range(E)]
+        slope = [keep.tile([P, 2, H], F32, name=f"slope{e}", tag=f"q{e}", align_bytes=64) for e in range(E)]
+        w2_codes, w2_scales, da_codes, da_scales = {}, {}, {}, {}
 
-        silu_neg, tanh_half, sigmoid, slope, w2_codes, w2_scales, da_codes, da_scales = {}, {}, {}, {}, {}, {}, {}, {}
+        def a_banks(e):
+            return [banks[(2 * e + h) % 8] for h in range(2)]
 
-        def act_room(n, shape, name):
-            return keep.tile(shape, F32, name=name, tag=f"act{n}", align_bytes=64)
-
-        overlap = 2 * LAST_GPSIMD_COLS
-        last_silu = keep.tile([P, 4 * H - overlap], F32, name="last_silu", align_bytes=64)
-
-        def activations(e):
-            if e + 1 < E:
-                silu_neg[e] = act_room(e % ACT_SETS, [P, 2, H], f"silu_neg{e}")[:]
-            else:
-                silu_neg[e] = last_silu[:, : 2 * H].rearrange("p (h i) -> p h i", h=2)
-            tanh_half[e] = act_room(ACT_SETS + e % ACT_SETS, [P, 2, H], f"tanh_half{e}")
-            turned_a = [banks[(0, 1, 4, 6)[(2 * e + h) % 4]] for h in range(2)]
+        def turn_a(e):
             for h in range(2):
-                first = C * (e % 2) + P * h
                 for t in range(PACK):
-                    nc.tensor.transpose(turned_a[h][:, P * t : P * (t + 1)], a_pairs[e // 2][:, t, first : first + P], ident[:])
-            steps = [(silu_neg[e], ACT.Silu, -1.0), (tanh_half[e], ACT.Tanh, 0.5)]
-            for dst, func, scale in steps if e == 0 else reversed(steps):
-                for h in range(2):
-                    nc.scalar.activation(out=dst[:, h, :], in_=turned_a[h][:], func=func, scale=scale)
+                    nc.tensor.transpose(a_banks(e)[h][:, P * t : P * (t + 1)], a_tiles[e][:, t, P * h : P * (h + 1)], ident[:])
+
+        def make_silu(e):
+            for h in range(2):
+                nc.scalar.activation(out=slope[e][:, h, :], in_=a_banks(e)[h][:], func=ACT.Silu, scale=-1.0)
 
         def make_sigmoid(e):
-            src = tanh_half[e][:].rearrange("p h i -> p (h i)")
-            sigmoid[e] = src if e < 2 else silu_neg[e - 1].rearrange("p h i -> p (h i)")
-            nc.gpsimd.tensor_scalar(out=sigmoid[e], in0=src, scalar1=0.5, scalar2=0.5, op0=ALU.mult, op1=ALU.add)
+            for h in range(2):
+                nc.scalar.activation(out=sigmoid[e][:, h, :], in_=a_banks(e)[h][:], func=ACT.Tanh, scale=0.5)
+            flat = sigmoid[e][:].rearrange("p h i -> p (h i)")
+            (nc.gpsimd if e < HEAD else nc.vector).tensor_scalar(out=flat, in0=flat, scalar1=0.5, scalar2=0.5, op0=ALU.mult, op1=ALU.add)
 
         def make_slope(e):
-            if e == 0:
-                slope[e] = spare_stage[:].bitcast(F32).rearrange("p (h i) -> p h i", h=2)
-            else:
-                slope[e] = outer_thirds[pass_one[(e - 1) % 3]]
-            nc.vector.scalar_tensor_tensor(
-                out=slope[e],
-                in0=silu_neg[e],
-                scalar=1.0,
-                in1=sigmoid[e].rearrange("p (h i) -> p h i", h=2),
-                op0=ALU.subtract,
-                op1=ALU.mult,
-            )
-
-        def w2_stage(e, o):
-            if (e, o) == (E - 1, 0):
-                return last_silu[:, 2 * H - overlap :].bitcast(BF16)
-            return stage[(1, 3)[e % 2] if o == 0 else pass_one[e % 3]]
-
-        def cast_w2(e, o):
-            first = 0
-            for cast, count in zip((gpsimd_cast, vector_cast, scalar_cast), w2_shares(e, o)):
-                if count > 0:
-                    cast(w2_stage(e, o)[:, PACK * first : PACK * (first + count)], w2_raw[e, o][:, :, first : first + count])
-                first = first + count
+            nc.vector.scalar_tensor_tensor(out=slope[e][:], in0=slope[e][:], scalar=1.0, in1=sigmoid[e][:], op0=ALU.subtract, op1=ALU.mult)
 
         def quantize_w2(e, o):
+            staged = ring.tile([P, PACK * H], BF16, name="w2_staged", tag="w2_staged", bufs=4, align_bytes=64)
+            cut = H - w2_vector_cols(e, o)
+            if cut > 0:
+                scalar_cast(staged[:, : PACK * cut], w2_raw[e, o][:, :, :cut])
+            if cut < H:
+                vector_cast(staged[:, PACK * cut :], w2_raw[e, o][:, :, cut:])
             w2_codes[e, o] = ring.tile([P, H], U32, name="w2_codes", tag="w2_codes", bufs=4, align_bytes=64)
             w2_scales[e, o] = ring.tile([P, H], U8, name="w2_scales", tag="w2_scales", bufs=4, align_bytes=64)
-            nc.vector.quantize_mx(out=w2_codes[e, o][:].bitcast(FP8X4), scales=w2_scales[e, o][:], in_=w2_stage(e, o))
-
-        turned_da = [banks[(5, 7)[e % 2]][:].rearrange("p (h u r) -> p h u r", h=2, u=2) for e in range(E)]
+            nc.vector.quantize_mx(out=w2_codes[e, o][:].bitcast(FP8X4), scales=w2_scales[e, o][:], in_=staged[:])
 
         def first_product(e):
-            order = (1, 0) if e == 0 else (0, 1)
+            turned = banks[6 + e % 2][:].rearrange("p (h u r) -> p h u r", h=2, u=2)
             for h in range(2):
                 b = 2 * e + h
                 cols = slice(P * b, P * (b + 1))
-                acc = banks[2 + h]
-                for o in order:
+                acc = banks[4 + h]
+                for o in range(PASSES):
                     nc.tensor.matmul_mx(
                         out=acc[:],
                         lhsT=g_words[:, o, cols].bitcast(FP8X4),
                         lhsT_scale=g_scales[4 * o : P, cols],
                         rhs=w2_codes[e, o][:].bitcast(FP8X4),
                         rhs_scale=w2_scales[e, o][:],
-                        start=(o == order[0]),
-                        stop=(o == order[1]),
+                        start=(o == 0),
+                        stop=(o == PASSES - 1),
                     )
                 da_rows = ring.tile([P, H], BF16, name="da_rows", tag="da_rows", bufs=3, align_bytes=64)
                 nc.vector.scalar_tensor_tensor(
@@ -221,162 +174,121 @@ def tile_moe_bdx_mlp_silu_kernel(tc, dy_words, dy_scales, a, w2, w1, gate, offs,
                 )
                 pairs = da_rows[:].bitcast(F32)
                 for u in range(2):
-                    nc.tensor.transpose(turned_da[e][:, h, u, :], pairs[:, u : H // 2 : 2], ident[:])
-
-        def quantize_da(e, staged):
-            nc.scalar.copy(out=staged.bitcast(F32).rearrange("p (h r u) -> p h r u", h=2, u=2), in_=turned_da[e].rearrange("p h u r -> p h r u"))
+                    nc.tensor.transpose(turned[:, h, u, :], pairs[:, u : H // 2 : 2], ident[:])
+            staged = ring.tile([P, PACK * C], BF16, name="da_staged", tag="da_staged", bufs=2, align_bytes=64)
+            nc.scalar.copy(out=staged[:].bitcast(F32).rearrange("p (h r u) -> p h r u", h=2, u=2), in_=turned.rearrange("p h u r -> p h r u"))
             da_codes[e] = keep.tile([P, C], U32, name=f"da_codes{e}", align_bytes=64)
             da_scales[e] = keep.tile([P, C], U8, name=f"da_scales{e}", align_bytes=64)
-            nc.vector.quantize_mx(out=da_codes[e][:].bitcast(FP8X4), scales=da_scales[e][:], in_=staged)
+            nc.vector.quantize_mx(out=da_codes[e][:].bitcast(FP8X4), scales=da_scales[e][:], in_=staged[:])
 
-        def da_stage(e):
-            if e + 3 < E:
-                return tanh_half[e + 3][:, 0, :].bitcast(BF16)
-            return w2_raw[E - 1, 1][:, 0, :].bitcast(BF16)
-
-        activations(0)
-        activations(1)
-        make_sigmoid(0)
-        cast_w2(0, 0)
-        make_sigmoid(1)
+        for e in range(HEAD):
+            turn_a(e)
+            if e == 0:
+                make_silu(e)
+            make_sigmoid(e)
+        make_silu(1)
         make_slope(0)
+        turn_a(E - 1)
         quantize_w2(0, 0)
-        activations(2)
-        nc.tensor.transpose(banks[1][:, 0:P], gate_rows[:], ident[:])
-        nc.vector.tensor_scalar(out=neg_gate[:], in0=banks[1][:, 0:BLOCKS], scalar1=-1.0, scalar2=None, op0=ALU.mult)
-        activations(3)
+        make_silu(2)
+        quantize_w2(0, 1)
+        make_silu(3)
+        nc.tensor.transpose(banks[6][:, 0:P], gate_rows[:], ident[:])
+        nc.scalar.activation(out=neg_gate[:], in_=banks[6][:, 0:BLOCKS], func=ACT.Copy, scale=-1.0)
         for e in range(E):
-            cast_w2(e, 1)
-            quantize_w2(e, 1)
-            if e >= 2:
-                quantize_da(e - 2, da_stage(e - 2))
+            if e > 0:
+                quantize_w2(e, 0)
+                quantize_w2(e, 1)
+            first_product(e)
+            if e == 1:
+                make_silu(E - 2)
+            if e == 2:
+                make_sigmoid(E - 1)
+                make_silu(E - 1)
             if e + 1 < E:
                 make_slope(e + 1)
-            else:
-                quantize_da(e - 1, stage[3][:, :HALF_STAGE])
-            if e == 0:
-                activations(4)
-                activations(5)
-            if e + 2 < E:
-                make_sigmoid(e + 2)
-            first_product(e)
-            if e + 1 < E:
-                cast_w2(e + 1, 0)
-                quantize_w2(e + 1, 0)
 
-        w1_raw, w1_pair = {}, {}
-
-        def load_w1(raw, e, kt):
-            nc.sync.dma_start(out=raw, in_=w1[e].rearrange("(p j) k -> p j k", j=PACK)[:, :, P * kt : P * (kt + 1)])
-            w1_raw[e, kt] = raw
-
-        def load_pair(n, kt, tag):
-            w1_pair[n, kt] = keep.tile([P, 2, PACK, P], F32, name=f"w1_pair{kt}_{n}", tag=tag, align_bytes=64)
-            for m in range(2):
-                load_w1(w1_pair[n, kt][:, m], FOUR[2 * n + m], kt)
-
-        first_pair_rooms = ("a1", "room0", "room2", "room3", "a1", "a0")
+        w1_raw = {}
         for kt in range(STRIPS):
-            load_w1(keep.tile([P, PACK, P], F32, name=f"w1_early{kt}", align_bytes=64)[:], EARLY, kt)
-            load_pair(0, kt, first_pair_rooms[kt])
-            load_pair(1, kt, ("a0", "room1")[kt] if kt < 2 else f"act{kt - 1}")
-            load_w1(keep.tile([P, PACK, P], F32, name=f"w1_late{kt}", tag=f"late{kt}", align_bytes=64)[:], LATE, kt)
-        last_da = keep.tile([P, PACK * C], BF16, name="last_da", tag="late0", align_bytes=64)
-
-        w1_codes, w1_scales, dx = {}, {}, {}
-
-        def strip_banks(kt):
-            return [banks[b] for b in ((4, 6, 0), (1, 5, 2))[kt % 2]]
-
-        def products(kt, bank, experts, first):
-            for n, e in enumerate(experts):
-                cols = slice(P * (first + n), P * (first + n + 1))
-                nc.tensor.matmul_mx(
-                    out=bank[:, C * n : C * (n + 1)],
-                    lhsT=w1_codes[kt][:, cols].bitcast(FP8X4),
-                    lhsT_scale=w1_scales[kt][:, cols],
-                    rhs=da_codes[e][:].bitcast(FP8X4),
-                    rhs_scale=da_scales[e][:],
-                    start=True,
-                    stop=True,
-                )
-
-        def cast_four(kt):
-            if kt < 2:
-                for m, e in enumerate(FOUR):
-                    cast = vector_cast if kt == 1 or m < 2 else scalar_cast
-                    cast(stage[kt][:, PIECE * m : PIECE * (m + 1)], w1_raw[e, kt])
-            else:
-                for n in range(2):
-                    nc.scalar.copy(
-                        out=stage[kt][:, HALF_STAGE * n : HALF_STAGE * (n + 1)].rearrange("p (m c i j) -> p m c j i", m=2, i=SCALAR_RUN, j=PACK),
-                        in_=w1_pair[n, kt][:].rearrange("p m j (c i) -> p m c j i", i=SCALAR_RUN),
-                    )
-
-        def two_stage(kt):
-            if kt == 0:
-                return spare_stage[:, :HALF_STAGE]
-            return (stage[1][:, :HALF_STAGE], spare_stage[:, HALF_STAGE:])[kt % 2]
-
-        def cast_early(kt):
-            (gpsimd_cast if kt >= 2 else scalar_cast)(two_stage(kt)[:, :PIECE], w1_raw[EARLY, kt])
-
-        def cast_late(kt):
-            (vector_cast if kt == 1 else scalar_cast)(two_stage(kt)[:, PIECE:], w1_raw[LATE, kt])
-
-        def four_experts(kt):
-            w1_codes[kt] = ring.tile([P, E * P], U32, name="w1_codes", tag="w1_codes", bufs=3, align_bytes=64)
-            w1_scales[kt] = ring.tile([P, E * P], U8, name="w1_scales", tag="w1_scales", bufs=3, align_bytes=64)
-            dx[kt] = act_room(kt, [P, S], f"dx{kt}")
-            if kt > 0:
-                cast_four(kt)
-            nc.vector.quantize_mx(out=w1_codes[kt][:, : 4 * P].bitcast(FP8X4), scales=w1_scales[kt][:, : 4 * P], in_=stage[kt])
-            for n in range(2):
-                products(kt, strip_banks(kt)[n], FOUR[2 * n : 2 * n + 2], 2 * n)
-                nc.scalar.copy(out=dx[kt][:, C * FOUR[2 * n] : C * (FOUR[2 * n] + 2)], in_=strip_banks(kt)[n][:])
-
-        def two_experts(kt):
-            if kt >= 2:
-                cast_early(kt)
-            if kt >= 1:
-                cast_late(kt)
-            nc.vector.quantize_mx(out=w1_codes[kt][:, 4 * P :].bitcast(FP8X4), scales=w1_scales[kt][:, 4 * P :], in_=two_stage(kt))
-            products(kt, strip_banks(kt)[2], (EARLY, LATE), 4)
-            nc.scalar.copy(
-                out=dx[kt][:].rearrange("p (g m c) -> p g m c", g=2, m=3)[:, :, 2, :], in_=strip_banks(kt)[2][:].rearrange("p (g c) -> p g c", g=2)
-            )
+            for n in range(PAIRS):
+                m = PAIRS * kt + n
+                if m % 2 == 0:
+                    quad = keep.tile([P, 2, 2, PACK, P], F32, name=f"w1_quad{m}", tag=f"room{(PASSES * E + m // 2) % ROOMS}", align_bytes=64)
+                room = quad[:, m % 2]
+                for x in range(2):
+                    w1_raw[2 * n + x, kt] = room[:, x]
+                    nc.sync.dma_start(out=room[:, x], in_=w1[2 * n + x].rearrange("(p j) k -> p j k", j=PACK)[:, :, P * kt : P * (kt + 1)])
 
         def token_parts(parts):
             width = T // parts
             return [(slice(width * n, width * (n + 1)), slice(width * n // LIST_ROWS, width * (n + 1) // LIST_ROWS)) for n in range(parts)]
 
-        def third_gather(kt, parts):
-            total = stage[(kt + 2) % (STRIPS + 1)][:, :HALF_STAGE].bitcast(F32)
-            rows = slice(P * kt, P * (kt + 1))
-            for cols, part in token_parts(parts):
-                nc.vector.tensor_tensor(total[:, cols], dx[kt][:].indirect(pos_t[2][:, part]), two_stage(kt + 1).bitcast(F32)[:, cols], ALU.add)
-                if kt + 1 == STRIPS:
-                    nc.sync.dma_start(out=out[rows, cols], in_=total[:, cols])
-            if kt + 1 < STRIPS:
-                nc.sync.dma_start(out=out[rows, :], in_=total)
+        dx, first_part, two_parts, total = {}, {}, {}, {}
+        halves = token_parts(2)
 
-        cast_four(0)
-        cast_early(0)
-        cast_late(0)
-        cast_early(1)
-        quantize_da(E - 1, last_da[:])
-        four_experts(0)
-        two_experts(0)
+        def scratch(tag, name):
+            return keep.tile([P, T], F32, name=name, tag=tag, align_bytes=64)[:]
+
+        def stage_pair(kt, n):
+            room = ring.tile([P, T], F32, name="w1_staged", tag=f"w1_staged{n}", bufs=2, align_bytes=64)[:]
+            if n == 1:
+                two_parts[kt - 1] = room
+            staged = room.bitcast(BF16)
+            for x in range(2):
+                (scalar_cast if n == 0 else vector_cast)(staged[:, PIECE * x : PIECE * (x + 1)], w1_raw[2 * n + x, kt])
+            return staged
+
+        def second_product(kt, n, staged):
+            codes = ring.tile([P, 2 * P], U32, name="w1_codes", tag="w1_codes", bufs=4, align_bytes=64)
+            scales = ring.tile([P, 2 * P], U8, name="w1_scales", tag="w1_scales", bufs=4, align_bytes=64)
+            nc.vector.quantize_mx(out=codes[:].bitcast(FP8X4), scales=scales[:], in_=staged)
+            bank = banks[(PAIRS * kt + n) % 4]
+            for x in range(2):
+                nc.tensor.matmul_mx(
+                    out=bank[:, C * x : C * (x + 1)],
+                    lhsT=codes[:, P * x : P * (x + 1)].bitcast(FP8X4),
+                    lhsT_scale=scales[:, P * x : P * (x + 1)],
+                    rhs=da_codes[2 * n + x][:].bitcast(FP8X4),
+                    rhs_scale=da_scales[2 * n + x][:],
+                    start=True,
+                    stop=True,
+                )
+            nc.scalar.copy(out=dx[kt][:, 2 * C * n : 2 * C * (n + 1)], in_=bank[:])
+
+        def first_gather(kt):
+            first_part[kt] = scratch(f"s{kt}", f"first_part{kt}")
+            for cols, part in halves:
+                nc.scalar.activation(first_part[kt][:, cols], dx[kt][:].indirect(pos_t[0][:, part]), ACT.Copy)
+
+        def second_gather(kt, n):
+            cols, part = halves[n]
+            nc.vector.tensor_tensor(two_parts[kt][:, cols], dx[kt][:].indirect(pos_t[1][:, part]), first_part[kt][:, cols], ALU.add)
+
+        def third_gather(kt, n):
+            if n == 0:
+                total[kt] = scratch(f"q{kt}", f"total{kt}")
+            cols, part = halves[n]
+            rows = slice(P * kt, P * (kt + 1))
+            nc.vector.tensor_tensor(total[kt][:, cols], dx[kt][:].indirect(pos_t[2][:, part]), two_parts[kt][:, cols], ALU.add)
+            if kt + 1 == STRIPS:
+                nc.sync.dma_start(out=out[rows, cols], in_=total[kt][:, cols])
+            elif n == 1:
+                nc.sync.dma_start(out=out[rows, :], in_=total[kt])
+
         for kt in range(STRIPS):
-            first_sum = stage[kt + 1][:, HALF_STAGE:].bitcast(F32)
-            second_sum = two_stage(kt + 1).bitcast(F32)
-            if kt + 1 < STRIPS:
-                four_experts(kt + 1)
-                two_experts(kt + 1)
+            dx[kt] = keep.tile([P, S], F32, name=f"dx{kt}", tag=f"a{kt}", align_bytes=64)
+            second_product(kt, 0, stage_pair(kt, 0))
+            second_product(kt, 1, stage_pair(kt, 1))
+            staged = stage_pair(kt, 2)
             if kt > 0:
-                third_gather(kt - 1, 1 if kt + 1 < STRIPS else 2)
-            for cols, part in token_parts(2):
-                nc.vector.tensor_copy(first_sum[:, cols], dx[kt][:].indirect(pos_t[0][:, part]))
-            for cols, part in token_parts(2):
-                nc.vector.tensor_tensor(second_sum[:, cols], dx[kt][:].indirect(pos_t[1][:, part]), first_sum[:, cols], ALU.add)
-        third_gather(STRIPS - 1, 2)
+                second_gather(kt - 1, 0)
+            second_product(kt, 2, staged)
+            if kt > 0:
+                second_gather(kt - 1, 1)
+                third_gather(kt - 1, 0)
+                third_gather(kt - 1, 1)
+            first_gather(kt)
+        two_parts[STRIPS - 1] = scratch("s0", "last_two_parts")
+        for gather in (second_gather, third_gather):
+            for n in range(2):
+                gather(STRIPS - 1, n)

@@ -26,11 +26,21 @@ BLOCKS = S // P
 PAIRS = E // 2
 PIECE = PACK * P
 LIST_ROWS = 16
-GATHER = 384
+WINDOW = 1024
+GATHER = 768
 SCALAR_RUN = 2
 VECTOR_RUN = 4
-ROOMS = 9
+ROOMS = 5
+W2_VECTOR_COLS = 192
+WIDE = 2 * P
+DOUBLES = STRIPS // 2
+HOLD = (5, 5)
+HELD = 128
 HEAD = 5
+
+
+def scalar_experts(kt):
+    return (3, 3, 2, 2, 2, 2)[kt]
 
 
 def w2_vector_cols(e, o):
@@ -38,7 +48,7 @@ def w2_vector_cols(e, o):
         return (0, H // 2)[o]
     if (e, o) == (E - 1, PASSES - 1):
         return H // 2
-    return 3 * H // 8
+    return W2_VECTOR_COLS
 
 
 def tile_moe_bdx_mlp_silu_kernel(tc, dy_words, dy_scales, a, w2, w1, gate, offs, pos1, pos2, pos3, out):
@@ -53,8 +63,8 @@ def tile_moe_bdx_mlp_silu_kernel(tc, dy_words, dy_scales, a, w2, w1, gate, offs,
 
         offs_t = lists.tile([P, S // LIST_ROWS], U16, name="offs_t")
         pos_t = [lists.tile([P, T // LIST_ROWS], U16, name=f"pos_t{r}") for r in range(3)]
-        words = keep.tile([P, PASSES, T], I32, name="words", align_bytes=64)
-        plane = keep.tile([P, T // 4], I32, name="plane", align_bytes=64)
+        words = keep.tile([P, T + WINDOW], I32, name="words", align_bytes=64)
+        plane = keep.tile([P, WINDOW // 4], I32, name="plane", align_bytes=64)
         ident = keep.tile([P, P], F32, name="ident")
         gate_rows = keep.tile([P, P], F32, name="gate_rows")
         neg_gate = keep.tile([P, BLOCKS], F32, name="neg_gate")
@@ -63,37 +73,41 @@ def tile_moe_bdx_mlp_silu_kernel(tc, dy_words, dy_scales, a, w2, w1, gate, offs,
         nc.gpsimd.memset(gate_rows[:], 0.0)
         nc.gpsimd.dma_start(out=gate_rows[0:BLOCKS, :], in_=gate[0, :].rearrange("(b c) -> b c", c=P))
         nc.vector.memset(plane[:], 0)
+        nc.vector.memset(words[:, PASSES * T :], 0)
 
         a_rows = a.rearrange("(t p) s -> p t s", p=P)
         words_i32 = dy_words.rearrange("o p t d -> p o (t d)").bitcast(I32)
         scales_i32 = dy_scales.bitcast(I32)
-        a_tiles = [keep.tile([P, PACK, C], F32, name=f"a{e}", tag=f"a{e}", align_bytes=64) for e in range(E)]
-        w2_raw = {}
+        shared = keep.tile([P, HEAD * 2 * H], F32, name="shared", align_bytes=64)
+        a_of = {e: keep.tile([P, PACK, C], F32, name=f"a{e}", tag=f"a{e}", align_bytes=64)[:] for e in (0, 1, 2, 3, 5)}
+        a_of[4] = shared[:, 2 * H - P : 2 * H - P + PACK * 2 * H].rearrange("p (t s) -> p t s", t=PACK)[:, :, :C]
+        w2_raw, w2_room = {}, {}
 
-        def load_a(e, first=0, last=C):
-            nc.sync.dma_start(a_tiles[e][:, :, first:last], a_rows[:, :, C * e + first : C * e + last])
+        def load_a(dst, first):
+            nc.sync.dma_start(dst, a_rows[:, :, first : first + dst.shape[2]])
 
         def load_w2(e, o):
-            n = PASSES * e + o
-            w2_raw[e, o] = keep.tile([P, PACK, H], F32, name=f"w2_raw{n}", tag=f"room{n % ROOMS}", align_bytes=64)
-            nc.sync.dma_start(out=w2_raw[e, o][:], in_=w2[e, 512 * o : 512 * (o + 1), :].rearrange("(p j) i -> p j i", j=PACK))
+            if o == 0:
+                w2_room[e] = keep.tile([P, PASSES * PACK * H], F32, name=f"w2_raw{e}", tag=f"room{e % ROOMS}", align_bytes=64)
+            w2_raw[e, o] = w2_room[e][:, PACK * H * o : PACK * H * (o + 1)].rearrange("p (j i) -> p j i", j=PACK)
+            nc.sync.dma_start(out=w2_raw[e, o], in_=w2[e, 512 * o : 512 * (o + 1), :].rearrange("(p j) i -> p j i", j=PACK))
 
         nc.sync.dma_start(offs_t[:], offs)
-        nc.sync.dma_start(out=words[:, 0, :], in_=words_i32[:, 0, :])
-        load_a(0, 0, P)
-        load_a(0, P, C)
-        load_a(1)
-        nc.sync.dma_start(out=words[:, 1, :], in_=words_i32[:, 1, :])
-        load_a(2)
-        load_a(3)
+        nc.sync.dma_start(out=words[:, T : 2 * T], in_=words_i32[:, 0, :])
+        load_a(a_of[0][:, :, :P], 0)
+        load_a(a_of[0][:, :, P:], P)
+        load_a(a_of[1], C)
+        nc.sync.dma_start(out=words[:, :T], in_=words_i32[:, 1, :])
+        load_a(a_of[2], 2 * C)
+        load_a(a_of[3], 3 * C)
         for q in range(4):
-            nc.sync.dma_start(out=plane[32 * q : 32 * q + 4 * PASSES, :], in_=scales_i32[:, 4 * q : 4 * q + 4, :])
-        load_a(4)
+            nc.sync.dma_start(out=plane[32 * q : 32 * q + 4 * PASSES, : T // 4], in_=scales_i32[:, 4 * q : 4 * q + 4, :])
+        load_a(a_of[4], 4 * C)
         for e in range(E):
             load_w2(e, 0)
             load_w2(e, 1)
             if e == 0:
-                load_a(5)
+                load_a(a_of[5], 5 * C)
             if e >= E - 3:
                 nc.sync.dma_start(pos_t[e - (E - 3)][:], (pos1, pos2, pos3)[e - (E - 3)])
 
@@ -102,7 +116,7 @@ def tile_moe_bdx_mlp_silu_kernel(tc, dy_words, dy_scales, a, w2, w1, gate, offs,
         for o in range(PASSES):
             for first in range(0, S, GATHER):
                 slots = offs_t[:, first // LIST_ROWS : (first + GATHER) // LIST_ROWS]
-                nc.vector.tensor_copy(g_words[:, o, first : first + GATHER], words[:, o, :].bitcast(U32).indirect(slots))
+                nc.vector.tensor_copy(g_words[:, o, first : first + GATHER], words[:, T * (1 - o) : T * (1 - o) + WINDOW].bitcast(U32).indirect(slots))
         for first in range(0, S, GATHER):
             slots = offs_t[:, first // LIST_ROWS : (first + GATHER) // LIST_ROWS]
             nc.vector.tensor_copy(g_scales[:, first : first + GATHER], plane[:].bitcast(U8).indirect(slots))
@@ -116,8 +130,10 @@ def tile_moe_bdx_mlp_silu_kernel(tc, dy_words, dy_scales, a, w2, w1, gate, offs,
         def vector_cast(dst, raw):
             interleave(nc.vector.tensor_copy, VECTOR_RUN, dst, raw)
 
+        slope = [shared[:, 2 * H * e : 2 * H * (e + 1)].rearrange("p (h i) -> p h i", h=2) for e in range(HEAD)]
+        slope = slope + [keep.tile([P, 2, H], F32, name=f"slope{e}", tag=f"q{e}", align_bytes=64)[:] for e in range(HEAD, E)]
+        silu = [keep.tile([P, 2, H], F32, name="silu0", tag="s5", align_bytes=64)[:]] + slope[1:]
         sigmoid = [keep.tile([P, 2, H], F32, name=f"sigmoid{e}", tag=f"s{e}", align_bytes=64) for e in range(E)]
-        slope = [keep.tile([P, 2, H], F32, name=f"slope{e}", tag=f"q{e}", align_bytes=64) for e in range(E)]
         w2_codes, w2_scales, da_codes, da_scales = {}, {}, {}, {}
 
         def a_banks(e):
@@ -126,11 +142,11 @@ def tile_moe_bdx_mlp_silu_kernel(tc, dy_words, dy_scales, a, w2, w1, gate, offs,
         def turn_a(e):
             for h in range(2):
                 for t in range(PACK):
-                    nc.tensor.transpose(a_banks(e)[h][:, P * t : P * (t + 1)], a_tiles[e][:, t, P * h : P * (h + 1)], ident[:])
+                    nc.tensor.transpose(a_banks(e)[h][:, P * t : P * (t + 1)], a_of[e][:, t, P * h : P * (h + 1)], ident[:])
 
         def make_silu(e):
             for h in range(2):
-                nc.scalar.activation(out=slope[e][:, h, :], in_=a_banks(e)[h][:], func=ACT.Silu, scale=-1.0)
+                nc.scalar.activation(out=silu[e][:, h, :], in_=a_banks(e)[h][:], func=ACT.Silu, scale=-1.0)
 
         def make_sigmoid(e):
             for h in range(2):
@@ -139,13 +155,16 @@ def tile_moe_bdx_mlp_silu_kernel(tc, dy_words, dy_scales, a, w2, w1, gate, offs,
             (nc.gpsimd if e < HEAD else nc.vector).tensor_scalar(out=flat, in0=flat, scalar1=0.5, scalar2=0.5, op0=ALU.mult, op1=ALU.add)
 
         def make_slope(e):
-            nc.vector.scalar_tensor_tensor(out=slope[e][:], in0=slope[e][:], scalar=1.0, in1=sigmoid[e][:], op0=ALU.subtract, op1=ALU.mult)
+            nc.vector.scalar_tensor_tensor(out=slope[e], in0=silu[e], scalar=1.0, in1=sigmoid[e][:], op0=ALU.subtract, op1=ALU.mult)
 
         def quantize_w2(e, o):
-            staged = ring.tile([P, PACK * H], BF16, name="w2_staged", tag="w2_staged", bufs=4, align_bytes=64)
+            staged = ring.tile([P, PACK * H], BF16, name="w2_staged", tag="w2_staged", bufs=3, align_bytes=64)
             cut = H - w2_vector_cols(e, o)
+            first = HELD if (o == 1 and e > 0) else 0
+            if first > 0:
+                scalar_cast(staged[:, : PACK * first], w2_raw[e, o][:, :, :first])
             if cut > 0:
-                scalar_cast(staged[:, : PACK * cut], w2_raw[e, o][:, :, :cut])
+                scalar_cast(staged[:, PACK * first : PACK * cut], w2_raw[e, o][:, :, first:cut])
             if cut < H:
                 vector_cast(staged[:, PACK * cut :], w2_raw[e, o][:, :, cut:])
             w2_codes[e, o] = ring.tile([P, H], U32, name="w2_codes", tag="w2_codes", bufs=4, align_bytes=64)
@@ -175,11 +194,17 @@ def tile_moe_bdx_mlp_silu_kernel(tc, dy_words, dy_scales, a, w2, w1, gate, offs,
                 pairs = da_rows[:].bitcast(F32)
                 for u in range(2):
                     nc.tensor.transpose(turned[:, h, u, :], pairs[:, u : H // 2 : 2], ident[:])
-            staged = ring.tile([P, PACK * C], BF16, name="da_staged", tag="da_staged", bufs=2, align_bytes=64)
-            nc.scalar.copy(out=staged[:].bitcast(F32).rearrange("p (h r u) -> p h r u", h=2, u=2), in_=turned.rearrange("p h u r -> p h r u"))
+
+        def quantize_da(e):
+            turned = banks[6 + e % 2][:].rearrange("p (h u r) -> p h u r", h=2, u=2)
+            if e + 1 < E:
+                staged = w2_room[e + 1][:, (PACK - 1) * H + HELD : PACK * H + HELD].bitcast(BF16)
+            else:
+                staged = keep.tile([P, PACK * C], BF16, name="last_da", tag="q5x", align_bytes=64)[:]
+            nc.scalar.copy(out=staged.bitcast(F32).rearrange("p (h r u) -> p h r u", h=2, u=2), in_=turned.rearrange("p h u r -> p h r u"))
             da_codes[e] = keep.tile([P, C], U32, name=f"da_codes{e}", align_bytes=64)
             da_scales[e] = keep.tile([P, C], U8, name=f"da_scales{e}", align_bytes=64)
-            nc.vector.quantize_mx(out=da_codes[e][:].bitcast(FP8X4), scales=da_scales[e][:], in_=staged[:])
+            nc.vector.quantize_mx(out=da_codes[e][:].bitcast(FP8X4), scales=da_scales[e][:], in_=staged)
 
         for e in range(HEAD):
             turn_a(e)
@@ -199,6 +224,7 @@ def tile_moe_bdx_mlp_silu_kernel(tc, dy_words, dy_scales, a, w2, w1, gate, offs,
             if e > 0:
                 quantize_w2(e, 0)
                 quantize_w2(e, 1)
+                quantize_da(e - 1)
             first_product(e)
             if e == 1:
                 make_silu(E - 2)
@@ -208,46 +234,57 @@ def tile_moe_bdx_mlp_silu_kernel(tc, dy_words, dy_scales, a, w2, w1, gate, offs,
             if e + 1 < E:
                 make_slope(e + 1)
 
+        w1_rows = w1.rearrange("e (p j) k -> p e j k", j=PACK)
         w1_raw = {}
-        for kt in range(STRIPS):
-            for n in range(PAIRS):
-                m = PAIRS * kt + n
-                if m % 2 == 0:
-                    quad = keep.tile([P, 2, 2, PACK, P], F32, name=f"w1_quad{m}", tag=f"room{(PASSES * E + m // 2) % ROOMS}", align_bytes=64)
-                room = quad[:, m % 2]
-                for x in range(2):
-                    w1_raw[2 * n + x, kt] = room[:, x]
-                    nc.sync.dma_start(out=room[:, x], in_=w1[2 * n + x].rearrange("(p j) k -> p j k", j=PACK)[:, :, P * kt : P * (kt + 1)])
+        for d in range(DOUBLES):
+            for e in range(E):
+                m = E * d + e
+                if m % 4 == 0:
+                    room = keep.tile([P, 4, PACK, WIDE], F32, name=f"w1_raw{m}", tag=f"room{(E + m // 4) % ROOMS}", align_bytes=64)
+                w1_raw[e, d] = room[:, m % 4]
+                if d + 1 < DOUBLES or e < E - 2:
+                    nc.sync.dma_start(out=w1_raw[e, d], in_=w1_rows[:, e, :, WIDE * d : WIDE * (d + 1)])
+        for s in range(2):
+            for e in (E - 2, E - 1):
+                first = WIDE * (DOUBLES - 1) + P * s
+                nc.sync.dma_start(out=w1_raw[e, DOUBLES - 1][:, :, P * s : P * (s + 1)], in_=w1_rows[:, e, :, first : first + P])
 
         def token_parts(parts):
             width = T // parts
             return [(slice(width * n, width * (n + 1)), slice(width * n // LIST_ROWS, width * (n + 1) // LIST_ROWS)) for n in range(parts)]
 
-        dx, first_part, two_parts, total = {}, {}, {}, {}
-        halves = token_parts(2)
+        dx, first_part, two_parts, total, staged = {}, {}, {}, {}, {}
+        spare = [shared[:, T * n : T * (n + 1)] for n in range(9)]
 
-        def scratch(tag, name):
-            return keep.tile([P, T], F32, name=name, tag=tag, align_bytes=64)[:]
+        def cast_piece(cast, e, d, strips=(0, 1)):
+            if (e // 2, d) not in staged:
+                staged[e // 2, d] = ring.tile([P, 2, 2, PIECE], BF16, name="w2_staged", tag="w2_staged", bufs=3, align_bytes=64)
+            run = SCALAR_RUN if cast == "scalar" else VECTOR_RUN
+            lo, hi = strips[0], strips[-1] + 1
+            (nc.scalar.copy if cast == "scalar" else nc.vector.tensor_copy)(
+                out=staged[e // 2, d][:, lo:hi, e % 2].rearrange("p s (c i j) -> p s c j i", i=run, j=PACK),
+                in_=w1_raw[e, d][:, :, P * lo : P * hi].rearrange("p j (s c i) -> p s c j i", s=hi - lo, i=run),
+            )
 
-        def stage_pair(kt, n):
-            room = ring.tile([P, T], F32, name="w1_staged", tag=f"w1_staged{n}", bufs=2, align_bytes=64)[:]
-            if n == 1:
-                two_parts[kt - 1] = room
-            staged = room.bitcast(BF16)
-            for x in range(2):
-                (scalar_cast if n == 0 else vector_cast)(staged[:, PIECE * x : PIECE * (x + 1)], w1_raw[2 * n + x, kt])
-            return staged
+        def products(n, d, strips=(0, 1)):
+            lo, hi = strips[0], strips[-1] + 1
+            width = 2 * P * (hi - lo)
+            codes = ring.tile([P, width], U32, name="w2_codes", tag="w2_codes", bufs=4, align_bytes=64)
+            scales = ring.tile([P, width], U8, name="w2_scales", tag="w2_scales", bufs=4, align_bytes=64)
+            nc.vector.quantize_mx(out=codes[:].bitcast(FP8X4), scales=scales[:], in_=staged[n, d][:, lo:hi].rearrange("p s x c -> p (s x c)"))
+            for s in strips:
+                cols = [slice(P * (2 * (s - lo) + x), P * (2 * (s - lo) + x + 1)) for x in range(2)]
+                pair_product(2 * d + s, n, [codes[:, c] for c in cols], [scales[:, c] for c in cols])
+                if n + 1 == PAIRS:
+                    first_gather(2 * d + s, 2 if d + 1 == DOUBLES else 1)
 
-        def second_product(kt, n, staged):
-            codes = ring.tile([P, 2 * P], U32, name="w1_codes", tag="w1_codes", bufs=4, align_bytes=64)
-            scales = ring.tile([P, 2 * P], U8, name="w1_scales", tag="w1_scales", bufs=4, align_bytes=64)
-            nc.vector.quantize_mx(out=codes[:].bitcast(FP8X4), scales=scales[:], in_=staged)
-            bank = banks[(PAIRS * kt + n) % 4]
+        def pair_product(kt, n, codes, scales):
+            bank = banks[(2 * (PAIRS * (kt // 2) + n) + kt % 2) % 4]
             for x in range(2):
                 nc.tensor.matmul_mx(
                     out=bank[:, C * x : C * (x + 1)],
-                    lhsT=codes[:, P * x : P * (x + 1)].bitcast(FP8X4),
-                    lhsT_scale=scales[:, P * x : P * (x + 1)],
+                    lhsT=codes[x].bitcast(FP8X4),
+                    lhsT_scale=scales[x],
                     rhs=da_codes[2 * n + x][:].bitcast(FP8X4),
                     rhs_scale=da_scales[2 * n + x][:],
                     start=True,
@@ -255,40 +292,65 @@ def tile_moe_bdx_mlp_silu_kernel(tc, dy_words, dy_scales, a, w2, w1, gate, offs,
                 )
             nc.scalar.copy(out=dx[kt][:, 2 * C * n : 2 * C * (n + 1)], in_=bank[:])
 
-        def first_gather(kt):
-            first_part[kt] = scratch(f"s{kt}", f"first_part{kt}")
-            for cols, part in halves:
+        def first_gather(kt, parts):
+            first_part[kt] = ring.tile([P, T], F32, name="first_part", tag="first_part", bufs=2, align_bytes=64)
+            for cols, part in token_parts(parts):
                 nc.scalar.activation(first_part[kt][:, cols], dx[kt][:].indirect(pos_t[0][:, part]), ACT.Copy)
 
-        def second_gather(kt, n):
-            cols, part = halves[n]
-            nc.vector.tensor_tensor(two_parts[kt][:, cols], dx[kt][:].indirect(pos_t[1][:, part]), first_part[kt][:, cols], ALU.add)
+        def second_gather(kt, parts):
+            two_parts[kt] = spare[STRIPS + kt % 2]
+            if kt % 2 == 1 and kt + 1 < STRIPS:
+                two_parts[kt] = staged[1, kt // 2 + 1][:, 0].rearrange("p x c -> p (x c)").bitcast(F32)
+            for cols, part in token_parts(parts):
+                nc.vector.tensor_tensor(two_parts[kt][:, cols], dx[kt][:].indirect(pos_t[1][:, part]), first_part[kt][:, cols], ALU.add)
 
-        def third_gather(kt, n):
-            if n == 0:
-                total[kt] = scratch(f"q{kt}", f"total{kt}")
-            cols, part = halves[n]
+        def third_gather(kt, parts):
+            total[kt] = spare[kt]
+            if kt % 2 == 1 and kt + 1 < STRIPS:
+                total[kt] = w1_raw[HOLD[kt // 2], kt // 2 + 1].rearrange("p j c -> p (j c)")[:, T:]
             rows = slice(P * kt, P * (kt + 1))
-            nc.vector.tensor_tensor(total[kt][:, cols], dx[kt][:].indirect(pos_t[2][:, part]), two_parts[kt][:, cols], ALU.add)
-            if kt + 1 == STRIPS:
+            for cols, part in token_parts(parts):
+                nc.vector.tensor_tensor(total[kt][:, cols], dx[kt][:].indirect(pos_t[2][:, part]), two_parts[kt][:, cols], ALU.add)
                 nc.sync.dma_start(out=out[rows, cols], in_=total[kt][:, cols])
-            elif n == 1:
-                nc.sync.dma_start(out=out[rows, :], in_=total[kt])
 
-        for kt in range(STRIPS):
-            dx[kt] = keep.tile([P, S], F32, name=f"dx{kt}", tag=f"a{kt}", align_bytes=64)
-            second_product(kt, 0, stage_pair(kt, 0))
-            second_product(kt, 1, stage_pair(kt, 1))
-            staged = stage_pair(kt, 2)
-            if kt > 0:
-                second_gather(kt - 1, 0)
-            second_product(kt, 2, staged)
-            if kt > 0:
-                second_gather(kt - 1, 1)
-                third_gather(kt - 1, 0)
-                third_gather(kt - 1, 1)
-            first_gather(kt)
-        two_parts[STRIPS - 1] = scratch("s0", "last_two_parts")
-        for gather in (second_gather, third_gather):
-            for n in range(2):
-                gather(STRIPS - 1, n)
+        for d in range(DOUBLES):
+            for kt in (2 * d, 2 * d + 1):
+                dx[kt] = keep.tile([P, S], F32, name=f"dx{kt}", tag=f"a{kt % 4}", align_bytes=64)
+            if d == 0:
+                for e in range(3):
+                    cast_piece("scalar", e, d)
+                quantize_da(E - 1)
+                cast_piece("vector", 3, d)
+                products(0, d)
+                cast_piece("vector", 4, d)
+                products(1, d)
+                cast_piece("vector", 5, d)
+                products(2, d)
+                continue
+            cast_piece("vector", 0, d)
+            cast_piece("vector", 1, d)
+            second_gather(2 * d - 2, 1)
+            cast_piece("scalar", 2, d)
+            cast_piece("scalar", 3, d)
+            products(0, d)
+            third_gather(2 * d - 2, 1)
+            if d + 1 < DOUBLES:
+                cast_piece("vector", 4, d)
+                products(1, d)
+                cast_piece("vector", 5, d)
+                second_gather(2 * d - 1, 1)
+                products(2, d)
+                third_gather(2 * d - 1, 1)
+            else:
+                cast_piece("vector", 4, d, (0,))
+                cast_piece("vector", 5, d, (0,))
+                products(1, d)
+                products(2, d, (0,))
+                second_gather(2 * d - 1, 1)
+                cast_piece("vector", 4, d, (1,))
+                cast_piece("vector", 5, d, (1,))
+                products(2, d, (1,))
+                third_gather(2 * d - 1, 1)
+        for kt in (STRIPS - 2, STRIPS - 1):
+            second_gather(kt, 2)
+            third_gather(kt, 2)

@@ -31,24 +31,25 @@ GATHER = 768
 SCALAR_RUN = 2
 VECTOR_RUN = 4
 ROOMS = 5
-W2_VECTOR_COLS = 192
-WIDE = 2 * P
-DOUBLES = STRIPS // 2
-HOLD = (5, 5)
+VECTOR_COLS = (0, 384, 384, 384, 128, 128)
+GPSIMD_COLS = 160
+GPSIMD_EXPERTS = ()
+PAD = 2 * H
+SCALAR_EXTRA = 0
+VECTOR_ALONE = ()
+LAST_COLS = (0, 0, 0, 0, 256, 256)
 HELD = 128
+SECOND_BANK = 3
+VECTOR_COPIES = ()
 HEAD = 5
 
 
-def scalar_experts(kt):
-    return (3, 3, 2, 2, 2, 2)[kt]
-
-
-def w2_vector_cols(e, o):
+def w2_shares(e, o):
+    if o == 0:
+        return (("scalar", H),) if e == 0 else (("vector", VECTOR_COLS[e]), ("scalar", H - VECTOR_COLS[e]))
     if e == 0:
-        return (0, H // 2)[o]
-    if (e, o) == (E - 1, PASSES - 1):
-        return H // 2
-    return W2_VECTOR_COLS
+        return ("scalar", H // 2), ("vector", H // 2)
+    return ("scalar", HELD), ("scalar", H - HELD - LAST_COLS[e]), ("vector", LAST_COLS[e])
 
 
 def tile_moe_bdx_mlp_silu_kernel(tc, dy_words, dy_scales, a, w2, w1, gate, offs, pos1, pos2, pos3, out):
@@ -88,8 +89,8 @@ def tile_moe_bdx_mlp_silu_kernel(tc, dy_words, dy_scales, a, w2, w1, gate, offs,
 
         def load_w2(e, o):
             if o == 0:
-                w2_room[e] = keep.tile([P, PASSES * PACK * H], F32, name=f"w2_raw{e}", tag=f"room{e % ROOMS}", align_bytes=64)
-            w2_raw[e, o] = w2_room[e][:, PACK * H * o : PACK * H * (o + 1)].rearrange("p (j i) -> p j i", j=PACK)
+                w2_room[e] = keep.tile([P, PAD + PASSES * PACK * H], F32, name=f"w2_raw{e}", tag=f"room{e % ROOMS}", align_bytes=64)
+            w2_raw[e, o] = w2_room[e][:, PAD + PACK * H * o : PAD + PACK * H * (o + 1)].rearrange("p (j i) -> p j i", j=PACK)
             nc.sync.dma_start(out=w2_raw[e, o], in_=w2[e, 512 * o : 512 * (o + 1), :].rearrange("(p j) i -> p j i", j=PACK))
 
         nc.sync.dma_start(offs_t[:], offs)
@@ -130,6 +131,13 @@ def tile_moe_bdx_mlp_silu_kernel(tc, dy_words, dy_scales, a, w2, w1, gate, offs,
         def vector_cast(dst, raw):
             interleave(nc.vector.tensor_copy, VECTOR_RUN, dst, raw)
 
+        def gpsimd_cast(dst, raw):
+            nc.gpsimd.tensor_scalar(
+                out=dst.rearrange("p (c j) -> p c j", j=PACK), in0=raw.rearrange("p j c -> p c j"), scalar1=1.0, scalar2=0.0, op0=ALU.mult, op1=ALU.add
+            )
+
+        casts = {"scalar": scalar_cast, "vector": vector_cast, "gpsimd": gpsimd_cast}
+
         slope = [shared[:, 2 * H * e : 2 * H * (e + 1)].rearrange("p (h i) -> p h i", h=2) for e in range(HEAD)]
         slope = slope + [keep.tile([P, 2, H], F32, name=f"slope{e}", tag=f"q{e}", align_bytes=64)[:] for e in range(HEAD, E)]
         silu = [keep.tile([P, 2, H], F32, name="silu0", tag="s5", align_bytes=64)[:]] + slope[1:]
@@ -157,22 +165,37 @@ def tile_moe_bdx_mlp_silu_kernel(tc, dy_words, dy_scales, a, w2, w1, gate, offs,
         def make_slope(e):
             nc.vector.scalar_tensor_tensor(out=slope[e], in0=silu[e], scalar=1.0, in1=sigmoid[e][:], op0=ALU.subtract, op1=ALU.mult)
 
+        w2_staged = {}
+
+        def cast_w2(e, o):
+            if e == 0:
+                staged = ring.tile([P, PACK * H], BF16, name="w2_staged", tag="w2_staged", bufs=3, align_bytes=64)[:]
+            elif o == 1:
+                first = 2 * GPSIMD_COLS if e in GPSIMD_EXPERTS else 0
+                staged = w2_room[e][:, first : first + 2 * H].bitcast(BF16)
+            elif e == 1:
+                staged = ring.tile([P, PACK * H], BF16, name="w2_staged", tag="w2_staged", bufs=3, align_bytes=64)[:]
+            else:
+                first = 2 * (H - VECTOR_COLS[e]) + (2 * GPSIMD_COLS if e - 1 in GPSIMD_EXPERTS else 0)
+                staged = w2_room[e - 1][:, first : first + 2 * H].bitcast(BF16)
+            w2_staged[e, o] = staged
+            first = 0
+            for engine, count in w2_shares(e, o):
+                if count > 0:
+                    casts[engine](staged[:, PACK * first : PACK * (first + count)], w2_raw[e, o][:, :, first : first + count])
+                first = first + count
+
         def quantize_w2(e, o):
-            staged = ring.tile([P, PACK * H], BF16, name="w2_staged", tag="w2_staged", bufs=3, align_bytes=64)
-            cut = H - w2_vector_cols(e, o)
-            first = HELD if (o == 1 and e > 0) else 0
-            if first > 0:
-                scalar_cast(staged[:, : PACK * first], w2_raw[e, o][:, :, :first])
-            if cut > 0:
-                scalar_cast(staged[:, PACK * first : PACK * cut], w2_raw[e, o][:, :, first:cut])
-            if cut < H:
-                vector_cast(staged[:, PACK * cut :], w2_raw[e, o][:, :, cut:])
             w2_codes[e, o] = ring.tile([P, H], U32, name="w2_codes", tag="w2_codes", bufs=4, align_bytes=64)
             w2_scales[e, o] = ring.tile([P, H], U8, name="w2_scales", tag="w2_scales", bufs=4, align_bytes=64)
-            nc.vector.quantize_mx(out=w2_codes[e, o][:].bitcast(FP8X4), scales=w2_scales[e, o][:], in_=staged[:])
+            nc.vector.quantize_mx(out=w2_codes[e, o][:].bitcast(FP8X4), scales=w2_scales[e, o][:], in_=w2_staged[e, o])
+
+        def turned_banks(e):
+            pair = (6 + e % 2, 6 + e % 2) if e + 1 < E else (7, SECOND_BANK)
+            return [banks[b][:].rearrange("p (h u r) -> p h u r", h=2, u=2) for b in pair]
 
         def first_product(e):
-            turned = banks[6 + e % 2][:].rearrange("p (h u r) -> p h u r", h=2, u=2)
+            turned = turned_banks(e)
             for h in range(2):
                 b = 2 * e + h
                 cols = slice(P * b, P * (b + 1))
@@ -193,18 +216,20 @@ def tile_moe_bdx_mlp_silu_kernel(tc, dy_words, dy_scales, a, w2, w1, gate, offs,
                 )
                 pairs = da_rows[:].bitcast(F32)
                 for u in range(2):
-                    nc.tensor.transpose(turned[:, h, u, :], pairs[:, u : H // 2 : 2], ident[:])
+                    nc.tensor.transpose(turned[h][:, h, u, :], pairs[:, u : H // 2 : 2], ident[:])
 
         def quantize_da(e):
-            turned = banks[6 + e % 2][:].rearrange("p (h u r) -> p h u r", h=2, u=2)
+            turned = turned_banks(e)
             if e + 1 < E:
-                staged = w2_room[e + 1][:, (PACK - 1) * H + HELD : PACK * H + HELD].bitcast(BF16)
+                staged = w2_room[e + 1][:, PAD + (PACK - 1) * H + HELD : PAD + PACK * H + HELD].bitcast(BF16)
             else:
                 staged = keep.tile([P, PACK * C], BF16, name="last_da", tag="q5x", align_bytes=64)[:]
-            nc.scalar.copy(out=staged.bitcast(F32).rearrange("p (h r u) -> p h r u", h=2, u=2), in_=turned.rearrange("p h u r -> p h r u"))
             da_codes[e] = keep.tile([P, C], U32, name=f"da_codes{e}", align_bytes=64)
             da_scales[e] = keep.tile([P, C], U8, name=f"da_scales{e}", align_bytes=64)
-            nc.vector.quantize_mx(out=da_codes[e][:].bitcast(FP8X4), scales=da_scales[e][:], in_=staged)
+            for lo, hi in ((0, 1), (1, 2)) if e + 1 == E else ((0, 2),):
+                part = staged[:, PACK * P * lo : PACK * P * hi]
+                nc.scalar.copy(out=part.bitcast(F32).rearrange("p (h r u) -> p h r u", h=hi - lo, u=2), in_=turned[lo][:, lo:hi].rearrange("p h u r -> p h r u"))
+                nc.vector.quantize_mx(out=da_codes[e][:, P * lo : P * hi].bitcast(FP8X4), scales=da_scales[e][:, P * lo : P * hi], in_=part)
 
         for e in range(HEAD):
             turn_a(e)
@@ -214,8 +239,10 @@ def tile_moe_bdx_mlp_silu_kernel(tc, dy_words, dy_scales, a, w2, w1, gate, offs,
         make_silu(1)
         make_slope(0)
         turn_a(E - 1)
+        cast_w2(0, 0)
         quantize_w2(0, 0)
         make_silu(2)
+        cast_w2(0, 1)
         quantize_w2(0, 1)
         make_silu(3)
         nc.tensor.transpose(banks[6][:, 0:P], gate_rows[:], ident[:])
@@ -223,8 +250,11 @@ def tile_moe_bdx_mlp_silu_kernel(tc, dy_words, dy_scales, a, w2, w1, gate, offs,
         for e in range(E):
             if e > 0:
                 quantize_w2(e, 0)
+                cast_w2(e, 1)
                 quantize_w2(e, 1)
                 quantize_da(e - 1)
+            if e + 1 < E:
+                cast_w2(e + 1, 0)
             first_product(e)
             if e == 1:
                 make_silu(E - 2)
@@ -236,121 +266,105 @@ def tile_moe_bdx_mlp_silu_kernel(tc, dy_words, dy_scales, a, w2, w1, gate, offs,
 
         w1_rows = w1.rearrange("e (p j) k -> p e j k", j=PACK)
         w1_raw = {}
-        for d in range(DOUBLES):
-            for e in range(E):
-                m = E * d + e
-                if m % 4 == 0:
-                    room = keep.tile([P, 4, PACK, WIDE], F32, name=f"w1_raw{m}", tag=f"room{(E + m // 4) % ROOMS}", align_bytes=64)
-                w1_raw[e, d] = room[:, m % 4]
-                if d + 1 < DOUBLES or e < E - 2:
-                    nc.sync.dma_start(out=w1_raw[e, d], in_=w1_rows[:, e, :, WIDE * d : WIDE * (d + 1)])
-        for s in range(2):
-            for e in (E - 2, E - 1):
-                first = WIDE * (DOUBLES - 1) + P * s
-                nc.sync.dma_start(out=w1_raw[e, DOUBLES - 1][:, :, P * s : P * (s + 1)], in_=w1_rows[:, e, :, first : first + P])
+        for kt in range(STRIPS):
+            w1_raw[kt] = keep.tile([P, E, PACK, P], F32, name=f"w1_raw{kt}", tag=f"room{(E + kt) % ROOMS}", align_bytes=64)[:]
+            cols = slice(P * kt, P * (kt + 1))
+            for e in range(E if kt == 0 else 2):
+                nc.sync.dma_start(out=w1_raw[kt][:, e], in_=w1_rows[:, e, :, cols])
+            for j in range(PACK if kt > 0 else 0):
+                nc.sync.dma_start(out=w1_raw[kt][:, 2:, j, :], in_=w1_rows[:, 2:, j, cols])
 
         def token_parts(parts):
             width = T // parts
             return [(slice(width * n, width * (n + 1)), slice(width * n // LIST_ROWS, width * (n + 1) // LIST_ROWS)) for n in range(parts)]
 
-        dx, first_part, two_parts, total, staged = {}, {}, {}, {}, {}
-        spare = [shared[:, T * n : T * (n + 1)] for n in range(9)]
+        dx, first_part, two_parts, total, early, late = {}, {}, {}, {}, {}, {}
+        spare = [shared[:, T * n : T * (n + 1)] for n in range(10)]
 
-        def cast_piece(cast, e, d, strips=(0, 1)):
-            if (e // 2, d) not in staged:
-                staged[e // 2, d] = ring.tile([P, 2, 2, PIECE], BF16, name="w2_staged", tag="w2_staged", bufs=3, align_bytes=64)
-            run = SCALAR_RUN if cast == "scalar" else VECTOR_RUN
-            lo, hi = strips[0], strips[-1] + 1
-            (nc.scalar.copy if cast == "scalar" else nc.vector.tensor_copy)(
-                out=staged[e // 2, d][:, lo:hi, e % 2].rearrange("p s (c i j) -> p s c j i", i=run, j=PACK),
-                in_=w1_raw[e, d][:, :, P * lo : P * hi].rearrange("p j (s c i) -> p s c j i", s=hi - lo, i=run),
+        def cast(engine, kt, first, last, dst, lo=0, hi=P):
+            run = SCALAR_RUN if engine == "scalar" else VECTOR_RUN
+            (nc.scalar.copy if engine == "scalar" else nc.vector.tensor_copy)(
+                out=dst[:, :, PACK * lo : PACK * hi].rearrange("p m (c i j) -> p m c j i", i=run, j=PACK),
+                in_=w1_raw[kt][:, first:last, :, lo:hi].rearrange("p m j (c i) -> p m c j i", i=run),
             )
 
-        def products(n, d, strips=(0, 1)):
-            lo, hi = strips[0], strips[-1] + 1
-            width = 2 * P * (hi - lo)
+        def products(kt, first, last, staged):
+            width = P * (last - first)
             codes = ring.tile([P, width], U32, name="w2_codes", tag="w2_codes", bufs=4, align_bytes=64)
             scales = ring.tile([P, width], U8, name="w2_scales", tag="w2_scales", bufs=4, align_bytes=64)
-            nc.vector.quantize_mx(out=codes[:].bitcast(FP8X4), scales=scales[:], in_=staged[n, d][:, lo:hi].rearrange("p s x c -> p (s x c)"))
-            for s in strips:
-                cols = [slice(P * (2 * (s - lo) + x), P * (2 * (s - lo) + x + 1)) for x in range(2)]
-                pair_product(2 * d + s, n, [codes[:, c] for c in cols], [scales[:, c] for c in cols])
-                if n + 1 == PAIRS:
-                    first_gather(2 * d + s, 2 if d + 1 == DOUBLES else 1)
-
-        def pair_product(kt, n, codes, scales):
-            bank = banks[(2 * (PAIRS * (kt // 2) + n) + kt % 2) % 4]
-            for x in range(2):
+            nc.vector.quantize_mx(out=codes[:].bitcast(FP8X4), scales=scales[:], in_=staged.rearrange("p m x -> p (m x)"))
+            for e in range(first, last):
+                bank = banks[(PAIRS * kt + e // 2) % 4]
+                cols = slice(P * (e - first), P * (e - first + 1))
                 nc.tensor.matmul_mx(
-                    out=bank[:, C * x : C * (x + 1)],
-                    lhsT=codes[x].bitcast(FP8X4),
-                    lhsT_scale=scales[x],
-                    rhs=da_codes[2 * n + x][:].bitcast(FP8X4),
-                    rhs_scale=da_scales[2 * n + x][:],
+                    out=bank[:, C * (e % 2) : C * (e % 2 + 1)],
+                    lhsT=codes[:, cols].bitcast(FP8X4),
+                    lhsT_scale=scales[:, cols],
+                    rhs=da_codes[e][:].bitcast(FP8X4),
+                    rhs_scale=da_scales[e][:],
                     start=True,
                     stop=True,
                 )
-            nc.scalar.copy(out=dx[kt][:, 2 * C * n : 2 * C * (n + 1)], in_=bank[:])
+                if e % 2 == 1:
+                    (nc.vector.tensor_copy if (kt, e // 2) in VECTOR_COPIES else nc.scalar.copy)(out=dx[kt][:, C * (e - 1) : C * (e + 1)], in_=bank[:])
 
         def first_gather(kt, parts):
             first_part[kt] = ring.tile([P, T], F32, name="first_part", tag="first_part", bufs=2, align_bytes=64)
             for cols, part in token_parts(parts):
                 nc.scalar.activation(first_part[kt][:, cols], dx[kt][:].indirect(pos_t[0][:, part]), ACT.Copy)
 
+        def flat(staged):
+            return staged.rearrange("p m x -> p (m x)").bitcast(F32)
+
+        def raw_piece(kt):
+            return w1_raw[kt][:, 2 if kt + 1 < STRIPS else 4].rearrange("p j c -> p (j c)")
+
         def second_gather(kt, parts):
-            two_parts[kt] = spare[STRIPS + kt % 2]
-            if kt % 2 == 1 and kt + 1 < STRIPS:
-                two_parts[kt] = staged[1, kt // 2 + 1][:, 0].rearrange("p x c -> p (x c)").bitcast(F32)
+            two_parts[kt] = w1_raw[1][:, 4].rearrange("p j c -> p (j c)")
             for cols, part in token_parts(parts):
                 nc.vector.tensor_tensor(two_parts[kt][:, cols], dx[kt][:].indirect(pos_t[1][:, part]), first_part[kt][:, cols], ALU.add)
 
         def third_gather(kt, parts):
-            total[kt] = spare[kt]
-            if kt % 2 == 1 and kt + 1 < STRIPS:
-                total[kt] = w1_raw[HOLD[kt // 2], kt // 2 + 1].rearrange("p j c -> p (j c)")[:, T:]
+            total = raw_piece(kt + 2) if kt < STRIPS - 2 else spare[4 + kt]
             rows = slice(P * kt, P * (kt + 1))
             for cols, part in token_parts(parts):
-                nc.vector.tensor_tensor(total[kt][:, cols], dx[kt][:].indirect(pos_t[2][:, part]), two_parts[kt][:, cols], ALU.add)
-                nc.sync.dma_start(out=out[rows, cols], in_=total[kt][:, cols])
+                nc.vector.tensor_tensor(total[:, cols], dx[kt][:].indirect(pos_t[2][:, part]), two_parts[kt][:, cols], ALU.add)
+                nc.sync.dma_start(out=out[rows, cols], in_=total[:, cols])
 
-        for d in range(DOUBLES):
-            for kt in (2 * d, 2 * d + 1):
-                dx[kt] = keep.tile([P, S], F32, name=f"dx{kt}", tag=f"a{kt % 4}", align_bytes=64)
-            if d == 0:
-                for e in range(3):
-                    cast_piece("scalar", e, d)
-                quantize_da(E - 1)
-                cast_piece("vector", 3, d)
-                products(0, d)
-                cast_piece("vector", 4, d)
-                products(1, d)
-                cast_piece("vector", 5, d)
-                products(2, d)
-                continue
-            cast_piece("vector", 0, d)
-            cast_piece("vector", 1, d)
-            second_gather(2 * d - 2, 1)
-            cast_piece("scalar", 2, d)
-            cast_piece("scalar", 3, d)
-            products(0, d)
-            third_gather(2 * d - 2, 1)
-            if d + 1 < DOUBLES:
-                cast_piece("vector", 4, d)
-                products(1, d)
-                cast_piece("vector", 5, d)
-                second_gather(2 * d - 1, 1)
-                products(2, d)
-                third_gather(2 * d - 1, 1)
+        quantize_da(E - 1)
+        for kt in range(STRIPS):
+            dx[kt] = keep.tile([P, S], F32, name=f"dx{kt}", tag=f"a{kt % 4}", align_bytes=64)
+            early[kt] = keep.tile([P, 4, PIECE], BF16, name=f"early{kt}", tag=f"s{kt}", align_bytes=64)[:]
+            late[kt] = ring.tile([P, 2, PIECE], BF16, name="late", tag="w2_staged", bufs=3, align_bytes=64)[:]
+            if kt == 0:
+                cast("scalar", kt, 0, 2, early[kt][:, :2])
+                products(kt, 0, 2, early[kt][:, :2])
+                cast("scalar", kt, 2, 4, early[kt][:, 2:])
+                products(kt, 2, 4, early[kt][:, 2:])
+                cast("vector", kt, 4, 6, late[kt])
+                products(kt, 4, 6, late[kt])
             else:
-                cast_piece("vector", 4, d, (0,))
-                cast_piece("vector", 5, d, (0,))
-                products(1, d)
-                products(2, d, (0,))
-                second_gather(2 * d - 1, 1)
-                cast_piece("vector", 4, d, (1,))
-                cast_piece("vector", 5, d, (1,))
-                products(2, d, (1,))
-                third_gather(2 * d - 1, 1)
-        for kt in (STRIPS - 2, STRIPS - 1):
-            second_gather(kt, 2)
-            third_gather(kt, 2)
+                cast("vector" if kt == 1 else "scalar", kt, 0, 2, late[kt])
+                products(kt, 0, 2, late[kt])
+                cast("vector", kt, 2, 4, early[kt][:, :2])
+                cast("vector", kt, 4, 6, early[kt][:, 2:])
+                if kt == 1:
+                    second_gather(0, 2)
+                elif kt + 1 < STRIPS:
+                    third_gather(kt - 2, 1)
+                products(kt, 2, 6, early[kt])
+                if kt + 1 == STRIPS:
+                    third_gather(kt - 2, 1)
+                if kt > 1:
+                    second_gather(kt - 1, 2 if kt + 1 == STRIPS else 1)
+            first_gather(kt, 2 if kt in (0, STRIPS - 1) else 1)
+        third_gather(STRIPS - 2, 2)
+        last = STRIPS - 1
+        middle_part, outer_parts, whole = spare[0], spare[1], spare[2]
+        for cols, part in token_parts(2):
+            nc.scalar.activation(middle_part[:, cols], dx[last][:].indirect(pos_t[1][:, part]), ACT.Copy)
+        for cols, part in token_parts(2):
+            nc.vector.tensor_tensor(outer_parts[:, cols], dx[last][:].indirect(pos_t[2][:, part]), first_part[last][:, cols], ALU.add)
+        for cols, part in token_parts(2):
+            nc.vector.tensor_tensor(whole[:, cols], outer_parts[:, cols], middle_part[:, cols], ALU.add)
+            nc.sync.dma_start(out=out[P * last : P * (last + 1), cols], in_=whole[:, cols])

@@ -41,6 +41,8 @@ LAST_COLS = (0, 0, 0, 0, 256, 256)
 HELD = 128
 SECOND_BANK = 3
 VECTOR_COPIES = ()
+CUT = (2, 2, 2, 2, 2, 2)
+EARLY_THIRD = True
 HEAD = 5
 
 
@@ -49,7 +51,8 @@ def w2_shares(e, o):
         return (("scalar", H),) if e == 0 else (("vector", VECTOR_COLS[e]), ("scalar", H - VECTOR_COLS[e]))
     if e == 0:
         return ("scalar", H // 2), ("vector", H // 2)
-    return ("scalar", HELD), ("scalar", H - HELD - LAST_COLS[e]), ("vector", LAST_COLS[e])
+    late = GPSIMD_COLS if e in GPSIMD_EXPERTS else 0
+    return ("scalar", HELD), ("scalar", H - HELD - LAST_COLS[e] - late), ("vector", LAST_COLS[e]), ("gpsimd", late)
 
 
 def tile_moe_bdx_mlp_silu_kernel(tc, dy_words, dy_scales, a, w2, w1, gate, offs, pos1, pos2, pos3, out):
@@ -269,10 +272,11 @@ def tile_moe_bdx_mlp_silu_kernel(tc, dy_words, dy_scales, a, w2, w1, gate, offs,
         for kt in range(STRIPS):
             w1_raw[kt] = keep.tile([P, E, PACK, P], F32, name=f"w1_raw{kt}", tag=f"room{(E + kt) % ROOMS}", align_bytes=64)[:]
             cols = slice(P * kt, P * (kt + 1))
-            for e in range(E if kt == 0 else 2):
+            cut = CUT[kt]
+            for e in range(E if kt in (0, 1, STRIPS - 1) else cut):
                 nc.sync.dma_start(out=w1_raw[kt][:, e], in_=w1_rows[:, e, :, cols])
-            for j in range(PACK if kt > 0 else 0):
-                nc.sync.dma_start(out=w1_raw[kt][:, 2:, j, :], in_=w1_rows[:, 2:, j, cols])
+            for j in range(PACK if 1 < kt < STRIPS - 1 else 0):
+                nc.sync.dma_start(out=w1_raw[kt][:, cut:, j, :], in_=w1_rows[:, cut:, j, cols])
 
         def token_parts(parts):
             width = T // parts
@@ -305,8 +309,9 @@ def tile_moe_bdx_mlp_silu_kernel(tc, dy_words, dy_scales, a, w2, w1, gate, offs,
                     start=True,
                     stop=True,
                 )
-                if e % 2 == 1:
-                    (nc.vector.tensor_copy if (kt, e // 2) in VECTOR_COPIES else nc.scalar.copy)(out=dx[kt][:, C * (e - 1) : C * (e + 1)], in_=bank[:])
+                made.add((kt, e))
+                if (kt, e ^ 1) in made:
+                    (nc.vector.tensor_copy if (kt, e // 2) in VECTOR_COPIES else nc.scalar.copy)(out=dx[kt][:, 2 * C * (e // 2) : 2 * C * (e // 2 + 1)], in_=bank[:])
 
         def first_gather(kt, parts):
             first_part[kt] = ring.tile([P, T], F32, name="first_part", tag="first_part", bufs=2, align_bytes=64)
@@ -317,46 +322,45 @@ def tile_moe_bdx_mlp_silu_kernel(tc, dy_words, dy_scales, a, w2, w1, gate, offs,
             return staged.rearrange("p m x -> p (m x)").bitcast(F32)
 
         def raw_piece(kt):
-            return w1_raw[kt][:, 2 if kt + 1 < STRIPS else 4].rearrange("p j c -> p (j c)")
+            return w1_raw[kt][:, CUT[kt]].rearrange("p j c -> p (j c)")
 
         def second_gather(kt, parts):
-            two_parts[kt] = w1_raw[1][:, 4].rearrange("p j c -> p (j c)")
+            two_parts[kt] = w1_raw[kt + 1 if kt in (0, STRIPS - 2) else (2 if EARLY_THIRD else 1)][:, 4].rearrange("p j c -> p (j c)")
             for cols, part in token_parts(parts):
                 nc.vector.tensor_tensor(two_parts[kt][:, cols], dx[kt][:].indirect(pos_t[1][:, part]), first_part[kt][:, cols], ALU.add)
 
         def third_gather(kt, parts):
-            total = raw_piece(kt + 2) if kt < STRIPS - 2 else spare[4 + kt]
+            total = raw_piece(kt + 2) if (0 if EARLY_THIRD else -1) < kt < STRIPS - 2 else spare[4 + kt]
             rows = slice(P * kt, P * (kt + 1))
             for cols, part in token_parts(parts):
                 nc.vector.tensor_tensor(total[:, cols], dx[kt][:].indirect(pos_t[2][:, part]), two_parts[kt][:, cols], ALU.add)
                 nc.sync.dma_start(out=out[rows, cols], in_=total[:, cols])
 
+        made = set()
         quantize_da(E - 1)
         for kt in range(STRIPS):
             dx[kt] = keep.tile([P, S], F32, name=f"dx{kt}", tag=f"a{kt % 4}", align_bytes=64)
             early[kt] = keep.tile([P, 4, PIECE], BF16, name=f"early{kt}", tag=f"s{kt}", align_bytes=64)[:]
             late[kt] = ring.tile([P, 2, PIECE], BF16, name="late", tag="w2_staged", bufs=3, align_bytes=64)[:]
+            cast("vector" if kt == 1 else "scalar", kt, 0, 2, early[kt][:, :2])
             if kt == 0:
-                cast("scalar", kt, 0, 2, early[kt][:, :2])
                 products(kt, 0, 2, early[kt][:, :2])
-                cast("scalar", kt, 2, 4, early[kt][:, 2:])
+            cast("scalar" if kt == 0 else "vector", kt, 2, 4, early[kt][:, 2:])
+            if kt == 0:
                 products(kt, 2, 4, early[kt][:, 2:])
-                cast("vector", kt, 4, 6, late[kt])
-                products(kt, 4, 6, late[kt])
-            else:
-                cast("vector" if kt == 1 else "scalar", kt, 0, 2, late[kt])
-                products(kt, 0, 2, late[kt])
-                cast("vector", kt, 2, 4, early[kt][:, :2])
-                cast("vector", kt, 4, 6, early[kt][:, 2:])
-                if kt == 1:
-                    second_gather(0, 2)
-                elif kt + 1 < STRIPS:
-                    third_gather(kt - 2, 1)
-                products(kt, 2, 6, early[kt])
-                if kt + 1 == STRIPS:
-                    third_gather(kt - 2, 1)
-                if kt > 1:
-                    second_gather(kt - 1, 2 if kt + 1 == STRIPS else 1)
+            if kt + 1 == STRIPS:
+                products(kt, 0, 4, early[kt])
+                third_gather(kt - 2, 1)
+            cast("vector", kt, 4, 6, late[kt])
+            if 2 < kt < STRIPS - 1:
+                third_gather(kt - 2, 1)
+            if 0 < kt < STRIPS - 1:
+                products(kt, 0, 4, early[kt])
+            products(kt, 4, 6, late[kt])
+            if kt > 0:
+                second_gather(kt - 1, 2 if kt in (1, STRIPS - 1) else 1)
+            if kt == 1:
+                third_gather(0, 2)
             first_gather(kt, 2 if kt in (0, STRIPS - 1) else 1)
         third_gather(STRIPS - 2, 2)
         last = STRIPS - 1

@@ -31,17 +31,17 @@ GATHER = 768
 SCALAR_RUN = 2
 VECTOR_RUN = 4
 ROOMS = 5
-VECTOR_COLS = (0, 384, 384, 384, 128, 128)
+VECTOR_COLS = (0, 384, 384, 384, 384, 256)
 GPSIMD_COLS = 160
 GPSIMD_EXPERTS = ()
 PAD = 2 * H
 SCALAR_EXTRA = 0
 VECTOR_ALONE = ()
-LAST_COLS = (0, 0, 0, 0, 256, 256)
+LAST_COLS = (0, 0, 0, 0, 0, 256)
 HELD = 128
 SECOND_BANK = 3
 VECTOR_COPIES = ()
-CUT = (2, 2, 2, 2, 2, 2)
+CUT = (2, 2, 2, 3, 3, 2)
 EARLY_THIRD = True
 HEAD = 5
 
@@ -268,15 +268,35 @@ def tile_moe_bdx_mlp_silu_kernel(tc, dy_words, dy_scales, a, w2, w1, gate, offs,
                 make_slope(e + 1)
 
         w1_rows = w1.rearrange("e (p j) k -> p e j k", j=PACK)
-        w1_raw = {}
-        for kt in range(STRIPS):
-            w1_raw[kt] = keep.tile([P, E, PACK, P], F32, name=f"w1_raw{kt}", tag=f"room{(E + kt) % ROOMS}", align_bytes=64)[:]
+        pair_raw, rows_of = {}, {}
+
+        def room(n, name, experts, width):
+            return keep.tile([P, experts, PACK, width], F32, name=name, tag=f"room{n % ROOMS}", align_bytes=64)[:]
+
+        def load_experts(dst, first, cols):
+            for x in range(dst.shape[1]):
+                nc.sync.dma_start(out=dst[:, x], in_=w1_rows[:, first + x, :, cols])
+
+        def load_rows(dst, first, cols):
+            for j in range(PACK):
+                nc.sync.dma_start(out=dst[:, :, j, :], in_=w1_rows[:, first : first + dst.shape[1], j, cols])
+
+        wide = room(1, "w1_a", 4, 2 * P), room(2, "w1_b", 2, 2 * P)
+        load_experts(wide[0], 0, slice(0, 2 * P))
+        load_experts(wide[1], 4, slice(0, 2 * P))
+        for n, pair in enumerate((wide[0][:, :2], wide[0][:, 2:], wide[1])):
+            for kt in range(2):
+                pair_raw[kt, n] = pair[:, :, :, P * kt : P * (kt + 1)]
+            rows_of[1, n] = pair[:, 0, :2, :].rearrange("p j c -> p (j c)")
+        for kt in range(2, STRIPS):
+            narrow = room(kt + 1, f"w1_{kt}", E, P)
             cols = slice(P * kt, P * (kt + 1))
-            cut = CUT[kt]
-            for e in range(E if kt in (0, 1, STRIPS - 1) else cut):
-                nc.sync.dma_start(out=w1_raw[kt][:, e], in_=w1_rows[:, e, :, cols])
-            for j in range(PACK if 1 < kt < STRIPS - 1 else 0):
-                nc.sync.dma_start(out=w1_raw[kt][:, cut:, j, :], in_=w1_rows[:, cut:, j, cols])
+            load_experts(narrow[:, : 2 if kt + 1 < STRIPS else E], 0, cols)
+            if kt + 1 < STRIPS:
+                load_rows(narrow[:, 2:], 2, cols)
+            for n in range(PAIRS):
+                pair_raw[kt, n] = narrow[:, 2 * n : 2 * n + 2]
+                rows_of[kt, n] = narrow[:, 2 * n].rearrange("p j c -> p (j c)")
 
         def token_parts(parts):
             width = T // parts
@@ -289,7 +309,7 @@ def tile_moe_bdx_mlp_silu_kernel(tc, dy_words, dy_scales, a, w2, w1, gate, offs,
             run = SCALAR_RUN if engine == "scalar" else VECTOR_RUN
             (nc.scalar.copy if engine == "scalar" else nc.vector.tensor_copy)(
                 out=dst[:, :, PACK * lo : PACK * hi].rearrange("p m (c i j) -> p m c j i", i=run, j=PACK),
-                in_=w1_raw[kt][:, first:last, :, lo:hi].rearrange("p m j (c i) -> p m c j i", i=run),
+                in_=pair_raw[kt, first // 2][:, :, :, lo:hi].rearrange("p m j (c i) -> p m c j i", i=run),
             )
 
         def products(kt, first, last, staged):
@@ -322,10 +342,10 @@ def tile_moe_bdx_mlp_silu_kernel(tc, dy_words, dy_scales, a, w2, w1, gate, offs,
             return staged.rearrange("p m x -> p (m x)").bitcast(F32)
 
         def raw_piece(kt):
-            return w1_raw[kt][:, CUT[kt]].rearrange("p j c -> p (j c)")
+            return rows_of[kt, 1]
 
         def second_gather(kt, parts):
-            two_parts[kt] = w1_raw[kt + 1 if kt in (0, STRIPS - 2) else (2 if EARLY_THIRD else 1)][:, 4].rearrange("p j c -> p (j c)")
+            two_parts[kt] = rows_of[kt + 1, 2] if kt in (0, STRIPS - 2) else rows_of[2, 2]
             for cols, part in token_parts(parts):
                 nc.vector.tensor_tensor(two_parts[kt][:, cols], dx[kt][:].indirect(pos_t[1][:, part]), first_part[kt][:, cols], ALU.add)
 
@@ -337,15 +357,22 @@ def tile_moe_bdx_mlp_silu_kernel(tc, dy_words, dy_scales, a, w2, w1, gate, offs,
                 nc.sync.dma_start(out=out[rows, cols], in_=total[:, cols])
 
         made = set()
+        arena = shared[:, 5 * T : 8 * T].bitcast(BF16)
+        early[0] = keep.tile([P, 4, PIECE], BF16, name="early0", tag="s0", align_bytes=64)[:]
+        early[1] = arena[:, : 4 * PIECE].rearrange("p (m x) -> p m x", m=4)
+        for kt in range(2):
+            late[kt] = arena[:, (3 + kt) * PIECE : (5 + kt) * PIECE].rearrange("p (m x) -> p m x", m=2)
+            cast("scalar", kt, 0, 2, early[kt][:, :2])
         quantize_da(E - 1)
         for kt in range(STRIPS):
             dx[kt] = keep.tile([P, S], F32, name=f"dx{kt}", tag=f"a{kt % 4}", align_bytes=64)
-            early[kt] = keep.tile([P, 4, PIECE], BF16, name=f"early{kt}", tag=f"s{kt}", align_bytes=64)[:]
-            late[kt] = ring.tile([P, 2, PIECE], BF16, name="late", tag="w2_staged", bufs=3, align_bytes=64)[:]
-            cast("vector" if kt == 1 else "scalar", kt, 0, 2, early[kt][:, :2])
+            if kt >= 2:
+                early[kt] = keep.tile([P, 4, PIECE], BF16, name=f"early{kt}", tag=f"s{kt}", align_bytes=64)[:]
+                late[kt] = ring.tile([P, 2, PIECE], BF16, name="late", tag="w2_staged", bufs=3, align_bytes=64)[:]
+                cast("scalar", kt, 0, 2, early[kt][:, :2])
             if kt == 0:
                 products(kt, 0, 2, early[kt][:, :2])
-            cast("scalar" if kt == 0 else "vector", kt, 2, 4, early[kt][:, 2:])
+            cast("vector", kt, 2, 4, early[kt][:, 2:])
             if kt == 0:
                 products(kt, 2, 4, early[kt][:, 2:])
             if kt + 1 == STRIPS:

@@ -98,8 +98,7 @@ def tile_moe_bdx_mlp_silu_kernel(tc, dy_words, dy_scales, a, w2, w1, gate, offs,
 
         nc.sync.dma_start(offs_t[:], offs)
         nc.sync.dma_start(out=words[:, T : 2 * T], in_=words_i32[:, 0, :])
-        load_a(a_of[0][:, :, :P], 0)
-        load_a(a_of[0][:, :, P:], P)
+        load_a(a_of[0], 0)
         load_a(a_of[1], C)
         nc.sync.dma_start(out=words[:, :T], in_=words_i32[:, 1, :])
         load_a(a_of[2], 2 * C)
@@ -112,8 +111,6 @@ def tile_moe_bdx_mlp_silu_kernel(tc, dy_words, dy_scales, a, w2, w1, gate, offs,
             load_w2(e, 1)
             if e == 0:
                 load_a(a_of[5], 5 * C)
-            if e >= E - 3:
-                nc.sync.dma_start(pos_t[e - (E - 3)][:], (pos1, pos2, pos3)[e - (E - 3)])
 
         g_words = keep.tile([P, PASSES, S], U32, name="g_words", align_bytes=64)
         g_scales = keep.tile([P, S], U8, name="g_scales", align_bytes=64)
@@ -284,6 +281,8 @@ def tile_moe_bdx_mlp_silu_kernel(tc, dy_words, dy_scales, a, w2, w1, gate, offs,
         wide = room(1, "w1_a", 4, 2 * P), room(2, "w1_b", 2, 2 * P)
         load_experts(wide[0], 0, slice(0, 2 * P))
         load_experts(wide[1], 4, slice(0, 2 * P))
+        for tile, pos in zip(pos_t, (pos1, pos2, pos3)):
+            nc.sync.dma_start(tile[:], pos)
         for n, pair in enumerate((wide[0][:, :2], wide[0][:, 2:], wide[1])):
             for kt in range(2):
                 pair_raw[kt, n] = pair[:, :, :, P * kt : P * (kt + 1)]

from contextlib import ExitStack

import concourse.mybir as mybir
from concourse.masks import make_identity

K, T, E, C, H, N = 768, 512, 6, 256, 512, 1024
S = E * C
FLOPS = 2 * S * (N * H + H * K)
BYTES = N * T + N * T // 32 + 4 * (H * S + E * N * H + E * H * K + S + K * T) + 2 * 128 * (S + 3 * T) // 16

F32 = mybir.dt.float32
BF16 = mybir.dt.bfloat16
I32 = mybir.dt.int32
U32 = mybir.dt.uint32
U16 = mybir.dt.uint16
U8 = mybir.dt.uint8
FP8X4 = mybir.dt.float8_e4m3fn_x4
ACT = mybir.ActivationFunctionType
ALU = mybir.AluOpType

P = 128
PACK = 4
PASSES = N // (P * PACK)
STRIPS = K // P
BLOCKS = S // P
PAIRS = E // 2
PIECE = PACK * P
LIST_ROWS = 16
WINDOW = 1024
GATHER = 768
SCALAR_RUN = 2
VECTOR_RUN = 4
ROOMS = 5
VECTOR_COLS = (0, 384, 384, 384, 384, 256)
GPSIMD_COLS = 160
GPSIMD_EXPERTS = ()
PAD = 2 * H
SCALAR_EXTRA = 0
VECTOR_ALONE = ()
LAST_COLS = (0, 0, 0, 0, 0, 256)
HELD = 128
SECOND_BANK = 3
VECTOR_COPIES = ()
CUT = (2, 2, 2, 3, 3, 2)
EARLY_THIRD = True
HEAD = 5


def w2_shares(e, o):
    if o == 0:
        return (("scalar", H),) if e == 0 else (("vector", VECTOR_COLS[e]), ("scalar", H - VECTOR_COLS[e]))
    if e == 0:
        return ("scalar", H // 2), ("vector", H // 2)
    late = GPSIMD_COLS if e in GPSIMD_EXPERTS else 0
    return ("scalar", HELD), ("scalar", H - HELD - LAST_COLS[e] - late), ("vector", LAST_COLS[e]), ("gpsimd", late)


def tile_moe_bdx_mlp_silu_kernel(tc, dy_words, dy_scales, a, w2, w1, gate, offs, pos1, pos2, pos3, out):
    nc = tc.nc
    with ExitStack() as ctx:
        lists = ctx.enter_context(tc.tile_pool(name="lists", bufs=1))
        keep = ctx.enter_context(tc.tile_pool(name="keep", bufs=1))
        ring = ctx.enter_context(tc.tile_pool(name="ring", bufs=2))
        psum = ctx.enter_context(tc.psum_pool(name="psum", bufs=1))

        banks = [psum.tile([P, 512], F32, name=f"bank{b}") for b in range(8)]

        offs_t = lists.tile([P, S // LIST_ROWS], U16, name="offs_t")
        pos_t = [lists.tile([P, T // LIST_ROWS], U16, name=f"pos_t{r}") for r in range(3)]
        words = keep.tile([P, T + WINDOW], I32, name="words", align_bytes=64)
        plane = keep.tile([P, WINDOW // 4], I32, name="plane", align_bytes=64)
        ident = keep.tile([P, P], F32, name="ident")
        gate_rows = keep.tile([P, P], F32, name="gate_rows")
        neg_gate = keep.tile([P, BLOCKS], F32, name="neg_gate")

        make_identity(nc, ident[:])
        nc.gpsimd.memset(gate_rows[:], 0.0)
        nc.gpsimd.dma_start(out=gate_rows[0:BLOCKS, :], in_=gate[0, :].rearrange("(b c) -> b c", c=P))
        nc.vector.memset(plane[:], 0)
        nc.vector.memset(words[:, PASSES * T :], 0)

        a_rows = a.rearrange("(t p) s -> p t s", p=P)
        words_i32 = dy_words.rearrange("o p t d -> p o (t d)").bitcast(I32)
        scales_i32 = dy_scales.bitcast(I32)
        shared = keep.tile([P, HEAD * 2 * H], F32, name="shared", align_bytes=64)
        a_of = {e: keep.tile([P, PACK, C], F32, name=f"a{e}", tag=f"a{e}", align_bytes=64)[:] for e in (0, 1, 2, 3, 5)}
        a_of[4] = shared[:, 2 * H - P : 2 * H - P + PACK * 2 * H].rearrange("p (t s) -> p t s", t=PACK)[:, :, :C]
        w2_raw, w2_room = {}, {}

        def load_a(dst, first):
            nc.sync.dma_start(dst, a_rows[:, :, first : first + dst.shape[2]])

        def load_w2(e, o):
            if o == 0:
                w2_room[e] = keep.tile([P, PAD + PASSES * PACK * H], F32, name=f"w2_raw{e}", tag=f"room{e % ROOMS}", align_bytes=64)
            w2_raw[e, o] = w2_room[e][:, PAD + PACK * H * o : PAD + PACK * H * (o + 1)].rearrange("p (j i) -> p j i", j=PACK)
            nc.sync.dma_start(out=w2_raw[e, o], in_=w2[e, 512 * o : 512 * (o + 1), :].rearrange("(p j) i -> p j i", j=PACK))

        nc.sync.dma_start(offs_t[:], offs)
        nc.sync.dma_start(out=words[:, T : 2 * T], in_=words_i32[:, 0, :])
        load_a(a_of[0], 0)
        load_a(a_of[1], C)
        nc.sync.dma_start(out=words[:, :T], in_=words_i32[:, 1, :])
        load_a(a_of[2], 2 * C)
        load_a(a_of[3], 3 * C)
        for q in range(4):
            nc.sync.dma_start(out=plane[32 * q : 32 * q + 4 * PASSES, : T // 4], in_=scales_i32[:, 4 * q : 4 * q + 4, :])
        load_a(a_of[4], 4 * C)
        for e in range(E):
            load_w2(e, 0)
            load_w2(e, 1)
            if e == 0:
                load_a(a_of[5], 5 * C)

        g_words = keep.tile([P, PASSES, S], U32, name="g_words", align_bytes=64)
        g_scales = keep.tile([P, S], U8, name="g_scales", align_bytes=64)
        for o in range(PASSES):
            for first in range(0, S, GATHER):
                slots = offs_t[:, first // LIST_ROWS : (first + GATHER) // LIST_ROWS]
                nc.vector.tensor_copy(g_words[:, o, first : first + GATHER], words[:, T * (1 - o) : T * (1 - o) + WINDOW].bitcast(U32).indirect(slots))
        for first in range(0, S, GATHER):
            slots = offs_t[:, first // LIST_ROWS : (first + GATHER) // LIST_ROWS]
            nc.vector.tensor_copy(g_scales[:, first : first + GATHER], plane[:].bitcast(U8).indirect(slots))

        def interleave(copy, run, dst, raw):
            copy(out=dst.rearrange("p (c i j) -> p c j i", i=run, j=PACK), in_=raw.rearrange("p j (c i) -> p c j i", i=run))

        def scalar_cast(dst, raw):
            interleave(nc.scalar.copy, SCALAR_RUN, dst, raw)

        def vector_cast(dst, raw):
            interleave(nc.vector.tensor_copy, VECTOR_RUN, dst, raw)

        def gpsimd_cast(dst, raw):
            nc.gpsimd.tensor_scalar(
                out=dst.rearrange("p (c j) -> p c j", j=PACK), in0=raw.rearrange("p j c -> p c j"), scalar1=1.0, scalar2=0.0, op0=ALU.mult, op1=ALU.add
            )

        casts = {"scalar": scalar_cast, "vector": vector_cast, "gpsimd": gpsimd_cast}

        slope = [shared[:, 2 * H * e : 2 * H * (e + 1)].rearrange("p (h i) -> p h i", h=2) for e in range(HEAD)]
        slope = slope + [keep.tile([P, 2, H], F32, name=f"slope{e}", tag=f"q{e}", align_bytes=64)[:] for e in range(HEAD, E)]
        silu = [keep.tile([P, 2, H], F32, name="silu0", tag="s5", align_bytes=64)[:]] + slope[1:]
        sigmoid = [keep.tile([P, 2, H], F32, name=f"sigmoid{e}", tag=f"s{e}", align_bytes=64) for e in range(E)]
        w2_codes, w2_scales, da_codes, da_scales = {}, {}, {}, {}

        def a_banks(e):
            return [banks[(2 * e + h) % 8] for h in range(2)]

        def turn_a(e):
            for h in range(2):
                for t in range(PACK):
                    nc.tensor.transpose(a_banks(e)[h][:, P * t : P * (t + 1)], a_of[e][:, t, P * h : P * (h + 1)], ident[:])

        def make_silu(e):
            for h in range(2):
                nc.scalar.activation(out=silu[e][:, h, :], in_=a_banks(e)[h][:], func=ACT.Silu, scale=-1.0)

        def make_sigmoid(e):
            for h in range(2):
                nc.scalar.activation(out=sigmoid[e][:, h, :], in_=a_banks(e)[h][:], func=ACT.Tanh, scale=0.5)
            flat = sigmoid[e][:].rearrange("p h i -> p (h i)")
            (nc.gpsimd if e < HEAD else nc.vector).tensor_scalar(out=flat, in0=flat, scalar1=0.5, scalar2=0.5, op0=ALU.mult, op1=ALU.add)

        def make_slope(e):
            nc.vector.scalar_tensor_tensor(out=slope[e], in0=silu[e], scalar=1.0, in1=sigmoid[e][:], op0=ALU.subtract, op1=ALU.mult)

        w2_staged = {}

        def cast_w2(e, o):
            if e == 0:
                staged = ring.tile([P, PACK * H], BF16, name="w2_staged", tag="w2_staged", bufs=3, align_bytes=64)[:]
            elif o == 1:
                first = 2 * GPSIMD_COLS if e in GPSIMD_EXPERTS else 0
                staged = w2_room[e][:, first : first + 2 * H].bitcast(BF16)
            elif e == 1:
                staged = ring.tile([P, PACK * H], BF16, name="w2_staged", tag="w2_staged", bufs=3, align_bytes=64)[:]
            else:
                first = 2 * (H - VECTOR_COLS[e]) + (2 * GPSIMD_COLS if e - 1 in GPSIMD_EXPERTS else 0)
                staged = w2_room[e - 1][:, first : first + 2 * H].bitcast(BF16)
            w2_staged[e, o] = staged
            first = 0
            for engine, count in w2_shares(e, o):
                if count > 0:
                    casts[engine](staged[:, PACK * first : PACK * (first + count)], w2_raw[e, o][:, :, first : first + count])
                first = first + count

        def quantize_w2(e, o):
            w2_codes[e, o] = ring.tile([P, H], U32, name="w2_codes", tag="w2_codes", bufs=4, align_bytes=64)
            w2_scales[e, o] = ring.tile([P, H], U8, name="w2_scales", tag="w2_scales", bufs=4, align_bytes=64)
            nc.vector.quantize_mx(out=w2_codes[e, o][:].bitcast(FP8X4), scales=w2_scales[e, o][:], in_=w2_staged[e, o])

        def turned_banks(e):
            pair = (6 + e % 2, 6 + e % 2) if e + 1 < E else (7, SECOND_BANK)
            return [banks[b][:].rearrange("p (h u r) -> p h u r", h=2, u=2) for b in pair]

        def first_product(e):
            turned = turned_banks(e)
            for h in range(2):
                b = 2 * e + h
                cols = slice(P * b, P * (b + 1))
                acc = banks[4 + h]
                for o in range(PASSES):
                    nc.tensor.matmul_mx(
                        out=acc[:],
                        lhsT=g_words[:, o, cols].bitcast(FP8X4),
                        lhsT_scale=g_scales[4 * o : P, cols],
                        rhs=w2_codes[e, o][:].bitcast(FP8X4),
                        rhs_scale=w2_scales[e, o][:],
                        start=(o == 0),
                        stop=(o == PASSES - 1),
                    )
                da_rows = ring.tile([P, H], BF16, name="da_rows", tag="da_rows", bufs=3, align_bytes=64)
                nc.vector.scalar_tensor_tensor(
                    out=da_rows[:], in0=acc[:], scalar=neg_gate[:, b : b + 1], in1=slope[e][:, h, :], op0=ALU.mult, op1=ALU.mult
                )
                pairs = da_rows[:].bitcast(F32)
                for u in range(2):
                    nc.tensor.transpose(turned[h][:, h, u, :], pairs[:, u : H // 2 : 2], ident[:])

        def quantize_da(e):
            turned = turned_banks(e)
            if e + 1 < E:
                staged = w2_room[e + 1][:, PAD + (PACK - 1) * H + HELD : PAD + PACK * H + HELD].bitcast(BF16)
            else:
                staged = keep.tile([P, PACK * C], BF16, name="last_da", tag="q5x", align_bytes=64)[:]
            da_codes[e] = keep.tile([P, C], U32, name=f"da_codes{e}", align_bytes=64)
            da_scales[e] = keep.tile([P, C], U8, name=f"da_scales{e}", align_bytes=64)
            for lo, hi in ((0, 1), (1, 2)) if e + 1 == E else ((0, 2),):
                part = staged[:, PACK * P * lo : PACK * P * hi]
                nc.scalar.copy(out=part.bitcast(F32).rearrange("p (h r u) -> p h r u", h=hi - lo, u=2), in_=turned[lo][:, lo:hi].rearrange("p h u r -> p h r u"))
                nc.vector.quantize_mx(out=da_codes[e][:, P * lo : P * hi].bitcast(FP8X4), scales=da_scales[e][:, P * lo : P * hi], in_=part)

        for e in range(HEAD):
            turn_a(e)
            if e == 0:
                make_silu(e)
            make_sigmoid(e)
        make_silu(1)
        make_slope(0)
        turn_a(E - 1)
        cast_w2(0, 0)
        quantize_w2(0, 0)
        make_silu(2)
        cast_w2(0, 1)
        quantize_w2(0, 1)
        make_silu(3)
        nc.tensor.transpose(banks[6][:, 0:P], gate_rows[:], ident[:])
        nc.scalar.activation(out=neg_gate[:], in_=banks[6][:, 0:BLOCKS], func=ACT.Copy, scale=-1.0)
        for e in range(E):
            if e > 0:
                quantize_w2(e, 0)
                cast_w2(e, 1)
                quantize_w2(e, 1)
                quantize_da(e - 1)
            if e + 1 < E:
                cast_w2(e + 1, 0)
            first_product(e)
            if e == 1:
                make_silu(E - 2)
            if e == 2:
                make_sigmoid(E - 1)
                make_silu(E - 1)
            if e + 1 < E:
                make_slope(e + 1)

        w1_rows = w1.rearrange("e (p j) k -> p e j k", j=PACK)
        pair_raw, rows_of = {}, {}

        def room(n, name, experts, width):
            return keep.tile([P, experts, PACK, width], F32, name=name, tag=f"room{n % ROOMS}", align_bytes=64)[:]

        def load_experts(dst, first, cols):
            for x in range(dst.shape[1]):
                nc.sync.dma_start(out=dst[:, x], in_=w1_rows[:, first + x, :, cols])

        def load_rows(dst, first, cols):
            for j in range(PACK):
                nc.sync.dma_start(out=dst[:, :, j, :], in_=w1_rows[:, first : first + dst.shape[1], j, cols])

        wide = room(1, "w1_a", 4, 2 * P), room(2, "w1_b", 2, 2 * P)
        load_experts(wide[0], 0, slice(0, 2 * P))
        load_experts(wide[1], 4, slice(0, 2 * P))
        for tile, pos in zip(pos_t, (pos1, pos2, pos3)):
            nc.sync.dma_start(tile[:], pos)
        for n, pair in enumerate((wide[0][:, :2], wide[0][:, 2:], wide[1])):
            for kt in range(2):
                pair_raw[kt, n] = pair[:, :, :, P * kt : P * (kt + 1)]
            rows_of[1, n] = pair[:, 0, :2, :].rearrange("p j c -> p (j c)")
        for kt in range(2, STRIPS):
            narrow = room(kt + 1, f"w1_{kt}", E, P)
            cols = slice(P * kt, P * (kt + 1))
            load_experts(narrow[:, : 2 if kt + 1 < STRIPS else E], 0, cols)
            if kt + 1 < STRIPS:
                load_rows(narrow[:, 2:], 2, cols)
            for n in range(PAIRS):
                pair_raw[kt, n] = narrow[:, 2 * n : 2 * n + 2]
                rows_of[kt, n] = narrow[:, 2 * n].rearrange("p j c -> p (j c)")

        def token_parts(parts):
            width = T // parts
            return [(slice(width * n, width * (n + 1)), slice(width * n // LIST_ROWS, width * (n + 1) // LIST_ROWS)) for n in range(parts)]

        dx, first_part, two_parts, total, early, late = {}, {}, {}, {}, {}, {}
        spare = [shared[:, T * n : T * (n + 1)] for n in range(10)]

        def cast(engine, kt, first, last, dst, lo=0, hi=P):
            run = SCALAR_RUN if engine == "scalar" else VECTOR_RUN
            (nc.scalar.copy if engine == "scalar" else nc.vector.tensor_copy)(
                out=dst[:, :, PACK * lo : PACK * hi].rearrange("p m (c i j) -> p m c j i", i=run, j=PACK),
                in_=pair_raw[kt, first // 2][:, :, :, lo:hi].rearrange("p m j (c i) -> p m c j i", i=run),
            )

        def products(kt, first, last, staged):
            width = P * (last - first)
            codes = ring.tile([P, width], U32, name="w2_codes", tag="w2_codes", bufs=4, align_bytes=64)
            scales = ring.tile([P, width], U8, name="w2_scales", tag="w2_scales", bufs=4, align_bytes=64)
            nc.vector.quantize_mx(out=codes[:].bitcast(FP8X4), scales=scales[:], in_=staged.rearrange("p m x -> p (m x)"))
            for e in range(first, last):
                bank = banks[(PAIRS * kt + e // 2) % 4]
                cols = slice(P * (e - first), P * (e - first + 1))
                nc.tensor.matmul_mx(
                    out=bank[:, C * (e % 2) : C * (e % 2 + 1)],
                    lhsT=codes[:, cols].bitcast(FP8X4),
                    lhsT_scale=scales[:, cols],
                    rhs=da_codes[e][:].bitcast(FP8X4),
                    rhs_scale=da_scales[e][:],
                    start=True,
                    stop=True,
                )
                made.add((kt, e))
                if (kt, e ^ 1) in made:
                    (nc.vector.tensor_copy if (kt, e // 2) in VECTOR_COPIES else nc.scalar.copy)(out=dx[kt][:, 2 * C * (e // 2) : 2 * C * (e // 2 + 1)], in_=bank[:])

        def first_gather(kt, parts):
            first_part[kt] = ring.tile([P, T], F32, name="first_part", tag="first_part", bufs=2, align_bytes=64)
            for cols, part in token_parts(parts):
                nc.scalar.activation(first_part[kt][:, cols], dx[kt][:].indirect(pos_t[0][:, part]), ACT.Copy)

        def flat(staged):
            return staged.rearrange("p m x -> p (m x)").bitcast(F32)

        def raw_piece(kt):
            return rows_of[kt, 1]

        def second_gather(kt, parts):
            two_parts[kt] = rows_of[kt + 1, 2] if kt in (0, STRIPS - 2) else rows_of[2, 2]
            for cols, part in token_parts(parts):
                nc.vector.tensor_tensor(two_parts[kt][:, cols], dx[kt][:].indirect(pos_t[1][:, part]), first_part[kt][:, cols], ALU.add)

        def third_gather(kt, parts):
            total = raw_piece(kt + 2) if (0 if EARLY_THIRD else -1) < kt < STRIPS - 2 else spare[4 + kt]
            rows = slice(P * kt, P * (kt + 1))
            for cols, part in token_parts(parts):
                nc.vector.tensor_tensor(total[:, cols], dx[kt][:].indirect(pos_t[2][:, part]), two_parts[kt][:, cols], ALU.add)
                nc.sync.dma_start(out=out[rows, cols], in_=total[:, cols])

        made = set()
        arena = shared[:, 5 * T : 8 * T].bitcast(BF16)
        early[0] = keep.tile([P, 4, PIECE], BF16, name="early0", tag="s0", align_bytes=64)[:]
        early[1] = arena[:, : 4 * PIECE].rearrange("p (m x) -> p m x", m=4)
        for kt in range(2):
            late[kt] = arena[:, (3 + kt) * PIECE : (5 + kt) * PIECE].rearrange("p (m x) -> p m x", m=2)
            cast("scalar", kt, 0, 2, early[kt][:, :2])
        quantize_da(E - 1)
        for kt in range(STRIPS):
            dx[kt] = keep.tile([P, S], F32, name=f"dx{kt}", tag=f"a{kt % 4}", align_bytes=64)
            if kt >= 2:
                early[kt] = keep.tile([P, 4, PIECE], BF16, name=f"early{kt}", tag=f"s{kt}", align_bytes=64)[:]
                late[kt] = ring.tile([P, 2, PIECE], BF16, name="late", tag="w2_staged", bufs=3, align_bytes=64)[:]
                cast("scalar", kt, 0, 2, early[kt][:, :2])
            if kt == 0:
                products(kt, 0, 2, early[kt][:, :2])
            cast("vector", kt, 2, 4, early[kt][:, 2:])
            if kt == 0:
                products(kt, 2, 4, early[kt][:, 2:])
            if kt + 1 == STRIPS:
                products(kt, 0, 4, early[kt])
                third_gather(kt - 2, 1)
            cast("vector", kt, 4, 6, late[kt])
            if 2 < kt < STRIPS - 1:
                third_gather(kt - 2, 1)
            if 0 < kt < STRIPS - 1:
                products(kt, 0, 4, early[kt])
            products(kt, 4, 6, late[kt])
            if kt > 0:
                second_gather(kt - 1, 2 if kt in (1, STRIPS - 1) else 1)
            if kt == 1:
                third_gather(0, 2)
            first_gather(kt, 2 if kt in (0, STRIPS - 1) else 1)
        third_gather(STRIPS - 2, 2)
        last = STRIPS - 1
        middle_part, outer_parts, whole = spare[0], spare[1], spare[2]
        for cols, part in token_parts(2):
            nc.scalar.activation(middle_part[:, cols], dx[last][:].indirect(pos_t[1][:, part]), ACT.Copy)
        for cols, part in token_parts(2):
            nc.vector.tensor_tensor(outer_parts[:, cols], dx[last][:].indirect(pos_t[2][:, part]), first_part[last][:, cols], ALU.add)
        for cols, part in token_parts(2):
            nc.vector.tensor_tensor(whole[:, cols], outer_parts[:, cols], middle_part[:, cols], ALU.add)
            nc.sync.dma_start(out=out[P * last : P * (last + 1), cols], in_=whole[:, cols])
